import numpy as np
import ml_dtypes


def mxq(x, axis, fmt="e4m3"):
    dtype, down = {"e4m3": (ml_dtypes.float8_e4m3fn, 7), "e5m2": (ml_dtypes.float8_e5m2, 14)}[fmt]
    v = np.moveaxis(np.asarray(x, np.float32).astype(ml_dtypes.bfloat16).astype(np.float64), axis, -1)
    blocks = v.reshape(v.shape[:-1] + (-1, 32))
    amax = np.abs(blocks).max(-1, keepdims=True)
    byte = np.maximum(np.where(amax > 0, np.frexp(amax)[1] - 1 + 127, 0) - down, 1)
    scale = np.exp2(byte - 127.0)
    codes = (blocks / scale).astype(np.float32).astype(dtype).astype(np.float64)
    return np.moveaxis((codes * scale).reshape(v.shape), -1, axis)


WIDE = False


def mx_kscale(k):
    if not WIDE:
        return np.ones(k)
    levels = np.array([10, -10, 5, -5, 0])
    if k % 512:
        return np.exp2(np.random.permutation(np.resize(levels, k // 32))).repeat(32)
    a = np.empty((k // 512, 16))
    for p in range(k // 512):
        a[p, :8] = np.random.permutation(np.resize(levels, 8))
        for g in range(8):
            far = levels[np.abs(levels - a[p, g]) >= 10]
            a[p, g + 8] = far[np.random.randint(len(far))]
    return np.exp2(a.ravel()).repeat(32)


def f64(x):
    return np.asarray(x).astype(np.float64)


def striped(idx):
    return np.tile(idx.reshape(-1, 16).T, (8, 1)).astype(np.uint16)


def unstriped(offs):
    return offs[:16].T.reshape(-1).astype(np.int64)


E2M1 = np.array([0.0, 0.5, 1.0, 1.5, 2.0, 3.0, 4.0, 6.0, -0.0, -0.5, -1.0, -1.5, -2.0, -3.0, -4.0, -6.0])


def pack_weight(w, fmt):
    k, n = w.shape
    w = f64(np.asarray(w, np.float32).astype(ml_dtypes.bfloat16)).reshape(k // 32, 32, n)
    amax = np.abs(w).max(1)
    if fmt == "e4m3":
        byte = np.frexp(amax)[1] - 1 + 127 - 7
    else:
        mant, ex = np.frexp(amax / 6.0)
        byte = np.where(mant > 0.5, ex, ex - 1) + 127
    byte = np.clip(np.where(amax > 0, byte, 1), 1, 254)
    scaled = (w * np.exp2(127.0 - byte)[:, None, :]).reshape(k, n).astype(np.float32)
    by_word = np.ascontiguousarray(scaled.reshape(k // 512, 128, 4, n).transpose(0, 1, 3, 2))
    if fmt == "e4m3":
        words = by_word.astype(ml_dtypes.float8_e4m3fn).view(np.uint8)
    else:
        c = by_word.astype(ml_dtypes.float4_e2m1fn).view(np.uint8) & 0xF
        words = (c[..., 0::2] | (c[..., 1::2] << 4)).reshape(k // 512, 128, 2 * n)
    return np.ascontiguousarray(words), np.ascontiguousarray(byte.astype(np.uint8).reshape(k // 512, 16, n))


def unpack_weight(words, scales, fmt):
    g, _, n = scales.shape
    words = np.ascontiguousarray(words).reshape(g, 128, n, -1)
    if fmt == "e4m3":
        vals = words.view(ml_dtypes.float8_e4m3fn).astype(np.float64)
    else:
        nib = np.empty((g, 128, n, 4), np.uint8)
        nib[..., 0::2] = words & 0xF
        nib[..., 1::2] = words >> 4
        vals = E2M1[nib]
    vals = vals * np.repeat(np.exp2(scales.astype(np.float64) - 127.0), 8, axis=1)[..., None]
    return vals.transpose(0, 1, 3, 2).reshape(g * 512, n)


K, T, E1, C1, E2, C2, H = 256, 512, 2, 256, 4, 128, 512
N = 1024


def by_expert(wq, xq, E, C):
    return np.concatenate([wq[e].T @ xq[:, e * C:(e + 1) * C] for e in range(E)], axis=1)


def setup_inputs():
    n = np.random.standard_normal
    v = mx_kscale(N)
    u = mx_kscale(H)
    slots1, slots2 = np.random.permutation(T), np.random.permutation(T)
    dy = pack_weight(n((N, T)) * v[:, None], "e4m3")
    w2t = pack_weight(n((N, H)) / np.sqrt(N) / v[:, None] * u, "e2m1")
    wat = [pack_weight(m, "e2m1") for m in n((E1, H, K)) / np.sqrt(H) / u[None, :, None]]
    wbt = [pack_weight(m, "e4m3") for m in n((E2, H, K)) / np.sqrt(H) / u[None, :, None]]
    return {
        "dy_words": dy[0],
        "dy_scales": dy[1],
        "w2t_words": w2t[0],
        "w2t_scales": w2t[1],
        "wat_words": np.stack([m[0] for m in wat]),
        "wat_scales": np.stack([m[1] for m in wat]),
        "wbt_words": np.stack([m[0] for m in wbt]),
        "wbt_scales": np.stack([m[1] for m in wbt]),
        "a": (n((H, T))).astype(np.float32),
        "c": (n((H, T))).astype(np.float32),
        "offs": striped(slots1),
        "offs2": striped(slots2),
    }


def reference(dy_words, dy_scales, w2t_words, w2t_scales, wat_words, wat_scales, wbt_words, wbt_scales, a, c, offs, offs2):
    w2t = unpack_weight(w2t_words, w2t_scales, "e2m1")
    wat = np.stack([unpack_weight(wat_words[e], wat_scales[e], "e2m1") for e in range(E1)])
    wbt = np.stack([unpack_weight(wbt_words[e], wbt_scales[e], "e4m3") for e in range(E2)])
    idx, idx2 = unstriped(offs), unstriped(offs2)
    dh = w2t.T @ unpack_weight(dy_words, dy_scales, "e4m3")
    da = dh * f64(c)
    dc = dh * f64(a)
    out = np.zeros((K, T))
    out[:, idx] = by_expert(wat, mxq(da[:, idx], 0, "e4m3"), E1, C1)
    out[:, idx2] += by_expert(wbt, mxq(dc[:, idx2], 0, "e4m3"), E2, C2)
    return out

@@ -1,0 +1,203 @@
+from contextlib import ExitStack
+
+import concourse.mybir as mybir
+
+K, T, H, N = 256, 512, 512, 1024
+E1, C1, E2, C2 = 2, 256, 4, 128
+FLOPS = 2 * N * H * T + 2 * 2 * H * K * T
+
+F32 = mybir.dt.float32
+BF16 = mybir.dt.bfloat16
+I32 = mybir.dt.int32
+U32 = mybir.dt.uint32
+U16 = mybir.dt.uint16
+U8 = mybir.dt.uint8
+FP8X4 = mybir.dt.float8_e4m3fn_x4
+FP4X4 = mybir.dt.float4_e2m1fn_x4
+MULT = mybir.AluOpType.mult
+ADD = mybir.AluOpType.add
+COPY = mybir.ActivationFunctionType.Copy
+
+P = 128
+PASSES = N // 512
+G = 256
+
+
+def load_scale_rows(queue, plane, rows):
+    for r in range(4):
+        queue.dma_start(out=plane[r:P:32, :, :].bitcast(I32), in_=rows[r].bitcast(I32))
+
+
+def tile_moe_plb_none_kernel(
+    tc, dy_words, dy_scales, w2t_words, w2t_scales, wat_words, wat_scales, wbt_words, wbt_scales, a, c, offs, offs2, out
+):
+    nc = tc.nc
+    with ExitStack() as ctx:
+        sb = ctx.enter_context(tc.tile_pool(name="sb", bufs=1))
+        ps = ctx.enter_context(tc.psum_pool(name="ps", bufs=1))
+
+        def tile(shape, dtype, name):
+            return sb.tile(shape, dtype, name=name, align_bytes=64)
+
+        list_a = tile([P, T // 16], U16, "list_a")
+        list_c = tile([P, T // 16], U16, "list_c")
+        w2_sc_raw = tile([P, PASSES, H], U8, "w2_sc_raw")
+        dy_sc = tile([P, PASSES, T], U8, "dy_sc")
+        wa_sc = tile([P, E1, K], U8, "wa_sc")
+        wb_sc = tile([P, E2, K], U8, "wb_sc")
+        w2_raw = tile([P, PASSES, 2 * H], U8, "w2_raw")
+        dy_w = [tile([P, PASSES, 256], I32, "dy_w%d" % i) for i in range(2)]
+        c_sb = [tile([P, 2, T], F32, "c_sb%d" % i) for i in range(2)]
+        a_sb = [tile([P, 2, T], F32, "a_sb%d" % i) for i in range(2)]
+        wa_w = tile([P, E1, 2 * K], U8, "wa_w")
+        wb_w = tile([P, E2, K], I32, "wb_w")
+
+        nc.vector.memset(w2_sc_raw[:].bitcast(I32), 0)
+        nc.vector.memset(dy_sc[:].bitcast(I32), 0)
+        nc.gpsimd.memset(wa_sc[:].bitcast(I32), 0)
+        nc.gpsimd.memset(wb_sc[:].bitcast(I32), 0)
+
+        load_scale_rows(nc.scalar, w2_sc_raw, w2t_scales.rearrange("s (q r) i -> r q s i", r=4))
+        nc.sync.dma_start(out=w2_raw[:].bitcast(I32), in_=w2t_words.rearrange("s p b -> p s b").bitcast(I32))
+        dy_view = dy_words.rearrange("s p t d -> p s (t d)")
+        for th in range(2):
+            nc.sync.dma_start(out=dy_w[th][:], in_=dy_view[:, :, th * 1024 : (th + 1) * 1024].bitcast(I32))
+        c_view = c.rearrange("(p j) t -> p j t", j=4)
+        a_view = a.rearrange("(p j) t -> p j t", j=4)
+        nc.sync.dma_start(out=c_sb[0][:], in_=c_view[:, 0:2, :])
+        load_scale_rows(nc.scalar, dy_sc, dy_scales.rearrange("s (q r) t -> r q s t", r=4))
+        nc.sync.dma_start(out=c_sb[1][:], in_=c_view[:, 2:4, :])
+        nc.sync.dma_start(list_a[:], offs)
+        nc.sync.dma_start(out=wa_w[:].bitcast(I32), in_=wat_words.rearrange("e s p b -> p (e s) b").bitcast(I32))
+        load_scale_rows(nc.gpsimd, wa_sc, wat_scales.rearrange("e s (q r) k -> r q (e s) k", r=4))
+        nc.sync.dma_start(out=a_sb[0][:], in_=a_view[:, 0:2, :])
+        nc.sync.dma_start(out=a_sb[1][:], in_=a_view[:, 2:4, :])
+        nc.sync.dma_start(list_c[:], offs2)
+        nc.sync.dma_start(out=wb_w[:], in_=wbt_words.rearrange("f s p k d -> p (f s) (k d)").bitcast(I32))
+        load_scale_rows(nc.gpsimd, wb_sc, wbt_scales.rearrange("f s (q r) k -> r q (f s) k", r=4))
+
+        warm = tile([P, 16], F32, "warm")
+        nc.vector.memset(warm[:, 0:8], 0.0)
+        nc.scalar.activation(warm[:, 8:16], warm[:, 0:8], COPY)
+
+        w2_p = [tile([P, PASSES, 2, 2 * P], U8, "w2_p%d" % h) for h in range(2)]
+        w2_sc = [tile([P, PASSES, 2, P], U8, "w2_sc%d" % h) for h in range(2)]
+        sc_view = w2_sc_raw[:].rearrange("p s (m j) -> p s m j", j=4)
+        w_view = w2_raw[:].bitcast(U16).rearrange("p s (m j) -> p s m j", j=4)
+        for h in range(2):
+            nc.vector.tensor_copy(out=w2_sc[h][:].rearrange("p s e m -> p s m e"), in_=sc_view[:, :, :, 2 * h : 2 * h + 2])
+            nc.vector.tensor_copy(out=w2_p[h][:].bitcast(U16).rearrange("p s e m -> p s m e"), in_=w_view[:, :, :, 2 * h : 2 * h + 2])
+
+        da = [tile([P, 2 * T], BF16, "da%d" % h) for h in range(2)]
+        dc = tile([P, 4, T], BF16, "dc")
+        dh = {}
+        for h in range(2):
+            for th in range(2):
+                bank = ps.tile([P, 2, 256], F32, name="dh%d%d" % (h, th))
+                dh[h, th] = bank
+                for tq in range(2):
+                    for e in range(2):
+                        t0 = th * 256 + tq * 128
+                        for s in range(PASSES):
+                            nc.tensor.matmul_mx(
+                                out=bank[:, e, tq * 128 : (tq + 1) * 128],
+                                lhsT=w2_p[h][:, s, e, :].bitcast(FP4X4),
+                                lhsT_scale=w2_sc[h][:, s, e, :],
+                                rhs=dy_w[th][:, s, tq * 128 : (tq + 1) * 128].bitcast(FP8X4),
+                                rhs_scale=dy_sc[:, s, t0 : t0 + 128],
+                                start=(s == 0),
+                                stop=(s == PASSES - 1),
+                            )
+                nc.vector.tensor_tensor(
+                    out=da[h][:, th * 512 : (th + 1) * 512].rearrange("p (t e) -> p t e", e=2),
+                    in0=bank[:].rearrange("p e t -> p t e"),
+                    in1=c_sb[h][:, :, th * 256 : (th + 1) * 256].rearrange("p e t -> p t e"),
+                    op=MULT,
+                )
+
+        r_tok = [tile([P, T], F32, "r_tok%d" % kt) for kt in range(2)]
+        q_tok = [tile([P, T], F32, "q_tok%d" % kt) for kt in range(2)]
+
+        def offsets(lst, g):
+            return lst[:, g * (G // 16) : (g + 1) * (G // 16)]
+
+        ga = [tile([P, G, 4], BF16, "ga%d" % g) for g in range(2)]
+        for g in range(2):
+            pairs = tile([P, 2, 2 * G], BF16, "pairs%d" % g)
+            for h in range(2):
+                nc.vector.tensor_copy(out=pairs[:, h, :].bitcast(U32), in_=da[h][:].bitcast(U32).indirect(offsets(list_a, g)))
+            nc.scalar.copy(out=ga[g][:].rearrange("p u (h e) -> p u h e", h=2), in_=pairs[:].rearrange("p h (u e) -> p u h e", e=2))
+
+        def quantise(src, name):
+            codes = tile([P, G], U32, name + "_w")
+            scales = tile([P, G], U8, name + "_s")
+            nc.vector.quantize_mx(out=codes[:].bitcast(FP8X4), scales=scales[:], in_=src[:].rearrange("p u j -> p (u j)"))
+            return codes, scales
+
+        def dc_mult(h, th):
+            cols = slice(th * 256, (th + 1) * 256)
+            nc.vector.tensor_tensor(out=dc[:, 2 * h : 2 * h + 2, cols], in0=dh[h, th][:], in1=a_sb[h][:, :, cols], op=MULT)
+
+        r_sb = []
+        for g in range(2):
+            codes, scales = quantise(ga[g], "qa%d" % g)
+            bank = ps.tile([P, 2, G], F32, name="r%d" % g)
+            for kt in range(2):
+                nc.tensor.matmul_mx(
+                    out=bank[:, kt, :],
+                    lhsT=wa_w[:, g, kt * 256 : (kt + 1) * 256].bitcast(FP4X4),
+                    lhsT_scale=wa_sc[:, g, kt * 128 : (kt + 1) * 128],
+                    rhs=codes[:].bitcast(FP8X4),
+                    rhs_scale=scales[:],
+                    start=True,
+                    stop=True,
+                )
+            res = tile([P, 2, G], F32, "r_sb%d" % g)
+            nc.scalar.activation(res[:], bank[:], COPY)
+            r_sb.append(res)
+            dc_mult(g, 0)
+            dc_mult(g, 1)
+
+        gc = [tile([P, G, 4], BF16, "gc%d" % g) for g in range(2)]
+        q_sb = []
+
+        def second_pool(g):
+            codes, scales = quantise(gc[g], "qc%d" % g)
+            bank = ps.tile([P, 2, G], F32, name="q%d" % g)
+            for kt in range(2):
+                for fl in range(2):
+                    f = 2 * g + fl
+                    cols = slice(fl * C2, (fl + 1) * C2)
+                    nc.tensor.matmul_mx(
+                        out=bank[:, kt, cols],
+                        lhsT=wb_w[:, f, kt * 128 : (kt + 1) * 128].bitcast(FP8X4),
+                        lhsT_scale=wb_sc[:, f, kt * 128 : (kt + 1) * 128],
+                        rhs=codes[:, cols].bitcast(FP8X4),
+                        rhs_scale=scales[:, cols],
+                        start=True,
+                        stop=True,
+                    )
+            res = tile([P, 2, G], F32, "q_sb%d" % g)
+            nc.scalar.activation(res[:], bank[:], COPY)
+            q_sb.append(res)
+
+        def gather_c(g):
+            for j in range(4):
+                nc.scalar.activation(gc[g][:, :, j], dc[:, j, :].indirect(offsets(list_c, g)), COPY)
+
+        def scatter(dst, lst, g, src):
+            nc.vector.tensor_copy(out=dst[:].indirect(offsets(lst, g)), in_=src)
+
+        gather_c(0)
+        second_pool(0)
+        gather_c(1)
+        second_pool(1)
+        for g in range(2):
+            for kt in range(2):
+                scatter(r_tok[kt], list_a, g, r_sb[g][:, kt, :])
+        for kt in range(2):
+            for g in range(2):
+                scatter(q_tok[kt], list_c, g, q_sb[g][:, kt, :])
+            res = tile([P, T], F32, "res%d" % kt)
+            nc.vector.tensor_tensor(out=res[:], in0=r_tok[kt][:], in1=q_tok[kt][:], op=ADD)
+            nc.sync.dma_start(out=out[kt * P : (kt + 1) * P, :], in_=res[:])

@@ -23,9 +23,9 @@ PASSES = N // 512
 G = 256
 
 
-def load_scale_rows(queue, plane, rows):
+def load_scale_rows(queues, plane, rows):
     for r in range(4):
-        queue.dma_start(out=plane[r:P:32, :, :].bitcast(I32), in_=rows[r].bitcast(I32))
+        queues[r].dma_start(out=plane[r:P:32, :, :].bitcast(I32), in_=rows[r].bitcast(I32))
 
 
 def tile_moe_plb_none_kernel(
@@ -46,35 +46,32 @@ def tile_moe_plb_none_kernel(
         wa_sc = tile([P, E1, K], U8, "wa_sc")
         wb_sc = tile([P, E2, K], U8, "wb_sc")
         w2_raw = tile([P, PASSES, 2 * H], U8, "w2_raw")
-        dy_w = [tile([P, PASSES, 256], I32, "dy_w%d" % i) for i in range(2)]
+        dy_w = tile([P, PASSES, T], I32, "dy_w")
         c_sb = [tile([P, 2, T], F32, "c_sb%d" % i) for i in range(2)]
-        a_sb = [tile([P, 2, T], F32, "a_sb%d" % i) for i in range(2)]
+        a_sb = tile([P, 4, T], F32, "a_sb")
         wa_w = tile([P, E1, 2 * K], U8, "wa_w")
         wb_w = tile([P, E2, K], I32, "wb_w")
 
         nc.vector.memset(w2_sc_raw[:].bitcast(I32), 0)
         nc.vector.memset(dy_sc[:].bitcast(I32), 0)
-        nc.gpsimd.memset(wa_sc[:].bitcast(I32), 0)
-        nc.gpsimd.memset(wb_sc[:].bitcast(I32), 0)
+        nc.vector.memset(wa_sc[:].bitcast(I32), 0)
+        nc.vector.memset(wb_sc[:].bitcast(I32), 0)
 
-        load_scale_rows(nc.scalar, w2_sc_raw, w2t_scales.rearrange("s (q r) i -> r q s i", r=4))
         nc.sync.dma_start(out=w2_raw[:].bitcast(I32), in_=w2t_words.rearrange("s p b -> p s b").bitcast(I32))
-        dy_view = dy_words.rearrange("s p t d -> p s (t d)")
-        for th in range(2):
-            nc.sync.dma_start(out=dy_w[th][:], in_=dy_view[:, :, th * 1024 : (th + 1) * 1024].bitcast(I32))
+        nc.sync.dma_start(list_a[:], offs)
+        nc.sync.dma_start(list_c[:], offs2)
+        load_scale_rows([nc.scalar] * 4, w2_sc_raw, w2t_scales.rearrange("s (q r) i -> r q s i", r=4))
+        load_scale_rows([nc.sync] * 4, dy_sc, dy_scales.rearrange("s (q r) t -> r q s t", r=4))
+        nc.gpsimd.dma_start(out=dy_w[:], in_=dy_words.rearrange("s p t d -> p s (t d)").bitcast(I32))
         c_view = c.rearrange("(p j) t -> p j t", j=4)
         a_view = a.rearrange("(p j) t -> p j t", j=4)
-        nc.sync.dma_start(out=c_sb[0][:], in_=c_view[:, 0:2, :])
-        load_scale_rows(nc.scalar, dy_sc, dy_scales.rearrange("s (q r) t -> r q s t", r=4))
-        nc.sync.dma_start(out=c_sb[1][:], in_=c_view[:, 2:4, :])
-        nc.sync.dma_start(list_a[:], offs)
-        nc.sync.dma_start(out=wa_w[:].bitcast(I32), in_=wat_words.rearrange("e s p b -> p (e s) b").bitcast(I32))
-        load_scale_rows(nc.gpsimd, wa_sc, wat_scales.rearrange("e s (q r) k -> r q (e s) k", r=4))
-        nc.sync.dma_start(out=a_sb[0][:], in_=a_view[:, 0:2, :])
-        nc.sync.dma_start(out=a_sb[1][:], in_=a_view[:, 2:4, :])
-        nc.sync.dma_start(list_c[:], offs2)
-        nc.sync.dma_start(out=wb_w[:], in_=wbt_words.rearrange("f s p k d -> p (f s) (k d)").bitcast(I32))
-        load_scale_rows(nc.gpsimd, wb_sc, wbt_scales.rearrange("f s (q r) k -> r q (f s) k", r=4))
+        nc.gpsimd.dma_start(out=c_sb[0][:], in_=c_view[:, 0:2, :])
+        nc.gpsimd.dma_start(out=c_sb[1][:], in_=c_view[:, 2:4, :])
+        nc.gpsimd.dma_start(out=a_sb[:], in_=a_view)
+        nc.gpsimd.dma_start(out=wa_w[:].bitcast(I32), in_=wat_words.rearrange("e s p b -> p (e s) b").bitcast(I32))
+        nc.gpsimd.dma_start(out=wb_w[:], in_=wbt_words.rearrange("f s p k d -> p (f s) (k d)").bitcast(I32))
+        load_scale_rows([nc.sync] * 4, wa_sc, wat_scales.rearrange("e s (q r) k -> r q (e s) k", r=4))
+        load_scale_rows([nc.sync] * 4, wb_sc, wbt_scales.rearrange("f s (q r) k -> r q (f s) k", r=4))
 
         warm = tile([P, 16], F32, "warm")
         nc.vector.memset(warm[:, 0:8], 0.0)
@@ -93,7 +90,7 @@ def tile_moe_plb_none_kernel(
         dh = {}
         for h in range(2):
             for th in range(2):
-                bank = ps.tile([P, 2, 256], F32, name="dh%d%d" % (h, th))
+                bank = ps.tile([P, 2, 256], F32, name="dh%d%d" % (h, th), tag="dh%d%d" % (h, th))
                 dh[h, th] = bank
                 for tq in range(2):
                     for e in range(2):
@@ -103,7 +100,7 @@ def tile_moe_plb_none_kernel(
                                 out=bank[:, e, tq * 128 : (tq + 1) * 128],
                                 lhsT=w2_p[h][:, s, e, :].bitcast(FP4X4),
                                 lhsT_scale=w2_sc[h][:, s, e, :],
-                                rhs=dy_w[th][:, s, tq * 128 : (tq + 1) * 128].bitcast(FP8X4),
+                                rhs=dy_w[:, s, t0 : t0 + 128].bitcast(FP8X4),
                                 rhs_scale=dy_sc[:, s, t0 : t0 + 128],
                                 start=(s == 0),
                                 stop=(s == PASSES - 1),
@@ -136,12 +133,11 @@ def tile_moe_plb_none_kernel(
 
         def dc_mult(h, th):
             cols = slice(th * 256, (th + 1) * 256)
-            nc.vector.tensor_tensor(out=dc[:, 2 * h : 2 * h + 2, cols], in0=dh[h, th][:], in1=a_sb[h][:, :, cols], op=MULT)
+            nc.vector.tensor_tensor(out=dc[:, 2 * h : 2 * h + 2, cols], in0=dh[h, th][:], in1=a_sb[:, 2 * h : 2 * h + 2, cols], op=MULT)
 
-        r_sb = []
-        for g in range(2):
+        def first_pool(g, bank_name):
             codes, scales = quantise(ga[g], "qa%d" % g)
-            bank = ps.tile([P, 2, G], F32, name="r%d" % g)
+            bank = ps.tile([P, 2, G], F32, name="r%d" % g, tag=bank_name)
             for kt in range(2):
                 nc.tensor.matmul_mx(
                     out=bank[:, kt, :],
@@ -152,14 +148,9 @@ def tile_moe_plb_none_kernel(
                     start=True,
                     stop=True,
                 )
-            res = tile([P, 2, G], F32, "r_sb%d" % g)
-            nc.scalar.activation(res[:], bank[:], COPY)
-            r_sb.append(res)
-            dc_mult(g, 0)
-            dc_mult(g, 1)
+            return bank
 
         gc = [tile([P, G, 4], BF16, "gc%d" % g) for g in range(2)]
-        q_sb = []
 
         def second_pool(g):
             codes, scales = quantise(gc[g], "qc%d" % g)
@@ -177,27 +168,38 @@ def tile_moe_plb_none_kernel(
                         start=True,
                         stop=True,
                     )
-            res = tile([P, 2, G], F32, "q_sb%d" % g)
-            nc.scalar.activation(res[:], bank[:], COPY)
-            q_sb.append(res)
+            return bank
 
-        def gather_c(g):
-            for j in range(4):
-                nc.scalar.activation(gc[g][:, :, j], dc[:, j, :].indirect(offsets(list_c, g)), COPY)
+        def gather_c(g, j):
+            nc.scalar.activation(gc[g][:, :, j], dc[:, j, :].indirect(offsets(list_c, g)), COPY)
 
-        def scatter(dst, lst, g, src):
-            nc.vector.tensor_copy(out=dst[:].indirect(offsets(lst, g)), in_=src)
+        def way_back(bank, kt, dst, lst, g, name):
+            res = tile([P, G], F32, name)
+            nc.scalar.activation(res[:], bank[:, kt, :], COPY)
+            nc.vector.tensor_copy(out=dst[kt][:].indirect(offsets(lst, g)), in_=res[:])
 
-        gather_c(0)
-        second_pool(0)
-        gather_c(1)
-        second_pool(1)
-        for g in range(2):
-            for kt in range(2):
-                scatter(r_tok[kt], list_a, g, r_sb[g][:, kt, :])
+        r0 = first_pool(0, "r0")
+        dc_mult(0, 0)
+        dc_mult(0, 1)
+        dc_mult(1, 0)
+        dc_mult(1, 1)
+        r1 = first_pool(1, "dh11")
+        way_back(r0, 0, r_tok, list_a, 0, "r00")
+        way_back(r0, 1, r_tok, list_a, 0, "r01")
+        for j in range(3):
+            gather_c(0, j)
+        way_back(r1, 0, r_tok, list_a, 1, "r10")
+        gather_c(0, 3)
+        q0 = second_pool(0)
+        way_back(r1, 1, r_tok, list_a, 1, "r11")
+        for j in range(3):
+            gather_c(1, j)
+        way_back(q0, 0, q_tok, list_c, 0, "q00")
+        gather_c(1, 3)
+        q1 = second_pool(1)
+        way_back(q0, 1, q_tok, list_c, 0, "q01")
         for kt in range(2):
-            for g in range(2):
-                scatter(q_tok[kt], list_c, g, q_sb[g][:, kt, :])
+            way_back(q1, kt, q_tok, list_c, 1, "q1%d" % kt)
             res = tile([P, T], F32, "res%d" % kt)
             nc.vector.tensor_tensor(out=res[:], in0=r_tok[kt][:], in1=q_tok[kt][:], op=ADD)
             nc.sync.dma_start(out=out[kt * P : (kt + 1) * P, :], in_=res[:])

@@ -36,111 +36,154 @@ def tile_moe_plb_none_kernel(
         sb = ctx.enter_context(tc.tile_pool(name="sb", bufs=1))
         ps = ctx.enter_context(tc.psum_pool(name="ps", bufs=1))
 
-        def tile(shape, dtype, name):
-            return sb.tile(shape, dtype, name=name, align_bytes=64)
+        def tile(shape, dtype, name, tag=None):
+            return sb.tile(shape, dtype, name=name, tag=tag or name, align_bytes=64)
 
         list_a = tile([P, T // 16], U16, "list_a")
         list_c = tile([P, T // 16], U16, "list_c")
         w2_sc_raw = tile([P, PASSES, H], U8, "w2_sc_raw")
         dy_sc = tile([P, PASSES, T], U8, "dy_sc")
-        wa_sc = tile([P, E1, K], U8, "wa_sc")
-        wb_sc = tile([P, E2, K], U8, "wb_sc")
         w2_raw = tile([P, PASSES, 2 * H], U8, "w2_raw")
         dy_w = tile([P, PASSES, T], I32, "dy_w")
-        c_sb = [tile([P, 2, T], F32, "c_sb%d" % i) for i in range(2)]
-        a_sb = tile([P, 4, T], F32, "a_sb")
+        c_row = [tile([P, T], F32, "c_row%d" % j) for j in range(2)]
+        a_row0 = tile([P, T], F32, "a_row0")
+        a_row1 = [tile([P, 256], F32, "a_row1%d" % th) for th in range(2)]
+        c_hi = tile([P, 2, T], F32, "c_hi")
+        a_hi = [tile([P, 2, 256], F32, "a_hi%d" % th) for th in range(2)]
         wa_w = tile([P, E1, 2 * K], U8, "wa_w")
         wb_w = tile([P, E2, K], I32, "wb_w")
 
         nc.vector.memset(w2_sc_raw[:].bitcast(I32), 0)
         nc.vector.memset(dy_sc[:].bitcast(I32), 0)
-        nc.vector.memset(wa_sc[:].bitcast(I32), 0)
-        nc.vector.memset(wb_sc[:].bitcast(I32), 0)
 
-        nc.sync.dma_start(out=w2_raw[:].bitcast(I32), in_=w2t_words.rearrange("s p b -> p s b").bitcast(I32))
-        nc.sync.dma_start(list_a[:], offs)
-        nc.sync.dma_start(list_c[:], offs2)
-        load_scale_rows([nc.scalar] * 4, w2_sc_raw, w2t_scales.rearrange("s (q r) i -> r q s i", r=4))
-        load_scale_rows([nc.sync] * 4, dy_sc, dy_scales.rearrange("s (q r) t -> r q s t", r=4))
-        nc.gpsimd.dma_start(out=dy_w[:], in_=dy_words.rearrange("s p t d -> p s (t d)").bitcast(I32))
         c_view = c.rearrange("(p j) t -> p j t", j=4)
         a_view = a.rearrange("(p j) t -> p j t", j=4)
-        nc.gpsimd.dma_start(out=c_sb[0][:], in_=c_view[:, 0:2, :])
-        nc.gpsimd.dma_start(out=c_sb[1][:], in_=c_view[:, 2:4, :])
-        nc.gpsimd.dma_start(out=a_sb[:], in_=a_view)
-        nc.gpsimd.dma_start(out=wa_w[:].bitcast(I32), in_=wat_words.rearrange("e s p b -> p (e s) b").bitcast(I32))
-        nc.gpsimd.dma_start(out=wb_w[:], in_=wbt_words.rearrange("f s p k d -> p (f s) (k d)").bitcast(I32))
-        load_scale_rows([nc.sync] * 4, wa_sc, wat_scales.rearrange("e s (q r) k -> r q (e s) k", r=4))
-        load_scale_rows([nc.sync] * 4, wb_sc, wbt_scales.rearrange("f s (q r) k -> r q (f s) k", r=4))
+        dy_rows = dy_scales.rearrange("s (q r) t -> r q s t", r=4)
 
+        def load_scale_row(queue, plane, rows, r):
+            queue.dma_start(out=plane[r:P:32, :, :].bitcast(I32), in_=rows[r].bitcast(I32))
+
+        w2_rows = w2t_scales.rearrange("s (q r) i -> r q s i", r=4)
         warm = tile([P, 16], F32, "warm")
         nc.vector.memset(warm[:, 0:8], 0.0)
+
+        nc.sync.dma_start(out=w2_raw[:].bitcast(I32), in_=w2t_words.rearrange("s p b -> p s b").bitcast(I32))
+        load_scale_rows([nc.scalar, nc.scalar, nc.sync, nc.sync], w2_sc_raw, w2_rows)
         nc.scalar.activation(warm[:, 8:16], warm[:, 0:8], COPY)
+        load_scale_row(nc.sync, dy_sc, dy_rows, 0)
+        load_scale_row(nc.sync, dy_sc, dy_rows, 1)
+        nc.sync.dma_start(out=dy_w[:], in_=dy_words.rearrange("s p t d -> p s (t d)").bitcast(I32))
+        load_scale_row(nc.scalar, dy_sc, dy_rows, 2)
+        load_scale_row(nc.sync, dy_sc, dy_rows, 3)
+        nc.sync.dma_start(out=c_row[0][:], in_=c_view[:, 0, :])
+        nc.sync.dma_start(out=a_row0[:], in_=a_view[:, 0, :])
+        nc.sync.dma_start(list_a[:], offs)
+        nc.sync.dma_start(out=c_row[1][:], in_=c_view[:, 1, :])
+        nc.sync.dma_start(out=a_row1[0][:], in_=a_view[:, 1, 0:256])
+        nc.sync.dma_start(out=c_hi[:], in_=c_view[:, 2:4, :])
+        nc.sync.dma_start(out=a_row1[1][:], in_=a_view[:, 1, 256:512])
+        nc.sync.dma_start(list_c[:], offs2)
+        nc.sync.dma_start(out=wa_w[:].bitcast(I32), in_=wat_words.rearrange("e s p b -> p (e s) b").bitcast(I32))
 
         w2_p = [tile([P, PASSES, 2, 2 * P], U8, "w2_p%d" % h) for h in range(2)]
         w2_sc = [tile([P, PASSES, 2, P], U8, "w2_sc%d" % h) for h in range(2)]
         sc_view = w2_sc_raw[:].rearrange("p s (m j) -> p s m j", j=4)
         w_view = w2_raw[:].bitcast(U16).rearrange("p s (m j) -> p s m j", j=4)
         for h in range(2):
-            nc.vector.tensor_copy(out=w2_sc[h][:].rearrange("p s e m -> p s m e"), in_=sc_view[:, :, :, 2 * h : 2 * h + 2])
             nc.vector.tensor_copy(out=w2_p[h][:].bitcast(U16).rearrange("p s e m -> p s m e"), in_=w_view[:, :, :, 2 * h : 2 * h + 2])
+            nc.vector.tensor_copy(out=w2_sc[h][:].rearrange("p s e m -> p s m e"), in_=sc_view[:, :, :, 2 * h : 2 * h + 2])
 
-        da = [tile([P, 2 * T], BF16, "da%d" % h) for h in range(2)]
-        dc = tile([P, 4, T], BF16, "dc")
-        dh = {}
-        for h in range(2):
-            for th in range(2):
-                bank = ps.tile([P, 2, 256], F32, name="dh%d%d" % (h, th), tag="dh%d%d" % (h, th))
-                dh[h, th] = bank
-                for tq in range(2):
-                    for e in range(2):
-                        t0 = th * 256 + tq * 128
-                        for s in range(PASSES):
-                            nc.tensor.matmul_mx(
-                                out=bank[:, e, tq * 128 : (tq + 1) * 128],
-                                lhsT=w2_p[h][:, s, e, :].bitcast(FP4X4),
-                                lhsT_scale=w2_sc[h][:, s, e, :],
-                                rhs=dy_w[:, s, t0 : t0 + 128].bitcast(FP8X4),
-                                rhs_scale=dy_sc[:, s, t0 : t0 + 128],
-                                start=(s == 0),
-                                stop=(s == PASSES - 1),
-                            )
-                nc.vector.tensor_tensor(
-                    out=da[h][:, th * 512 : (th + 1) * 512].rearrange("p (t e) -> p t e", e=2),
-                    in0=bank[:].rearrange("p e t -> p t e"),
-                    in1=c_sb[h][:, :, th * 256 : (th + 1) * 256].rearrange("p e t -> p t e"),
-                    op=MULT,
+        wa_sc = w2_sc_raw[:, 0, :].rearrange("p (e k) -> p e k", k=K)
+        wa_rows = wat_scales.rearrange("e s (q r) k -> r q (e s) k", r=4)
+        for r in range(3):
+            load_scale_row(nc.sync, wa_sc, wa_rows, r)
+        nc.sync.dma_start(out=a_hi[0][:], in_=a_view[:, 2:4, 0:256])
+        load_scale_row(nc.sync, wa_sc, wa_rows, 3)
+        nc.sync.dma_start(out=a_hi[1][:], in_=a_view[:, 2:4, 256:512])
+        nc.sync.dma_start(out=wb_w[:], in_=wbt_words.rearrange("f s p k d -> p (f s) (k d)").bitcast(I32))
+
+        def first_product(dst, h, e, t0, n):
+            for s in range(PASSES):
+                nc.tensor.matmul_mx(
+                    out=dst,
+                    lhsT=w2_p[h][:, s, e, :].bitcast(FP4X4),
+                    lhsT_scale=w2_sc[h][:, s, e, :],
+                    rhs=dy_w[:, s, t0 : t0 + n].bitcast(FP8X4),
+                    rhs_scale=dy_sc[:, s, t0 : t0 + n],
+                    start=(s == 0),
+                    stop=(s == PASSES - 1),
                 )
-
-        r_tok = [tile([P, T], F32, "r_tok%d" % kt) for kt in range(2)]
-        q_tok = [tile([P, T], F32, "q_tok%d" % kt) for kt in range(2)]
 
         def offsets(lst, g):
             return lst[:, g * (G // 16) : (g + 1) * (G // 16)]
 
+        da_row = [tile([P, T], BF16, "da_row%d" % j) for j in range(2)]
+        da_hi = tile([P, 2 * T], BF16, "da_hi")
+        dc_row = [tile([P, T], BF16, "dc_row%d" % j) for j in range(2)]
+        dc_hi = tile([P, 2, T], BF16, "dc_hi")
         ga = [tile([P, G, 4], BF16, "ga%d" % g) for g in range(2)]
-        for g in range(2):
-            pairs = tile([P, 2, 2 * G], BF16, "pairs%d" % g)
-            for h in range(2):
-                nc.vector.tensor_copy(out=pairs[:, h, :].bitcast(U32), in_=da[h][:].bitcast(U32).indirect(offsets(list_a, g)))
-            nc.scalar.copy(out=ga[g][:].rearrange("p u (h e) -> p u h e", h=2), in_=pairs[:].rearrange("p h (u e) -> p u h e", e=2))
+
+        dh_row = {}
+
+        def dc_row_mult(j, th):
+            cols = slice(th * 256, (th + 1) * 256)
+            factor = a_row0[:, cols] if j == 0 else a_row1[th][:]
+            nc.vector.tensor_tensor(out=dc_row[j][:, cols], in0=dh_row[j, th][:], in1=factor, op=MULT)
+
+        for j in range(2):
+            for th in range(2):
+                cols = slice(th * 256, (th + 1) * 256)
+                bank = ps.tile([P, 256], F32, name="dh%d%d" % (j, th), tag="dh%d%d" % (j, th))
+                dh_row[j, th] = bank
+                for tq in range(2):
+                    first_product(bank[:, tq * 128 : (tq + 1) * 128], 0, j, th * 256 + tq * 128, 128)
+                nc.vector.tensor_tensor(out=da_row[j][:, cols], in0=bank[:], in1=c_row[j][:, cols], op=MULT)
+                if j == 0:
+                    dc_row_mult(j, th)
+            if j == 1:
+                dc_row_mult(1, 0)
+            for g in range(2):
+                nc.scalar.activation(ga[g][:, :, j], da_row[j][:].indirect(offsets(list_a, g)), COPY)
+        dh_hi = []
+        for th in range(2):
+            bank = ps.tile([P, 2, 256], F32, name="dh_hi%d" % th, tag="dh_hi%d" % th)
+            dh_hi.append(bank)
+            for tq in range(2):
+                for e in range(2):
+                    first_product(bank[:, e, tq * 128 : (tq + 1) * 128], 1, e, th * 256 + tq * 128, 128)
+            nc.vector.tensor_tensor(
+                out=da_hi[:, th * 512 : (th + 1) * 512].rearrange("p (t e) -> p t e", e=2),
+                in0=bank[:].rearrange("p e t -> p t e"),
+                in1=c_hi[:, :, th * 256 : (th + 1) * 256].rearrange("p e t -> p t e"),
+                op=MULT,
+            )
+
+        wb_sc = dy_sc[:].rearrange("p s (f k) -> p (s f) k", k=K)
+        load_scale_rows([nc.sync] * 4, wb_sc, wbt_scales.rearrange("f s (q r) k -> r q (f s) k", r=4))
+
+        r_tok = [tile([P, T], F32, "r_tok%d" % kt) for kt in range(2)]
+        q_tok = [tile([P, T], F32, "q_tok%d" % kt) for kt in range(2)]
+
+        def gather_pairs(g):
+            words = ga[g][:].rearrange("p u j -> p (u j)").bitcast(U32).rearrange("p (u h) -> p u h", h=2)
+            nc.vector.tensor_copy(out=words[:, :, 1], in_=da_hi[:].bitcast(U32).indirect(offsets(list_a, g)))
 
         def quantise(src, name):
-            codes = tile([P, G], U32, name + "_w")
-            scales = tile([P, G], U8, name + "_s")
+            slots = src.shape[1]
+            codes = tile([P, slots], U32, name + "_w")
+            scales = tile([P, slots], U8, name + "_s")
             nc.vector.quantize_mx(out=codes[:].bitcast(FP8X4), scales=scales[:], in_=src[:].rearrange("p u j -> p (u j)"))
             return codes, scales
 
-        def dc_mult(h, th):
+        def dc_mult(th):
             cols = slice(th * 256, (th + 1) * 256)
-            nc.vector.tensor_tensor(out=dc[:, 2 * h : 2 * h + 2, cols], in0=dh[h, th][:], in1=a_sb[:, 2 * h : 2 * h + 2, cols], op=MULT)
+            nc.vector.tensor_tensor(out=dc_hi[:, :, cols], in0=dh_hi[th][:], in1=a_hi[th][:], op=MULT)
 
-        def first_pool(g, bank_name):
-            codes, scales = quantise(ga[g], "qa%d" % g)
-            bank = ps.tile([P, 2, G], F32, name="r%d" % g, tag=bank_name)
+        def first_pool(g, codes, scales, bank_tags):
+            banks = [ps.tile([P, 2, G], F32, name="r%d_%s" % (g, tag), tag=tag) for tag in bank_tags]
             for kt in range(2):
                 nc.tensor.matmul_mx(
-                    out=bank[:, kt, :],
+                    out=banks[kt % len(banks)][:, kt, :],
                     lhsT=wa_w[:, g, kt * 256 : (kt + 1) * 256].bitcast(FP4X4),
                     lhsT_scale=wa_sc[:, g, kt * 128 : (kt + 1) * 128],
                     rhs=codes[:].bitcast(FP8X4),
@@ -148,19 +191,16 @@ def tile_moe_plb_none_kernel(
                     start=True,
                     stop=True,
                 )
-            return bank
+            return banks
 
-        gc = [tile([P, G, 4], BF16, "gc%d" % g) for g in range(2)]
-
-        def second_pool(g):
-            codes, scales = quantise(gc[g], "qc%d" % g)
-            bank = ps.tile([P, 2, G], F32, name="q%d" % g)
+        def second_pool(src, f0, bank, name):
+            codes, scales = quantise(src, name)
             for kt in range(2):
-                for fl in range(2):
-                    f = 2 * g + fl
+                for fl in range(src.shape[1] // C2):
+                    f = f0 + fl
                     cols = slice(fl * C2, (fl + 1) * C2)
                     nc.tensor.matmul_mx(
-                        out=bank[:, kt, cols],
+                        out=bank[:, kt, (f % 2) * C2 : (f % 2 + 1) * C2],
                         lhsT=wb_w[:, f, kt * 128 : (kt + 1) * 128].bitcast(FP8X4),
                         lhsT_scale=wb_sc[:, f, kt * 128 : (kt + 1) * 128],
                         rhs=codes[:, cols].bitcast(FP8X4),
@@ -168,38 +208,44 @@ def tile_moe_plb_none_kernel(
                         start=True,
                         stop=True,
                     )
-            return bank
 
-        def gather_c(g, j):
-            nc.scalar.activation(gc[g][:, :, j], dc[:, j, :].indirect(offsets(list_c, g)), COPY)
+        def gather_c(f0, experts, name, slot):
+            dst = tile([P, experts * C2, 4], BF16, name, tag=slot)
+            lst = list_c[:, f0 * (C2 // 16) : (f0 + experts) * (C2 // 16)]
+            for j in range(4):
+                window = dc_row[j][:] if j < 2 else dc_hi[:, j - 2, :]
+                nc.scalar.activation(dst[:, :, j], window.indirect(lst), COPY)
+            return dst
 
         def way_back(bank, kt, dst, lst, g, name):
             res = tile([P, G], F32, name)
             nc.scalar.activation(res[:], bank[:, kt, :], COPY)
             nc.vector.tensor_copy(out=dst[kt][:].indirect(offsets(lst, g)), in_=res[:])
 
-        r0 = first_pool(0, "r0")
-        dc_mult(0, 0)
-        dc_mult(0, 1)
-        dc_mult(1, 0)
-        dc_mult(1, 1)
-        r1 = first_pool(1, "dh11")
-        way_back(r0, 0, r_tok, list_a, 0, "r00")
-        way_back(r0, 1, r_tok, list_a, 0, "r01")
-        for j in range(3):
-            gather_c(0, j)
-        way_back(r1, 0, r_tok, list_a, 1, "r10")
-        gather_c(0, 3)
-        q0 = second_pool(0)
-        way_back(r1, 1, r_tok, list_a, 1, "r11")
-        for j in range(3):
-            gather_c(1, j)
+        dc_row_mult(1, 1)
+        gather_pairs(0)
+        gather_pairs(1)
+        qa = [quantise(ga[g], "qa%d" % g) for g in range(2)]
+        r0 = first_pool(0, *qa[0], ["r00", "r01"])
+        dc_mult(0)
+        dc_mult(1)
+        r1 = first_pool(1, *qa[1], ["dh_hi1"])
+        way_back(r0[0], 0, r_tok, list_a, 0, "r00")
+        way_back(r0[1], 1, r_tok, list_a, 0, "r01")
+        q0 = ps.tile([P, 2, G], F32, name="q0", tag="dh01")
+        q1 = ps.tile([P, 2, G], F32, name="q1", tag="dh10")
+        second_pool(gather_c(0, 2, "gc01", "gc01"), 0, q0, "qc01")
+        way_back(r1[0], 0, r_tok, list_a, 1, "r10")
+        way_back(r1[0], 1, r_tok, list_a, 1, "r11")
+        second_pool(gather_c(2, 1, "gc2", "qa1_w"), 2, q1, "qc2")
         way_back(q0, 0, q_tok, list_c, 0, "q00")
-        gather_c(1, 3)
-        q1 = second_pool(1)
+        second_pool(gather_c(3, 1, "gc3", "qc01_w"), 3, q1, "qc3")
         way_back(q0, 1, q_tok, list_c, 0, "q01")
         for kt in range(2):
             way_back(q1, kt, q_tok, list_c, 1, "q1%d" % kt)
-            res = tile([P, T], F32, "res%d" % kt)
-            nc.vector.tensor_tensor(out=res[:], in0=r_tok[kt][:], in1=q_tok[kt][:], op=ADD)
-            nc.sync.dma_start(out=out[kt * P : (kt + 1) * P, :], in_=res[:])
+            parts = kt + 1
+            for part in range(parts):
+                cols = slice(part * T // parts, (part + 1) * T // parts)
+                res = tile([P, T // parts], F32, "res%d%d" % (kt, part))
+                nc.vector.tensor_tensor(out=res[:], in0=r_tok[kt][:, cols], in1=q_tok[kt][:, cols], op=ADD)
+                [nc.sync, nc.scalar][part].dma_start(out=out[kt * P : (kt + 1) * P, cols], in_=res[:])

@@ -152,9 +152,9 @@ def tile_moe_plb_none_kernel(
                 for e in range(2):
                     first_product(bank[:, e, tq * 128 : (tq + 1) * 128], 1, e, th * 256 + tq * 128, 128)
             nc.vector.tensor_tensor(
-                out=da_hi[:, th * 512 : (th + 1) * 512].rearrange("p (t e) -> p t e", e=2),
-                in0=bank[:].rearrange("p e t -> p t e"),
-                in1=c_hi[:, :, th * 256 : (th + 1) * 256].rearrange("p e t -> p t e"),
+                out=da_hi[:, th * 512 : (th + 1) * 512].rearrange("p (u i e) -> p u e i", i=4, e=2),
+                in0=bank[:].rearrange("p e (u i) -> p u e i", i=4),
+                in1=c_hi[:, :, th * 256 : (th + 1) * 256].rearrange("p e (u i) -> p u e i", i=4),
                 op=MULT,
             )
 

@@ -1,6 +1,7 @@
 from contextlib import ExitStack
 
 import concourse.mybir as mybir
+from concourse.masks import make_identity
 
 K, T, H, N = 256, 512, 512, 1024
 E1, C1, E2, C2 = 2, 256, 4, 128
@@ -73,7 +74,7 @@ def tile_moe_plb_none_kernel(
         load_scale_row(nc.sync, dy_sc, dy_rows, 0)
         load_scale_row(nc.sync, dy_sc, dy_rows, 1)
         nc.sync.dma_start(out=dy_w[:], in_=dy_words.rearrange("s p t d -> p s (t d)").bitcast(I32))
-        load_scale_row(nc.scalar, dy_sc, dy_rows, 2)
+        load_scale_row(nc.sync, dy_sc, dy_rows, 2)
         load_scale_row(nc.sync, dy_sc, dy_rows, 3)
         nc.sync.dma_start(out=c_row[0][:], in_=c_view[:, 0, :])
         nc.sync.dma_start(out=a_row0[:], in_=a_view[:, 0, :])
@@ -101,6 +102,9 @@ def tile_moe_plb_none_kernel(
         load_scale_row(nc.sync, wa_sc, wa_rows, 3)
         nc.sync.dma_start(out=a_hi[1][:], in_=a_view[:, 2:4, 256:512])
         nc.sync.dma_start(out=wb_w[:], in_=wbt_words.rearrange("f s p k d -> p (f s) (k d)").bitcast(I32))
+
+        ident = tile([P, P], F32, "ident", tag="w2_raw")
+        make_identity(nc, ident[:])
 
         def first_product(dst, h, e, t0, n):
             for s in range(PASSES):
@@ -217,8 +221,8 @@ def tile_moe_plb_none_kernel(
                 nc.scalar.activation(dst[:, :, j], window.indirect(lst), COPY)
             return dst
 
-        def way_back(bank, kt, dst, lst, g, name):
-            res = tile([P, G], F32, name)
+        def way_back(bank, kt, dst, lst, g, name, slot=None):
+            res = tile([P, G], F32, name, tag=slot)
             nc.scalar.activation(res[:], bank[:, kt, :], COPY)
             nc.vector.tensor_copy(out=dst[kt][:].indirect(offsets(lst, g)), in_=res[:])
 
@@ -236,16 +240,36 @@ def tile_moe_plb_none_kernel(
         q1 = ps.tile([P, 2, G], F32, name="q1", tag="dh10")
         second_pool(gather_c(0, 2, "gc01", "gc01"), 0, q0, "qc01")
         way_back(r1[0], 0, r_tok, list_a, 1, "r10")
-        way_back(r1[0], 1, r_tok, list_a, 1, "r11")
         second_pool(gather_c(2, 1, "gc2", "qa1_w"), 2, q1, "qc2")
         way_back(q0, 0, q_tok, list_c, 0, "q00")
         second_pool(gather_c(3, 1, "gc3", "qc01_w"), 3, q1, "qc3")
         way_back(q0, 1, q_tok, list_c, 0, "q01")
-        for kt in range(2):
-            way_back(q1, kt, q_tok, list_c, 1, "q1%d" % kt)
-            parts = kt + 1
-            for part in range(parts):
-                cols = slice(part * T // parts, (part + 1) * T // parts)
-                res = tile([P, T // parts], F32, "res%d%d" % (kt, part))
-                nc.vector.tensor_tensor(out=res[:], in0=r_tok[kt][:, cols], in1=q_tok[kt][:, cols], op=ADD)
-                [nc.sync, nc.scalar][part].dma_start(out=out[kt * P : (kt + 1) * P, cols], in_=res[:])
+        way_back(q1, 0, q_tok, list_c, 1, "q10")
+        way_back(r1[0], 1, r_tok, list_a, 1, "r11", "qc3_w")
+        way_back(q1, 1, q_tok, list_c, 1, "q11")
+
+        turned = [ps.tile([P, P], F32, name="turned%d" % b, tag=tag) for b, tag in enumerate(["dh01", "dh_hi1", "dh10", "dh00"])]
+
+        def turn(src, b, first):
+            nc.tensor.matmul(turned[b][:], src[:, b * P : (b + 1) * P], ident[:], start=first, stop=not first, is_transpose=True)
+
+        for b in range(3):
+            turn(r_tok[0], b, True)
+        for b in range(3):
+            turn(q_tok[0], b, False)
+        turn(q_tok[0], 3, True)
+        turn(r_tok[0], 3, False)
+        back = ps.tile([P, T], F32, name="back", tag="r01")
+        for b in range(4):
+            sum_t = tile([P, P], F32, "sum_t%d" % b)
+            nc.scalar.activation(sum_t[:], turned[b][:], COPY)
+            nc.tensor.transpose(back[:, b * P : (b + 1) * P], sum_t[:], ident[:])
+        res0 = tile([P, T], F32, "res0")
+        nc.scalar.activation(res0[:], back[:], COPY)
+        nc.scalar.dma_start(out=out[0:P, :], in_=res0[:])
+
+        for part in range(2):
+            cols = slice(part * T // 2, (part + 1) * T // 2)
+            res = tile([P, T // 2], F32, "res1%d" % part)
+            nc.vector.tensor_tensor(out=res[:], in0=r_tok[1][:, cols], in1=q_tok[1][:, cols], op=ADD)
+            nc.sync.dma_start(out=out[P : 2 * P, cols], in_=res[:])

@@ -1,7 +1,6 @@
 from contextlib import ExitStack
 
 import concourse.mybir as mybir
-from concourse.masks import make_identity
 
 K, T, H, N = 256, 512, 512, 1024
 E1, C1, E2, C2 = 2, 256, 4, 128
@@ -83,8 +82,9 @@ def tile_moe_plb_none_kernel(
         nc.sync.dma_start(out=a_row1[0][:], in_=a_view[:, 1, 0:256])
         nc.sync.dma_start(out=c_hi[:], in_=c_view[:, 2:4, :])
         nc.sync.dma_start(out=a_row1[1][:], in_=a_view[:, 1, 256:512])
-        nc.sync.dma_start(list_c[:], offs2)
         nc.sync.dma_start(out=wa_w[:].bitcast(I32), in_=wat_words.rearrange("e s p b -> p (e s) b").bitcast(I32))
+        nc.sync.dma_start(out=a_hi[0][:], in_=a_view[:, 2:4, 0:256])
+        nc.sync.dma_start(out=a_hi[1][:], in_=a_view[:, 2:4, 256:512])
 
         w2_p = [tile([P, PASSES, 2, 2 * P], U8, "w2_p%d" % h) for h in range(2)]
         w2_sc = [tile([P, PASSES, 2, P], U8, "w2_sc%d" % h) for h in range(2)]
@@ -96,15 +96,10 @@ def tile_moe_plb_none_kernel(
 
         wa_sc = w2_sc_raw[:, 0, :].rearrange("p (e k) -> p e k", k=K)
         wa_rows = wat_scales.rearrange("e s (q r) k -> r q (e s) k", r=4)
-        for r in range(3):
+        for r in range(4):
             load_scale_row(nc.sync, wa_sc, wa_rows, r)
-        nc.sync.dma_start(out=a_hi[0][:], in_=a_view[:, 2:4, 0:256])
-        load_scale_row(nc.sync, wa_sc, wa_rows, 3)
-        nc.sync.dma_start(out=a_hi[1][:], in_=a_view[:, 2:4, 256:512])
+        nc.sync.dma_start(list_c[:], offs2)
         nc.sync.dma_start(out=wb_w[:], in_=wbt_words.rearrange("f s p k d -> p (f s) (k d)").bitcast(I32))
-
-        ident = tile([P, P], F32, "ident", tag="w2_raw")
-        make_identity(nc, ident[:])
 
         def first_product(dst, h, e, t0, n):
             for s in range(PASSES):
@@ -118,14 +113,15 @@ def tile_moe_plb_none_kernel(
                     stop=(s == PASSES - 1),
                 )
 
-        def offsets(lst, g):
-            return lst[:, g * (G // 16) : (g + 1) * (G // 16)]
+        def offsets(lst, s0, n):
+            return lst[:, s0 // 16 : (s0 + n) // 16]
 
         da_row = [tile([P, T], BF16, "da_row%d" % j) for j in range(2)]
         da_hi = tile([P, 2 * T], BF16, "da_hi")
         dc_row = [tile([P, T], BF16, "dc_row%d" % j) for j in range(2)]
-        dc_hi = tile([P, 2, T], BF16, "dc_hi")
-        ga = [tile([P, G, 4], BF16, "ga%d" % g) for g in range(2)]
+        dc_hi = [tile([P, T], BF16, "dc_hi%d" % e) for e in range(2)]
+        units = [(0, 128), (128, 128), (256, 256)]
+        ga = {s0: tile([P, n, 4], BF16, "ga%d" % s0) for s0, n in units}
 
         dh_row = {}
 
@@ -146,8 +142,8 @@ def tile_moe_plb_none_kernel(
                     dc_row_mult(j, th)
             if j == 1:
                 dc_row_mult(1, 0)
-            for g in range(2):
-                nc.scalar.activation(ga[g][:, :, j], da_row[j][:].indirect(offsets(list_a, g)), COPY)
+            for s0, n in units:
+                nc.scalar.activation(ga[s0][:, :, j], da_row[j][:].indirect(offsets(list_a, s0, n)), COPY)
         dh_hi = []
         for th in range(2):
             bank = ps.tile([P, 2, 256], F32, name="dh_hi%d" % th, tag="dh_hi%d" % th)
@@ -168,28 +164,38 @@ def tile_moe_plb_none_kernel(
         r_tok = [tile([P, T], F32, "r_tok%d" % kt) for kt in range(2)]
         q_tok = [tile([P, T], F32, "q_tok%d" % kt) for kt in range(2)]
 
-        def gather_pairs(g):
-            words = ga[g][:].rearrange("p u j -> p (u j)").bitcast(U32).rearrange("p (u h) -> p u h", h=2)
-            nc.vector.tensor_copy(out=words[:, :, 1], in_=da_hi[:].bitcast(U32).indirect(offsets(list_a, g)))
+        def gather_pairs(s0, n):
+            words = ga[s0][:].rearrange("p u j -> p (u j)").bitcast(U32).rearrange("p (u h) -> p u h", h=2)
+            nc.vector.tensor_copy(out=words[:, :, 1], in_=da_hi[:].bitcast(U32).indirect(offsets(list_a, s0, n)))
 
         def quantise(src, name):
             slots = src.shape[1]
             codes = tile([P, slots], U32, name + "_w")
             scales = tile([P, slots], U8, name + "_s")
-            nc.vector.quantize_mx(out=codes[:].bitcast(FP8X4), scales=scales[:], in_=src[:].rearrange("p u j -> p (u j)"))
+            nc.vector.quantize_mx(out=codes[:].bitcast(FP8X4), scales=scales[:], in_=src.rearrange("p u j -> p (u j)"))
             return codes, scales
 
-        def dc_mult(th):
-            cols = slice(th * 256, (th + 1) * 256)
-            nc.vector.tensor_tensor(out=dc_hi[:, :, cols], in0=dh_hi[th][:], in1=a_hi[th][:], op=MULT)
+        def dc_mult():
+            held = [tile([P, 2, 256], F32, "dh_held%d" % th) for th in range(2)]
+            for th in range(2):
+                nc.scalar.activation(held[th][:], dh_hi[th][:], COPY)
+            for e in range(2):
+                for th in range(2):
+                    cols = slice(th * 256, (th + 1) * 256)
+                    nc.gpsimd.tensor_tensor(out=dc_hi[e][:, cols], in0=held[th][:, e, :], in1=a_hi[th][:, e, :], op=MULT)
 
-        def first_pool(g, codes, scales, bank_tags):
-            banks = [ps.tile([P, 2, G], F32, name="r%d_%s" % (g, tag), tag=tag) for tag in bank_tags]
+        def banks_for(n, name, tags):
+            tiles = [ps.tile([P, 2, n], F32, name="bank_%s_%s" % (name, tag), tag=tag) for tag in tags]
+            return [tiles[kt % len(tiles)] for kt in range(2)]
+
+        def first_pool(s0, n, name, tags):
+            codes, scales = quantise(ga[s0][:], name)
+            banks = banks_for(n, name, tags)
             for kt in range(2):
                 nc.tensor.matmul_mx(
-                    out=banks[kt % len(banks)][:, kt, :],
-                    lhsT=wa_w[:, g, kt * 256 : (kt + 1) * 256].bitcast(FP4X4),
-                    lhsT_scale=wa_sc[:, g, kt * 128 : (kt + 1) * 128],
+                    out=banks[kt][:, kt, :],
+                    lhsT=wa_w[:, s0 // G, kt * 256 : (kt + 1) * 256].bitcast(FP4X4),
+                    lhsT_scale=wa_sc[:, s0 // G, kt * 128 : (kt + 1) * 128],
                     rhs=codes[:].bitcast(FP8X4),
                     rhs_scale=scales[:],
                     start=True,
@@ -197,14 +203,14 @@ def tile_moe_plb_none_kernel(
                 )
             return banks
 
-        def second_pool(src, f0, bank, name):
-            codes, scales = quantise(src, name)
+        def second_pool(src, f0, banks, name):
+            codes, scales = quantise(src[:], name)
             for kt in range(2):
                 for fl in range(src.shape[1] // C2):
                     f = f0 + fl
                     cols = slice(fl * C2, (fl + 1) * C2)
                     nc.tensor.matmul_mx(
-                        out=bank[:, kt, (f % 2) * C2 : (f % 2 + 1) * C2],
+                        out=banks[kt][:, kt, (f % 2) * C2 : (f % 2 + 1) * C2],
                         lhsT=wb_w[:, f, kt * 128 : (kt + 1) * 128].bitcast(FP8X4),
                         lhsT_scale=wb_sc[:, f, kt * 128 : (kt + 1) * 128],
                         rhs=codes[:, cols].bitcast(FP8X4),
@@ -213,59 +219,45 @@ def tile_moe_plb_none_kernel(
                         stop=True,
                     )
 
-        def gather_c(f0, experts, name, slot):
-            dst = tile([P, experts * C2, 4], BF16, name, tag=slot)
-            lst = list_c[:, f0 * (C2 // 16) : (f0 + experts) * (C2 // 16)]
-            for j in range(4):
-                window = dc_row[j][:] if j < 2 else dc_hi[:, j - 2, :]
-                nc.scalar.activation(dst[:, :, j], window.indirect(lst), COPY)
+        def gather_c(dst, f0, rows=range(4)):
+            for j in rows:
+                window = dc_row[j] if j < 2 else dc_hi[j - 2]
+                nc.scalar.activation(dst[:, :, j], window[:].indirect(offsets(list_c, f0 * C2, dst.shape[1])), COPY)
             return dst
 
-        def way_back(bank, kt, dst, lst, g, name, slot=None):
-            res = tile([P, G], F32, name, tag=slot)
-            nc.scalar.activation(res[:], bank[:, kt, :], COPY)
-            nc.vector.tensor_copy(out=dst[kt][:].indirect(offsets(lst, g)), in_=res[:])
+        def way_back(banks, kts, dst, lst, s0, name, slot=None):
+            n = banks[0].shape[2]
+            res = tile([P, len(kts), n], F32, name, tag=slot)
+            nc.scalar.activation(res[:], banks[kts[0]][:, kts[0] : kts[-1] + 1, :], COPY)
+            for i, kt in enumerate(kts):
+                nc.vector.tensor_copy(out=dst[kt][:].indirect(offsets(lst, s0, n)), in_=res[:, i, :])
 
         dc_row_mult(1, 1)
-        gather_pairs(0)
-        gather_pairs(1)
-        qa = [quantise(ga[g], "qa%d" % g) for g in range(2)]
-        r0 = first_pool(0, *qa[0], ["r00", "r01"])
-        dc_mult(0)
-        dc_mult(1)
-        r1 = first_pool(1, *qa[1], ["dh_hi1"])
-        way_back(r0[0], 0, r_tok, list_a, 0, "r00")
-        way_back(r0[1], 1, r_tok, list_a, 0, "r01")
-        q0 = ps.tile([P, 2, G], F32, name="q0", tag="dh01")
-        q1 = ps.tile([P, 2, G], F32, name="q1", tag="dh10")
-        second_pool(gather_c(0, 2, "gc01", "gc01"), 0, q0, "qc01")
-        way_back(r1[0], 0, r_tok, list_a, 1, "r10")
-        second_pool(gather_c(2, 1, "gc2", "qa1_w"), 2, q1, "qc2")
-        way_back(q0, 0, q_tok, list_c, 0, "q00")
-        second_pool(gather_c(3, 1, "gc3", "qc01_w"), 3, q1, "qc3")
-        way_back(q0, 1, q_tok, list_c, 0, "q01")
-        way_back(q1, 0, q_tok, list_c, 1, "q10")
-        way_back(r1[0], 1, r_tok, list_a, 1, "r11", "qc3_w")
-        way_back(q1, 1, q_tok, list_c, 1, "q11")
+        dc_mult()
+        gather_pairs(0, 128)
+        gather_pairs(256, 256)
+        r0 = first_pool(0, 128, "qa0", ["r00"])
+        gather_pairs(128, 128)
+        r2 = first_pool(256, 256, "qa2", ["dh11", "dh_hi0"])
+        r1 = first_pool(128, 128, "qa1", ["r01"])
+        way_back(r0, [0, 1], r_tok, list_a, 0, "r0")
+        way_back(r1, [0, 1], r_tok, list_a, 128, "r1")
+        gc0 = tile([P, G, 4], BF16, "gc0", tag="qa0_w")
+        gather_c(gc0, 0, [0])
+        way_back(r2, [0], r_tok, list_a, 256, "r20")
+        q0 = banks_for(G, "q0", ["dh00", "dh01"])
+        q1 = banks_for(G, "q1", ["dh10"])
+        second_pool(gather_c(gc0, 0, [1, 2, 3]), 0, q0, "qc0")
+        way_back(r2, [1], r_tok, list_a, 256, "r21")
+        second_pool(gather_c(tile([P, C2, 4], BF16, "gc2", tag="qa2_s"), 2), 2, q1, "qc2")
+        way_back(q0, [0], q_tok, list_c, 0, "q00")
+        second_pool(gather_c(tile([P, C2, 4], BF16, "gc3", tag="qc0_w"), 3), 3, q1, "qc3")
+        way_back(q0, [1], q_tok, list_c, 0, "q01")
+        way_back(q1, [0], q_tok, list_c, 256, "q10")
+        way_back(q1, [1], q_tok, list_c, 256, "q11")
 
-        turned = [ps.tile([P, P], F32, name="turned%d" % b, tag=tag) for b, tag in enumerate(["dh01", "dh_hi1", "dh10", "dh00"])]
-
-        def turn(src, b, first):
-            nc.tensor.matmul(turned[b][:], src[:, b * P : (b + 1) * P], ident[:], start=first, stop=not first, is_transpose=True)
-
-        for b in range(3):
-            turn(r_tok[0], b, True)
-        for b in range(3):
-            turn(q_tok[0], b, False)
-        turn(q_tok[0], 3, True)
-        turn(r_tok[0], 3, False)
-        back = ps.tile([P, T], F32, name="back", tag="r01")
-        for b in range(4):
-            sum_t = tile([P, P], F32, "sum_t%d" % b)
-            nc.scalar.activation(sum_t[:], turned[b][:], COPY)
-            nc.tensor.transpose(back[:, b * P : (b + 1) * P], sum_t[:], ident[:])
         res0 = tile([P, T], F32, "res0")
-        nc.scalar.activation(res0[:], back[:], COPY)
+        nc.gpsimd.tensor_tensor(out=res0[:], in0=r_tok[0][:], in1=q_tok[0][:], op=ADD)
         nc.scalar.dma_start(out=out[0:P, :], in_=res0[:])
 
         for part in range(2):

@@ -49,7 +49,7 @@ def tile_moe_plb_none_kernel(
         a_row0 = tile([P, T], F32, "a_row0")
         a_row1 = [tile([P, 256], F32, "a_row1%d" % th) for th in range(2)]
         c_hi = tile([P, 2, T], F32, "c_hi")
-        a_hi = [tile([P, 2, 256], F32, "a_hi%d" % th) for th in range(2)]
+        a_hi = tile([P, 2, T], F32, "a_hi")
         wa_w = tile([P, E1, 2 * K], U8, "wa_w")
         wb_w = tile([P, E2, K], I32, "wb_w")
 
@@ -83,8 +83,7 @@ def tile_moe_plb_none_kernel(
         nc.sync.dma_start(out=c_hi[:], in_=c_view[:, 2:4, :])
         nc.sync.dma_start(out=a_row1[1][:], in_=a_view[:, 1, 256:512])
         nc.sync.dma_start(out=wa_w[:].bitcast(I32), in_=wat_words.rearrange("e s p b -> p (e s) b").bitcast(I32))
-        nc.sync.dma_start(out=a_hi[0][:], in_=a_view[:, 2:4, 0:256])
-        nc.sync.dma_start(out=a_hi[1][:], in_=a_view[:, 2:4, 256:512])
+        nc.sync.dma_start(out=a_hi[:], in_=a_view[:, 2:4, :])
 
         w2_p = [tile([P, PASSES, 2, 2 * P], U8, "w2_p%d" % h) for h in range(2)]
         w2_sc = [tile([P, PASSES, 2, P], U8, "w2_sc%d" % h) for h in range(2)]
@@ -119,7 +118,6 @@ def tile_moe_plb_none_kernel(
         da_row = [tile([P, T], BF16, "da_row%d" % j) for j in range(2)]
         da_hi = tile([P, 2 * T], BF16, "da_hi")
         dc_row = [tile([P, T], BF16, "dc_row%d" % j) for j in range(2)]
-        dc_hi = [tile([P, T], BF16, "dc_hi%d" % e) for e in range(2)]
         units = [(0, 128), (128, 128), (256, 256)]
         ga = {s0: tile([P, n, 4], BF16, "ga%d" % s0) for s0, n in units}
 
@@ -175,14 +173,7 @@ def tile_moe_plb_none_kernel(
             nc.vector.quantize_mx(out=codes[:].bitcast(FP8X4), scales=scales[:], in_=src.rearrange("p u j -> p (u j)"))
             return codes, scales
 
-        def dc_mult():
-            held = [tile([P, 2, 256], F32, "dh_held%d" % th) for th in range(2)]
-            for th in range(2):
-                nc.scalar.activation(held[th][:], dh_hi[th][:], COPY)
-            for e in range(2):
-                for th in range(2):
-                    cols = slice(th * 256, (th + 1) * 256)
-                    nc.gpsimd.tensor_tensor(out=dc_hi[e][:, cols], in0=held[th][:, e, :], in1=a_hi[th][:, e, :], op=MULT)
+        held = tile([P, 2, T], F32, "dh_held")
 
         def banks_for(n, name, tags):
             tiles = [ps.tile([P, 2, n], F32, name="bank_%s_%s" % (name, tag), tag=tag) for tag in tags]
@@ -219,40 +210,57 @@ def tile_moe_plb_none_kernel(
                         stop=True,
                     )
 
-        def gather_c(dst, f0, rows=range(4)):
+        def gather_c(pairs, g, rows):
             for j in rows:
-                window = dc_row[j] if j < 2 else dc_hi[j - 2]
-                nc.scalar.activation(dst[:, :, j], window[:].indirect(offsets(list_c, f0 * C2, dst.shape[1])), COPY)
+                window = dc_row[j][:] if j < 2 else dc_hi[:, j - 2, :]
+                nc.scalar.activation(pairs[:, j // 2, :, j % 2], window.indirect(offsets(list_c, g * G, G)), COPY)
+
+        def weave(pairs, name, slot=None):
+            dst = tile([P, G, 4], BF16, name, tag=slot)
+            nc.gpsimd.tensor_copy(
+                out=dst[:].rearrange("p u j -> p (u j)").bitcast(U32).rearrange("p (u h) -> p u h", h=2),
+                in_=pairs.rearrange("p h u e -> p (h u e)").bitcast(U32).rearrange("p (h u) -> p u h", h=2),
+            )
             return dst
 
-        def way_back(banks, kts, dst, lst, s0, name, slot=None):
+        def way_back(banks, kts, dst, lst, s0, name, room=None):
             n = banks[0].shape[2]
-            res = tile([P, len(kts), n], F32, name, tag=slot)
-            nc.scalar.activation(res[:], banks[kts[0]][:, kts[0] : kts[-1] + 1, :], COPY)
+            if room is None:
+                res = tile([P, len(kts), n], F32, name)[:]
+            else:
+                res = room.rearrange("p h u e -> p h (u e)").bitcast(F32)
+            nc.scalar.activation(res, banks[kts[0]][:, kts[0] : kts[-1] + 1, :], COPY)
             for i, kt in enumerate(kts):
                 nc.vector.tensor_copy(out=dst[kt][:].indirect(offsets(lst, s0, n)), in_=res[:, i, :])
 
         dc_row_mult(1, 1)
-        dc_mult()
+        for th in range(2):
+            nc.scalar.activation(held[:, :, th * 256 : (th + 1) * 256], dh_hi[th][:], COPY)
         gather_pairs(0, 128)
         gather_pairs(256, 256)
         r0 = first_pool(0, 128, "qa0", ["r00"])
         gather_pairs(128, 128)
         r2 = first_pool(256, 256, "qa2", ["dh11", "dh_hi0"])
         r1 = first_pool(128, 128, "qa1", ["r01"])
+        dc_hi = tile([P, 2, T], BF16, "dc_hi", tag="ga128")
+        for e in range(2):
+            nc.gpsimd.tensor_tensor(out=dc_hi[:, e, :], in0=held[:, e, :], in1=a_hi[:, e, :], op=MULT)
         way_back(r0, [0, 1], r_tok, list_a, 0, "r0")
         way_back(r1, [0, 1], r_tok, list_a, 128, "r1")
-        gc0 = tile([P, G, 4], BF16, "gc0", tag="qa0_w")
-        gather_c(gc0, 0, [0])
+        rooms = tile([P, 3, G, 2], BF16, "rooms", tag="qa0_w")
+        pairs0, pairs1 = rooms[:, 0:2], rooms[:, 1:3]
+        gather_c(pairs0, 0, [0])
         way_back(r2, [0], r_tok, list_a, 256, "r20")
         q0 = banks_for(G, "q0", ["dh00", "dh01"])
         q1 = banks_for(G, "q1", ["dh10"])
-        second_pool(gather_c(gc0, 0, [1, 2, 3]), 0, q0, "qc0")
-        way_back(r2, [1], r_tok, list_a, 256, "r21")
-        second_pool(gather_c(tile([P, C2, 4], BF16, "gc2", tag="qa2_s"), 2), 2, q1, "qc2")
+        gather_c(pairs0, 0, [1, 2, 3])
+        second_pool(weave(pairs0, "gc0"), 0, q0, "qc0")
+        gather_c(pairs1, 1, [2, 3])
+        way_back(r2, [1], r_tok, list_a, 256, "r21", rooms[:, 0:1])
+        gather_c(pairs1, 1, [0, 1])
         way_back(q0, [0], q_tok, list_c, 0, "q00")
-        second_pool(gather_c(tile([P, C2, 4], BF16, "gc3", tag="qc0_w"), 3), 3, q1, "qc3")
-        way_back(q0, [1], q_tok, list_c, 0, "q01")
+        second_pool(weave(pairs1, "gc1", "qc0_w"), 2, q1, "qc1")
+        way_back(q0, [1], q_tok, list_c, 0, "q01", rooms[:, 2:3])
         way_back(q1, [0], q_tok, list_c, 256, "q10")
         way_back(q1, [1], q_tok, list_c, 256, "q11")
 

@@ -83,6 +83,7 @@ def tile_moe_plb_none_kernel(
         nc.sync.dma_start(out=c_hi[:], in_=c_view[:, 2:4, :])
         nc.sync.dma_start(out=a_row1[1][:], in_=a_view[:, 1, 256:512])
         nc.sync.dma_start(out=wa_w[:].bitcast(I32), in_=wat_words.rearrange("e s p b -> p (e s) b").bitcast(I32))
+
         nc.sync.dma_start(out=a_hi[:], in_=a_view[:, 2:4, :])
 
         w2_p = [tile([P, PASSES, 2, 2 * P], U8, "w2_p%d" % h) for h in range(2)]
@@ -118,7 +119,7 @@ def tile_moe_plb_none_kernel(
         da_row = [tile([P, T], BF16, "da_row%d" % j) for j in range(2)]
         da_hi = tile([P, 2 * T], BF16, "da_hi")
         dc_row = [tile([P, T], BF16, "dc_row%d" % j) for j in range(2)]
-        units = [(0, 128), (128, 128), (256, 256)]
+        units = [(0, 128), (256, 256)]
         ga = {s0: tile([P, n, 4], BF16, "ga%d" % s0) for s0, n in units}
 
         dh_row = {}
@@ -174,6 +175,9 @@ def tile_moe_plb_none_kernel(
             return codes, scales
 
         held = tile([P, 2, T], F32, "dh_held")
+
+        def hold_bank(th):
+            nc.scalar.activation(held[:, :, th * 256 : (th + 1) * 256], dh_hi[th][:], COPY)
 
         def banks_for(n, name, tags):
             tiles = [ps.tile([P, 2, n], F32, name="bank_%s_%s" % (name, tag), tag=tag) for tag in tags]
@@ -234,18 +238,22 @@ def tile_moe_plb_none_kernel(
                 nc.vector.tensor_copy(out=dst[kt][:].indirect(offsets(lst, s0, n)), in_=res[:, i, :])
 
         dc_row_mult(1, 1)
-        for th in range(2):
-            nc.scalar.activation(held[:, :, th * 256 : (th + 1) * 256], dh_hi[th][:], COPY)
+        hold_bank(0)
+        ga[128] = tile([P, 128, 4], BF16, "ga128", tag="c_hi")
+        for j in range(2):
+            nc.scalar.activation(ga[128][:, :, j], da_row[j][:].indirect(offsets(list_a, 128, 128)), COPY)
+        hold_bank(1)
         gather_pairs(0, 128)
         gather_pairs(256, 256)
-        r0 = first_pool(0, 128, "qa0", ["r00"])
+        r0 = first_pool(0, 128, "qa0", ["r00", "r01"])
         gather_pairs(128, 128)
         r2 = first_pool(256, 256, "qa2", ["dh11", "dh_hi0"])
-        r1 = first_pool(128, 128, "qa1", ["r01"])
-        dc_hi = tile([P, 2, T], BF16, "dc_hi", tag="ga128")
+        r1 = first_pool(128, 128, "qa1", ["dh00"])
+        dc_hi = tile([P, 2, T], BF16, "dc_hi", tag="c_hi")
         for e in range(2):
             nc.gpsimd.tensor_tensor(out=dc_hi[:, e, :], in0=held[:, e, :], in1=a_hi[:, e, :], op=MULT)
-        way_back(r0, [0, 1], r_tok, list_a, 0, "r0")
+        way_back(r0, [0], r_tok, list_a, 0, "r00")
+        way_back(r0, [1], r_tok, list_a, 0, "r01")
         way_back(r1, [0, 1], r_tok, list_a, 128, "r1")
         rooms = tile([P, 3, G, 2], BF16, "rooms", tag="qa0_w")
         pairs0, pairs1 = rooms[:, 0:2], rooms[:, 1:3]

@@ -46,8 +46,7 @@ def tile_moe_plb_none_kernel(
         w2_raw = tile([P, PASSES, 2 * H], U8, "w2_raw")
         dy_w = tile([P, PASSES, T], I32, "dy_w")
         c_row = [tile([P, T], F32, "c_row%d" % j) for j in range(2)]
-        a_row0 = tile([P, T], F32, "a_row0")
-        a_row1 = [tile([P, 256], F32, "a_row1%d" % th) for th in range(2)]
+        a_row = [tile([P, T], F32, "a_row%d" % j) for j in range(2)]
         c_hi = tile([P, 2, T], F32, "c_hi")
         a_hi = tile([P, 2, T], F32, "a_hi")
         wa_w = tile([P, E1, 2 * K], U8, "wa_w")
@@ -76,12 +75,11 @@ def tile_moe_plb_none_kernel(
         load_scale_row(nc.sync, dy_sc, dy_rows, 2)
         load_scale_row(nc.sync, dy_sc, dy_rows, 3)
         nc.sync.dma_start(out=c_row[0][:], in_=c_view[:, 0, :])
-        nc.sync.dma_start(out=a_row0[:], in_=a_view[:, 0, :])
         nc.sync.dma_start(list_a[:], offs)
         nc.sync.dma_start(out=c_row[1][:], in_=c_view[:, 1, :])
-        nc.sync.dma_start(out=a_row1[0][:], in_=a_view[:, 1, 0:256])
+        nc.sync.dma_start(out=a_row[1][:], in_=a_view[:, 1, :])
         nc.sync.dma_start(out=c_hi[:], in_=c_view[:, 2:4, :])
-        nc.sync.dma_start(out=a_row1[1][:], in_=a_view[:, 1, 256:512])
+        nc.sync.dma_start(out=a_row[0][:], in_=a_view[:, 0, :])
         nc.sync.dma_start(out=wa_w[:].bitcast(I32), in_=wat_words.rearrange("e s p b -> p (e s) b").bitcast(I32))
 
         nc.sync.dma_start(out=a_hi[:], in_=a_view[:, 2:4, :])
@@ -126,8 +124,9 @@ def tile_moe_plb_none_kernel(
 
         def dc_row_mult(j, th):
             cols = slice(th * 256, (th + 1) * 256)
-            factor = a_row0[:, cols] if j == 0 else a_row1[th][:]
-            nc.vector.tensor_tensor(out=dc_row[j][:, cols], in0=dh_row[j, th][:], in1=factor, op=MULT)
+            nc.vector.tensor_tensor(out=dc_row[j][:, cols], in0=dh_row[j, th][:], in1=a_row[j][:, cols], op=MULT)
+
+        held_row = [tile([P, 256], F32, "held_row%d" % th) for th in range(2)]
 
         for j in range(2):
             for th in range(2):
@@ -138,9 +137,11 @@ def tile_moe_plb_none_kernel(
                     first_product(bank[:, tq * 128 : (tq + 1) * 128], 0, j, th * 256 + tq * 128, 128)
                 nc.vector.tensor_tensor(out=da_row[j][:, cols], in0=bank[:], in1=c_row[j][:, cols], op=MULT)
                 if j == 0:
-                    dc_row_mult(j, th)
+                    nc.scalar.activation(held_row[th][:], bank[:], COPY)
+                    nc.gpsimd.tensor_tensor(out=dc_row[0][:, cols], in0=held_row[th][:], in1=a_row[0][:, cols], op=MULT)
             if j == 1:
                 dc_row_mult(1, 0)
+                dc_row_mult(1, 1)
             for s0, n in units:
                 nc.scalar.activation(ga[s0][:, :, j], da_row[j][:].indirect(offsets(list_a, s0, n)), COPY)
         dh_hi = []
@@ -237,7 +238,6 @@ def tile_moe_plb_none_kernel(
             for i, kt in enumerate(kts):
                 nc.vector.tensor_copy(out=dst[kt][:].indirect(offsets(lst, s0, n)), in_=res[:, i, :])
 
-        dc_row_mult(1, 1)
         hold_bank(0)
         ga[128] = tile([P, 128, 4], BF16, "ga128", tag="c_hi")
         for j in range(2):

@@ -47,7 +47,8 @@ def tile_moe_plb_none_kernel(
         dy_w = tile([P, PASSES, T], I32, "dy_w")
         c_row = [tile([P, T], F32, "c_row%d" % j) for j in range(2)]
         a_row = [tile([P, T], F32, "a_row%d" % j) for j in range(2)]
-        c_hi = tile([P, 2, T], F32, "c_hi")
+        c_buf = tile([P, 2 * T + 128], F32, "c_buf")
+        c_hi = c_buf[:, 0 : 2 * T].rearrange("p (e t) -> p e t", e=2)
         a_hi = tile([P, 2, T], F32, "a_hi")
         wa_w = tile([P, E1, 2 * K], U8, "wa_w")
         wb_w = tile([P, E2, K], I32, "wb_w")
@@ -78,11 +79,9 @@ def tile_moe_plb_none_kernel(
         nc.sync.dma_start(list_a[:], offs)
         nc.sync.dma_start(out=c_row[1][:], in_=c_view[:, 1, :])
         nc.sync.dma_start(out=a_row[1][:], in_=a_view[:, 1, :])
-        nc.sync.dma_start(out=c_hi[:], in_=c_view[:, 2:4, :])
+        nc.sync.dma_start(out=c_hi, in_=c_view[:, 2:4, :])
         nc.sync.dma_start(out=a_row[0][:], in_=a_view[:, 0, :])
         nc.sync.dma_start(out=wa_w[:].bitcast(I32), in_=wat_words.rearrange("e s p b -> p (e s) b").bitcast(I32))
-
-        nc.sync.dma_start(out=a_hi[:], in_=a_view[:, 2:4, :])
 
         w2_p = [tile([P, PASSES, 2, 2 * P], U8, "w2_p%d" % h) for h in range(2)]
         w2_sc = [tile([P, PASSES, 2, P], U8, "w2_sc%d" % h) for h in range(2)]
@@ -96,6 +95,7 @@ def tile_moe_plb_none_kernel(
         wa_rows = wat_scales.rearrange("e s (q r) k -> r q (e s) k", r=4)
         for r in range(4):
             load_scale_row(nc.sync, wa_sc, wa_rows, r)
+        nc.sync.dma_start(out=a_hi[:], in_=a_view[:, 2:4, :])
         nc.sync.dma_start(list_c[:], offs2)
         nc.sync.dma_start(out=wb_w[:], in_=wbt_words.rearrange("f s p k d -> p (f s) (k d)").bitcast(I32))
 
@@ -116,48 +116,46 @@ def tile_moe_plb_none_kernel(
 
         da_row = [tile([P, T], BF16, "da_row%d" % j) for j in range(2)]
         da_hi = tile([P, 2 * T], BF16, "da_hi")
-        dc_row = [tile([P, T], BF16, "dc_row%d" % j) for j in range(2)]
-        units = [(0, 128), (256, 256)]
-        ga = {s0: tile([P, n, 4], BF16, "ga%d" % s0) for s0, n in units}
+        dc_row = [c_buf[:, 2 * T - 128 : 2 * T + 128].bitcast(BF16), tile([P, T], BF16, "dc_row1")[:]]
+        first = tile([P, 1536], BF16, "first")
+        halves = [first[:, 0:1024].rearrange("p (u j) -> p u j", j=4), tile([P, 256, 4], BF16, "second")[:]]
+        ga = {0: halves[0][:, 0:128, :], 128: halves[0][:, 128:256, :], 256: halves[1]}
+        dc_hi = first[:, 512:1536].rearrange("p (e t) -> p e t", e=2)
 
-        dh_row = {}
-
-        def dc_row_mult(j, th):
-            cols = slice(th * 256, (th + 1) * 256)
-            nc.vector.tensor_tensor(out=dc_row[j][:, cols], in0=dh_row[j, th][:], in1=a_row[j][:, cols], op=MULT)
-
-        held_row = [tile([P, 256], F32, "held_row%d" % th) for th in range(2)]
-
-        for j in range(2):
-            for th in range(2):
-                cols = slice(th * 256, (th + 1) * 256)
-                bank = ps.tile([P, 256], F32, name="dh%d%d" % (j, th), tag="dh%d%d" % (j, th))
-                dh_row[j, th] = bank
-                for tq in range(2):
-                    first_product(bank[:, tq * 128 : (tq + 1) * 128], 0, j, th * 256 + tq * 128, 128)
-                nc.vector.tensor_tensor(out=da_row[j][:, cols], in0=bank[:], in1=c_row[j][:, cols], op=MULT)
-                if j == 0:
-                    nc.scalar.activation(held_row[th][:], bank[:], COPY)
-                    nc.gpsimd.tensor_tensor(out=dc_row[0][:, cols], in0=held_row[th][:], in1=a_row[0][:, cols], op=MULT)
-            if j == 1:
-                dc_row_mult(1, 0)
-                dc_row_mult(1, 1)
-            for s0, n in units:
-                nc.scalar.activation(ga[s0][:, :, j], da_row[j][:].indirect(offsets(list_a, s0, n)), COPY)
-        dh_hi = []
+        held_row = [first[:, 1022:1534].bitcast(F32), tile([P, 256], F32, "held_row1")[:]]
         for th in range(2):
-            bank = ps.tile([P, 2, 256], F32, name="dh_hi%d" % th, tag="dh_hi%d" % th)
-            dh_hi.append(bank)
+            cols = slice(th * 256, (th + 1) * 256)
+            bank = ps.tile([P, 256], F32, name="dh0%d" % th, tag="dh0%d" % th)
             for tq in range(2):
+                first_product(bank[:, tq * 128 : (tq + 1) * 128], 0, 0, th * 256 + tq * 128, 128)
+            nc.vector.tensor_tensor(out=da_row[0][:, cols], in0=bank[:], in1=c_row[0][:, cols], op=MULT)
+            nc.scalar.activation(held_row[th], bank[:], COPY)
+            if th == 1:
+                nc.gpsimd.tensor_tensor(out=dc_row[0][:, cols], in0=held_row[th], in1=a_row[0][:, cols], op=MULT)
+        for g in range(2):
+            nc.scalar.activation(halves[g][:, :, 0], da_row[0][:].indirect(offsets(list_a, g * G, G)), COPY)
+        bank = ps.tile([P, T], F32, name="dh1", tag="dh1")
+        first_product(bank[:], 0, 1, 0, T)
+        nc.vector.tensor_tensor(out=da_row[1][:], in0=bank[:], in1=c_row[1][:], op=MULT)
+        nc.vector.tensor_tensor(out=dc_row[1], in0=bank[:], in1=a_row[1][:], op=MULT)
+        for g in range(2):
+            nc.scalar.activation(halves[g][:, :, 1], da_row[1][:].indirect(offsets(list_a, g * G, G)), COPY)
+        spans = [(0, 256), (256, 128), (384, 128)]
+        dh_hi = []
+        for b, (t0, n) in enumerate(spans):
+            bank = ps.tile([P, 2, n], F32, name="dh_hi%d" % b, tag="dh_hi%d" % b)
+            dh_hi.append(bank)
+            for tq in range(n // 128):
                 for e in range(2):
-                    first_product(bank[:, e, tq * 128 : (tq + 1) * 128], 1, e, th * 256 + tq * 128, 128)
+                    first_product(bank[:, e, tq * 128 : (tq + 1) * 128], 1, e, t0 + tq * 128, 128)
             nc.vector.tensor_tensor(
-                out=da_hi[:, th * 512 : (th + 1) * 512].rearrange("p (u i e) -> p u e i", i=4, e=2),
+                out=da_hi[:, 2 * t0 : 2 * (t0 + n)].rearrange("p (u i e) -> p u e i", i=4, e=2),
                 in0=bank[:].rearrange("p e (u i) -> p u e i", i=4),
-                in1=c_hi[:, :, th * 256 : (th + 1) * 256].rearrange("p e (u i) -> p u e i", i=4),
+                in1=c_hi[:, :, t0 : t0 + n].rearrange("p e (u i) -> p u e i", i=4),
                 op=MULT,
             )
 
+        nc.gpsimd.tensor_tensor(out=dc_row[0][:, 0:256], in0=held_row[0], in1=a_row[0][:, 0:256], op=MULT)
         wb_sc = dy_sc[:].rearrange("p s (f k) -> p (s f) k", k=K)
         load_scale_rows([nc.sync] * 4, wb_sc, wbt_scales.rearrange("f s (q r) k -> r q (f s) k", r=4))
 
@@ -165,7 +163,7 @@ def tile_moe_plb_none_kernel(
         q_tok = [tile([P, T], F32, "q_tok%d" % kt) for kt in range(2)]
 
         def gather_pairs(s0, n):
-            words = ga[s0][:].rearrange("p u j -> p (u j)").bitcast(U32).rearrange("p (u h) -> p u h", h=2)
+            words = ga[s0].rearrange("p u j -> p (u j)").bitcast(U32).rearrange("p (u h) -> p u h", h=2)
             nc.vector.tensor_copy(out=words[:, :, 1], in_=da_hi[:].bitcast(U32).indirect(offsets(list_a, s0, n)))
 
         def quantise(src, name):
@@ -175,17 +173,16 @@ def tile_moe_plb_none_kernel(
             nc.vector.quantize_mx(out=codes[:].bitcast(FP8X4), scales=scales[:], in_=src.rearrange("p u j -> p (u j)"))
             return codes, scales
 
-        held = tile([P, 2, T], F32, "dh_held")
-
-        def hold_bank(th):
-            nc.scalar.activation(held[:, :, th * 256 : (th + 1) * 256], dh_hi[th][:], COPY)
+        def hold_bank(b, held, col0):
+            n = spans[b][1]
+            nc.scalar.activation(held[:, :, col0 : col0 + n], dh_hi[b][:], COPY)
 
         def banks_for(n, name, tags):
             tiles = [ps.tile([P, 2, n], F32, name="bank_%s_%s" % (name, tag), tag=tag) for tag in tags]
             return [tiles[kt % len(tiles)] for kt in range(2)]
 
         def first_pool(s0, n, name, tags):
-            codes, scales = quantise(ga[s0][:], name)
+            codes, scales = quantise(ga[s0], name)
             banks = banks_for(n, name, tags)
             for kt in range(2):
                 nc.tensor.matmul_mx(
@@ -215,60 +212,76 @@ def tile_moe_plb_none_kernel(
                         stop=True,
                     )
 
-        def gather_c(pairs, g, rows):
-            for j in rows:
-                window = dc_row[j][:] if j < 2 else dc_hi[:, j - 2, :]
-                nc.scalar.activation(pairs[:, j // 2, :, j % 2], window.indirect(offsets(list_c, g * G, G)), COPY)
+        def gather_c(plane, j, s0):
+            window = dc_row[j] if j < 2 else dc_hi[:, j - 2, :]
+            pairs = plane.bitcast(BF16).rearrange("p (u e) -> p u e", e=2)
+            nc.scalar.activation(pairs[:, :, j % 2], window.indirect(offsets(list_c, s0, plane.shape[1])), COPY)
 
-        def weave(pairs, name, slot=None):
-            dst = tile([P, G, 4], BF16, name, tag=slot)
+        def weave(dst, room, w_lo, w_hi):
             nc.gpsimd.tensor_copy(
-                out=dst[:].rearrange("p u j -> p (u j)").bitcast(U32).rearrange("p (u h) -> p u h", h=2),
-                in_=pairs.rearrange("p h u e -> p (h u e)").bitcast(U32).rearrange("p (h u) -> p u h", h=2),
+                out=dst.rearrange("p u j -> p (u j)").bitcast(U32).rearrange("p (u h) -> p u h", h=2),
+                in_=room[:, w_lo : 2 * w_hi - w_lo].rearrange("p (h u) -> p u h", h=2)[:, 0 : dst.shape[1], :],
             )
-            return dst
 
-        def way_back(banks, kts, dst, lst, s0, name, room=None):
-            n = banks[0].shape[2]
+        def way_back(banks, kts, dst, lst, s0, name, room=None, part=None):
+            u0, n = part or (0, banks[0].shape[2])
             if room is None:
                 res = tile([P, len(kts), n], F32, name)[:]
+            elif not isinstance(room, int):
+                res = room[:]
             else:
-                res = room.rearrange("p h u e -> p h (u e)").bitcast(F32)
-            nc.scalar.activation(res, banks[kts[0]][:, kts[0] : kts[-1] + 1, :], COPY)
+                res = rooms[:, room : room + len(kts) * n].bitcast(F32).rearrange("p (h u) -> p h u", u=n)
+            nc.scalar.activation(res, banks[kts[0]][:, kts[0] : kts[-1] + 1, u0 : u0 + n], COPY)
             for i, kt in enumerate(kts):
-                nc.vector.tensor_copy(out=dst[kt][:].indirect(offsets(lst, s0, n)), in_=res[:, i, :])
+                nc.vector.tensor_copy(out=dst[kt][:].indirect(offsets(lst, s0 + u0, n)), in_=res[:, i, :])
 
-        hold_bank(0)
-        ga[128] = tile([P, 128, 4], BF16, "ga128", tag="c_hi")
-        for j in range(2):
-            nc.scalar.activation(ga[128][:, :, j], da_row[j][:].indirect(offsets(list_a, 128, 128)), COPY)
-        hold_bank(1)
+        rooms = tile([P, 1792], U32, "rooms")
+        LO0, HI0, LO1, HELD, HI1 = 0, 256, 256, 512, 768
+        held0 = rooms[:, HELD : HELD + 512].bitcast(F32).rearrange("p (e t) -> p e t", e=2)
+        hold_bank(0, held0, 0)
         gather_pairs(0, 128)
         gather_pairs(256, 256)
         r0 = first_pool(0, 128, "qa0", ["r00", "r01"])
         gather_pairs(128, 128)
-        r2 = first_pool(256, 256, "qa2", ["dh11", "dh_hi0"])
+        r2 = first_pool(256, 256, "qa2", ["dh1", "dh_hi0"])
         r1 = first_pool(128, 128, "qa1", ["dh00"])
-        dc_hi = tile([P, 2, T], BF16, "dc_hi", tag="c_hi")
-        for e in range(2):
-            nc.gpsimd.tensor_tensor(out=dc_hi[:, e, :], in0=held[:, e, :], in1=a_hi[:, e, :], op=MULT)
         way_back(r0, [0], r_tok, list_a, 0, "r00")
         way_back(r0, [1], r_tok, list_a, 0, "r01")
+        held1 = tile([P, 2, 256], F32, "held1", tag="qa0_s")
+        hold_bank(1, held1, 0)
+        hold_bank(2, held1, 128)
+        for e in range(2):
+            nc.gpsimd.tensor_tensor(out=dc_hi[:, e, 0:256], in0=held0[:, e, :], in1=a_hi[:, e, 0:256], op=MULT)
+            nc.gpsimd.tensor_tensor(out=dc_hi[:, e, 256:512], in0=held1[:, e, :], in1=a_hi[:, e, 256:512], op=MULT)
         way_back(r1, [0, 1], r_tok, list_a, 128, "r1")
-        rooms = tile([P, 3, G, 2], BF16, "rooms", tag="qa0_w")
-        pairs0, pairs1 = rooms[:, 0:2], rooms[:, 1:3]
-        gather_c(pairs0, 0, [0])
+        gather_c(rooms[:, LO0 : LO0 + G], 0, 0)
         way_back(r2, [0], r_tok, list_a, 256, "r20")
+        way_back(r2, [1], r_tok, list_a, 256, "r21a", part=(0, 64))
         q0 = banks_for(G, "q0", ["dh00", "dh01"])
-        q1 = banks_for(G, "q1", ["dh10"])
-        gather_c(pairs0, 0, [1, 2, 3])
-        second_pool(weave(pairs0, "gc0"), 0, q0, "qc0")
-        gather_c(pairs1, 1, [2, 3])
-        way_back(r2, [1], r_tok, list_a, 256, "r21", rooms[:, 0:1])
-        gather_c(pairs1, 1, [0, 1])
+        q1 = banks_for(G, "q1", ["r00", "r01"])
+        gather_c(rooms[:, LO0 : LO0 + G], 1, 0)
+        for j in range(2, 4):
+            gather_c(rooms[:, HI0 : HI0 + G], j, 0)
+        gc0 = tile([P, G, 4], BF16, "gc0")
+        weave(gc0[:], rooms, LO0, HI0)
+        second_pool(gc0, 0, q0, "qc0")
+        EARLY = 160
+        LATE = G - EARLY
+        for j in range(2, 4):
+            gather_c(rooms[:, HI1 : HI1 + EARLY], j, G)
+        way_back(r2, [1], r_tok, list_a, 256, "r21b", LO0, part=(64, 192))
+        for j in range(2):
+            gather_c(rooms[:, LO1 : LO1 + EARLY], j, G)
         way_back(q0, [0], q_tok, list_c, 0, "q00")
-        second_pool(weave(pairs1, "gc1", "qc0_w"), 2, q1, "qc1")
-        way_back(q0, [1], q_tok, list_c, 0, "q01", rooms[:, 2:3])
+        way_back(q0, [1], q_tok, list_c, 0, "q01a", part=(0, 64))
+        gc1 = tile([P, G, 4], BF16, "gc1", tag="qc0_w")
+        weave(gc1[:, 0:EARLY, :], rooms, LO1, HI1)
+        late = tile([P, 2 * LATE], U32, "late", tag="qc0_s")
+        for j in range(4):
+            gather_c(late[:, (j // 2) * LATE : (j // 2 + 1) * LATE], j, G + EARLY)
+        weave(gc1[:, EARLY:G, :], late, 0, LATE)
+        second_pool(gc1, 2, q1, "qc1")
+        way_back(q0, [1], q_tok, list_c, 0, "q01b", tile([P, 1, 192], F32, "q01b", tag="qc0_s"), part=(64, 192))
         way_back(q1, [0], q_tok, list_c, 256, "q10")
         way_back(q1, [1], q_tok, list_c, 256, "q11")
 

@@ -46,7 +46,8 @@ def tile_moe_plb_none_kernel(
         w2_raw = tile([P, PASSES, 2 * H], U8, "w2_raw")
         dy_w = tile([P, PASSES, T], I32, "dy_w")
         c_row = [tile([P, T], F32, "c_row%d" % j) for j in range(2)]
-        a_row = [tile([P, T], F32, "a_row%d" % j) for j in range(2)]
+        a_row0 = [tile([P, 256], F32, "a_row0%d" % th) for th in range(2)]
+        a_row1 = tile([P, T], F32, "a_row1")
         c_buf = tile([P, 2 * T + 128], F32, "c_buf")
         c_hi = c_buf[:, 0 : 2 * T].rearrange("p (e t) -> p e t", e=2)
         a_hi = tile([P, 2, T], F32, "a_hi")
@@ -77,10 +78,11 @@ def tile_moe_plb_none_kernel(
         load_scale_row(nc.sync, dy_sc, dy_rows, 3)
         nc.sync.dma_start(out=c_row[0][:], in_=c_view[:, 0, :])
         nc.sync.dma_start(list_a[:], offs)
+        nc.sync.dma_start(out=a_row0[1][:], in_=a_view[:, 0, 256:512])
         nc.sync.dma_start(out=c_row[1][:], in_=c_view[:, 1, :])
-        nc.sync.dma_start(out=a_row[1][:], in_=a_view[:, 1, :])
+        nc.sync.dma_start(out=a_row1[:], in_=a_view[:, 1, :])
         nc.sync.dma_start(out=c_hi, in_=c_view[:, 2:4, :])
-        nc.sync.dma_start(out=a_row[0][:], in_=a_view[:, 0, :])
+        nc.sync.dma_start(out=a_row0[0][:], in_=a_view[:, 0, 0:256])
         nc.sync.dma_start(out=wa_w[:].bitcast(I32), in_=wat_words.rearrange("e s p b -> p (e s) b").bitcast(I32))
 
         w2_p = [tile([P, PASSES, 2, 2 * P], U8, "w2_p%d" % h) for h in range(2)]
@@ -122,22 +124,23 @@ def tile_moe_plb_none_kernel(
         ga = {0: halves[0][:, 0:128, :], 128: halves[0][:, 128:256, :], 256: halves[1]}
         dc_hi = first[:, 512:1536].rearrange("p (e t) -> p e t", e=2)
 
-        held_row = [first[:, 1022:1534].bitcast(F32), tile([P, 256], F32, "held_row1")[:]]
+        held_row = first[:, 1022:1534].bitcast(F32)
         for th in range(2):
             cols = slice(th * 256, (th + 1) * 256)
             bank = ps.tile([P, 256], F32, name="dh0%d" % th, tag="dh0%d" % th)
             for tq in range(2):
                 first_product(bank[:, tq * 128 : (tq + 1) * 128], 0, 0, th * 256 + tq * 128, 128)
             nc.vector.tensor_tensor(out=da_row[0][:, cols], in0=bank[:], in1=c_row[0][:, cols], op=MULT)
-            nc.scalar.activation(held_row[th], bank[:], COPY)
-            if th == 1:
-                nc.gpsimd.tensor_tensor(out=dc_row[0][:, cols], in0=held_row[th], in1=a_row[0][:, cols], op=MULT)
+            if th == 0:
+                nc.scalar.activation(held_row, bank[:], COPY)
+            else:
+                nc.vector.tensor_tensor(out=dc_row[0][:, cols], in0=bank[:], in1=a_row0[1][:], op=MULT)
         for g in range(2):
             nc.scalar.activation(halves[g][:, :, 0], da_row[0][:].indirect(offsets(list_a, g * G, G)), COPY)
         bank = ps.tile([P, T], F32, name="dh1", tag="dh1")
         first_product(bank[:], 0, 1, 0, T)
         nc.vector.tensor_tensor(out=da_row[1][:], in0=bank[:], in1=c_row[1][:], op=MULT)
-        nc.vector.tensor_tensor(out=dc_row[1], in0=bank[:], in1=a_row[1][:], op=MULT)
+        nc.vector.tensor_tensor(out=dc_row[1], in0=bank[:], in1=a_row1[:], op=MULT)
         for g in range(2):
             nc.scalar.activation(halves[g][:, :, 1], da_row[1][:].indirect(offsets(list_a, g * G, G)), COPY)
         spans = [(0, 256), (256, 128), (384, 128)]
@@ -155,7 +158,7 @@ def tile_moe_plb_none_kernel(
                 op=MULT,
             )
 
-        nc.gpsimd.tensor_tensor(out=dc_row[0][:, 0:256], in0=held_row[0], in1=a_row[0][:, 0:256], op=MULT)
+        nc.gpsimd.tensor_tensor(out=dc_row[0][:, 0:256], in0=held_row, in1=a_row0[0][:], op=MULT)
         wb_sc = dy_sc[:].rearrange("p s (f k) -> p (s f) k", k=K)
         load_scale_rows([nc.sync] * 4, wb_sc, wbt_scales.rearrange("f s (q r) k -> r q (f s) k", r=4))
 
@@ -235,9 +238,8 @@ def tile_moe_plb_none_kernel(
             for i, kt in enumerate(kts):
                 nc.vector.tensor_copy(out=dst[kt][:].indirect(offsets(lst, s0 + u0, n)), in_=res[:, i, :])
 
-        rooms = tile([P, 1792], U32, "rooms")
         LO0, HI0, LO1, HELD, HI1 = 0, 256, 256, 512, 768
-        held0 = rooms[:, HELD : HELD + 512].bitcast(F32).rearrange("p (e t) -> p e t", e=2)
+        held0 = tile([P, 2, 256], F32, "held0")
         hold_bank(0, held0, 0)
         gather_pairs(0, 128)
         gather_pairs(256, 256)
@@ -247,33 +249,33 @@ def tile_moe_plb_none_kernel(
         r1 = first_pool(128, 128, "qa1", ["dh00"])
         way_back(r0, [0], r_tok, list_a, 0, "r00")
         way_back(r0, [1], r_tok, list_a, 0, "r01")
-        held1 = tile([P, 2, 256], F32, "held1", tag="qa0_s")
+        rooms = tile([P, 1280], U32, "rooms", tag="qa0_s")
+        held1 = rooms[:, HELD : HELD + 512].bitcast(F32).rearrange("p (e t) -> p e t", e=2)
         hold_bank(1, held1, 0)
         hold_bank(2, held1, 128)
+        nc.gpsimd.tensor_tensor(out=dc_hi[:, :, 0:256], in0=held0[:], in1=a_hi[:, :, 0:256], op=MULT)
         for e in range(2):
-            nc.gpsimd.tensor_tensor(out=dc_hi[:, e, 0:256], in0=held0[:, e, :], in1=a_hi[:, e, 0:256], op=MULT)
             nc.gpsimd.tensor_tensor(out=dc_hi[:, e, 256:512], in0=held1[:, e, :], in1=a_hi[:, e, 256:512], op=MULT)
         way_back(r1, [0, 1], r_tok, list_a, 128, "r1")
         gather_c(rooms[:, LO0 : LO0 + G], 0, 0)
         way_back(r2, [0], r_tok, list_a, 256, "r20")
-        way_back(r2, [1], r_tok, list_a, 256, "r21a", part=(0, 64))
         q0 = banks_for(G, "q0", ["dh00", "dh01"])
         q1 = banks_for(G, "q1", ["r00", "r01"])
         gather_c(rooms[:, LO0 : LO0 + G], 1, 0)
-        for j in range(2, 4):
-            gather_c(rooms[:, HI0 : HI0 + G], j, 0)
+        gather_c(rooms[:, HI0 : HI0 + G], 2, 0)
         gc0 = tile([P, G, 4], BF16, "gc0")
-        weave(gc0[:], rooms, LO0, HI0)
+        for u0 in range(0, G, C2):
+            gather_c(rooms[:, HI0 + u0 : HI0 + u0 + C2], 3, u0)
+            weave(gc0[:, u0 : u0 + C2, :], rooms, LO0 + u0, HI0 + u0)
         second_pool(gc0, 0, q0, "qc0")
         EARLY = 160
         LATE = G - EARLY
         for j in range(2, 4):
             gather_c(rooms[:, HI1 : HI1 + EARLY], j, G)
-        way_back(r2, [1], r_tok, list_a, 256, "r21b", LO0, part=(64, 192))
+        way_back(r2, [1], r_tok, list_a, 256, "r21", LO0)
         for j in range(2):
             gather_c(rooms[:, LO1 : LO1 + EARLY], j, G)
         way_back(q0, [0], q_tok, list_c, 0, "q00")
-        way_back(q0, [1], q_tok, list_c, 0, "q01a", part=(0, 64))
         gc1 = tile([P, G, 4], BF16, "gc1", tag="qc0_w")
         weave(gc1[:, 0:EARLY, :], rooms, LO1, HI1)
         late = tile([P, 2 * LATE], U32, "late", tag="qc0_s")
@@ -281,7 +283,7 @@ def tile_moe_plb_none_kernel(
             gather_c(late[:, (j // 2) * LATE : (j // 2 + 1) * LATE], j, G + EARLY)
         weave(gc1[:, EARLY:G, :], late, 0, LATE)
         second_pool(gc1, 2, q1, "qc1")
-        way_back(q0, [1], q_tok, list_c, 0, "q01b", tile([P, 1, 192], F32, "q01b", tag="qc0_s"), part=(64, 192))
+        way_back(q0, [1], q_tok, list_c, 0, "q01", tile([P, 1, G], F32, "q01", tag="qc0_s"))
         way_back(q1, [0], q_tok, list_c, 256, "q10")
         way_back(q1, [1], q_tok, list_c, 256, "q11")
 

@@ -65,12 +65,9 @@ def tile_moe_plb_none_kernel(
             queue.dma_start(out=plane[r:P:32, :, :].bitcast(I32), in_=rows[r].bitcast(I32))
 
         w2_rows = w2t_scales.rearrange("s (q r) i -> r q s i", r=4)
-        warm = tile([P, 16], F32, "warm")
-        nc.vector.memset(warm[:, 0:8], 0.0)
 
         nc.sync.dma_start(out=w2_raw[:].bitcast(I32), in_=w2t_words.rearrange("s p b -> p s b").bitcast(I32))
         load_scale_rows([nc.scalar, nc.scalar, nc.sync, nc.sync], w2_sc_raw, w2_rows)
-        nc.scalar.activation(warm[:, 8:16], warm[:, 0:8], COPY)
         load_scale_row(nc.sync, dy_sc, dy_rows, 0)
         load_scale_row(nc.sync, dy_sc, dy_rows, 1)
         nc.sync.dma_start(out=dy_w[:], in_=dy_words.rearrange("s p t d -> p s (t d)").bitcast(I32))

@@ -23,11 +23,6 @@ PASSES = N // 512
 G = 256
 
 
-def load_scale_rows(queues, plane, rows):
-    for r in range(4):
-        queues[r].dma_start(out=plane[r:P:32, :, :].bitcast(I32), in_=rows[r].bitcast(I32))
-
-
 def tile_moe_plb_none_kernel(
     tc, dy_words, dy_scales, w2t_words, w2t_scales, wat_words, wat_scales, wbt_words, wbt_scales, a, c, offs, offs2, out
 ):
@@ -39,6 +34,15 @@ def tile_moe_plb_none_kernel(
         def tile(shape, dtype, name, tag=None):
             return sb.tile(shape, dtype, name=name, tag=tag or name, align_bytes=64)
 
+        def bank(shape, name, tag=None):
+            return ps.tile(shape, F32, name=name, tag=tag or name)
+
+        def load_scale_row(queue, plane, rows, r):
+            queue.dma_start(out=plane[r:P:32, :, :].bitcast(I32), in_=rows[r].bitcast(I32))
+
+        def offsets(lst, s0, n):
+            return lst[:, s0 // 16 : (s0 + n) // 16]
+
         list_a = tile([P, T // 16], U16, "list_a")
         list_c = tile([P, T // 16], U16, "list_c")
         w2_sc_raw = tile([P, PASSES, H], U8, "w2_sc_raw")
@@ -46,10 +50,8 @@ def tile_moe_plb_none_kernel(
         w2_raw = tile([P, PASSES, 2 * H], U8, "w2_raw")
         dy_w = tile([P, PASSES, T], I32, "dy_w")
         c_row = [tile([P, T], F32, "c_row%d" % j) for j in range(2)]
-        a_row0 = [tile([P, 256], F32, "a_row0%d" % th) for th in range(2)]
-        a_row1 = tile([P, T], F32, "a_row1")
-        c_buf = tile([P, 2 * T + 128], F32, "c_buf")
-        c_hi = c_buf[:, 0 : 2 * T].rearrange("p (e t) -> p e t", e=2)
+        c_hi = tile([P, 2, T], F32, "c_hi")
+        a_lo = tile([P, 2, T], F32, "a_lo")
         a_hi = tile([P, 2, T], F32, "a_hi")
         wa_w = tile([P, E1, 2 * K], U8, "wa_w")
         wb_w = tile([P, E2, K], I32, "wb_w")
@@ -60,14 +62,11 @@ def tile_moe_plb_none_kernel(
         c_view = c.rearrange("(p j) t -> p j t", j=4)
         a_view = a.rearrange("(p j) t -> p j t", j=4)
         dy_rows = dy_scales.rearrange("s (q r) t -> r q s t", r=4)
-
-        def load_scale_row(queue, plane, rows, r):
-            queue.dma_start(out=plane[r:P:32, :, :].bitcast(I32), in_=rows[r].bitcast(I32))
-
         w2_rows = w2t_scales.rearrange("s (q r) i -> r q s i", r=4)
 
         nc.sync.dma_start(out=w2_raw[:].bitcast(I32), in_=w2t_words.rearrange("s p b -> p s b").bitcast(I32))
-        load_scale_rows([nc.scalar, nc.scalar, nc.sync, nc.sync], w2_sc_raw, w2_rows)
+        for r, queue in enumerate([nc.scalar, nc.scalar, nc.sync, nc.sync]):
+            load_scale_row(queue, w2_sc_raw, w2_rows, r)
         load_scale_row(nc.sync, dy_sc, dy_rows, 0)
         load_scale_row(nc.sync, dy_sc, dy_rows, 1)
         nc.sync.dma_start(out=dy_w[:], in_=dy_words.rearrange("s p t d -> p s (t d)").bitcast(I32))
@@ -75,11 +74,10 @@ def tile_moe_plb_none_kernel(
         load_scale_row(nc.sync, dy_sc, dy_rows, 3)
         nc.sync.dma_start(out=c_row[0][:], in_=c_view[:, 0, :])
         nc.sync.dma_start(list_a[:], offs)
-        nc.sync.dma_start(out=a_row0[1][:], in_=a_view[:, 0, 256:512])
         nc.sync.dma_start(out=c_row[1][:], in_=c_view[:, 1, :])
-        nc.sync.dma_start(out=a_row1[:], in_=a_view[:, 1, :])
-        nc.sync.dma_start(out=c_hi, in_=c_view[:, 2:4, :])
-        nc.sync.dma_start(out=a_row0[0][:], in_=a_view[:, 0, 0:256])
+        nc.sync.dma_start(out=c_hi[:], in_=c_view[:, 2:4, :])
+        nc.sync.dma_start(list_c[:], offs2)
+        nc.sync.dma_start(out=a_hi[:], in_=a_view[:, 2:4, :])
         nc.sync.dma_start(out=wa_w[:].bitcast(I32), in_=wat_words.rearrange("e s p b -> p (e s) b").bitcast(I32))
 
         w2_p = [tile([P, PASSES, 2, 2 * P], U8, "w2_p%d" % h) for h in range(2)]
@@ -94,77 +92,32 @@ def tile_moe_plb_none_kernel(
         wa_rows = wat_scales.rearrange("e s (q r) k -> r q (e s) k", r=4)
         for r in range(4):
             load_scale_row(nc.sync, wa_sc, wa_rows, r)
-        nc.sync.dma_start(out=a_hi[:], in_=a_view[:, 2:4, :])
-        nc.sync.dma_start(list_c[:], offs2)
+        nc.sync.dma_start(out=a_lo[:], in_=a_view[:, 0:2, :])
         nc.sync.dma_start(out=wb_w[:], in_=wbt_words.rearrange("f s p k d -> p (f s) (k d)").bitcast(I32))
 
-        def first_product(dst, h, e, t0, n):
+        def first_product(dst, j, t0, n):
             for s in range(PASSES):
                 nc.tensor.matmul_mx(
                     out=dst,
-                    lhsT=w2_p[h][:, s, e, :].bitcast(FP4X4),
-                    lhsT_scale=w2_sc[h][:, s, e, :],
+                    lhsT=w2_p[j // 2][:, s, j % 2, :].bitcast(FP4X4),
+                    lhsT_scale=w2_sc[j // 2][:, s, j % 2, :],
                     rhs=dy_w[:, s, t0 : t0 + n].bitcast(FP8X4),
                     rhs_scale=dy_sc[:, s, t0 : t0 + n],
                     start=(s == 0),
                     stop=(s == PASSES - 1),
                 )
 
-        def offsets(lst, s0, n):
-            return lst[:, s0 // 16 : (s0 + n) // 16]
-
-        da_row = [tile([P, T], BF16, "da_row%d" % j) for j in range(2)]
-        da_hi = tile([P, 2 * T], BF16, "da_hi")
-        dc_row = [c_buf[:, 2 * T - 128 : 2 * T + 128].bitcast(BF16), tile([P, T], BF16, "dc_row1")[:]]
-        first = tile([P, 1536], BF16, "first")
-        halves = [first[:, 0:1024].rearrange("p (u j) -> p u j", j=4), tile([P, 256, 4], BF16, "second")[:]]
-        ga = {0: halves[0][:, 0:128, :], 128: halves[0][:, 128:256, :], 256: halves[1]}
-        dc_hi = first[:, 512:1536].rearrange("p (e t) -> p e t", e=2)
-
-        held_row = first[:, 1022:1534].bitcast(F32)
-        for th in range(2):
-            cols = slice(th * 256, (th + 1) * 256)
-            bank = ps.tile([P, 256], F32, name="dh0%d" % th, tag="dh0%d" % th)
-            for tq in range(2):
-                first_product(bank[:, tq * 128 : (tq + 1) * 128], 0, 0, th * 256 + tq * 128, 128)
-            nc.vector.tensor_tensor(out=da_row[0][:, cols], in0=bank[:], in1=c_row[0][:, cols], op=MULT)
-            if th == 0:
-                nc.scalar.activation(held_row, bank[:], COPY)
-            else:
-                nc.vector.tensor_tensor(out=dc_row[0][:, cols], in0=bank[:], in1=a_row0[1][:], op=MULT)
-        for g in range(2):
-            nc.scalar.activation(halves[g][:, :, 0], da_row[0][:].indirect(offsets(list_a, g * G, G)), COPY)
-        bank = ps.tile([P, T], F32, name="dh1", tag="dh1")
-        first_product(bank[:], 0, 1, 0, T)
-        nc.vector.tensor_tensor(out=da_row[1][:], in0=bank[:], in1=c_row[1][:], op=MULT)
-        nc.vector.tensor_tensor(out=dc_row[1], in0=bank[:], in1=a_row1[:], op=MULT)
-        for g in range(2):
-            nc.scalar.activation(halves[g][:, :, 1], da_row[1][:].indirect(offsets(list_a, g * G, G)), COPY)
-        spans = [(0, 256), (256, 128), (384, 128)]
-        dh_hi = []
-        for b, (t0, n) in enumerate(spans):
-            bank = ps.tile([P, 2, n], F32, name="dh_hi%d" % b, tag="dh_hi%d" % b)
-            dh_hi.append(bank)
-            for tq in range(n // 128):
-                for e in range(2):
-                    first_product(bank[:, e, tq * 128 : (tq + 1) * 128], 1, e, t0 + tq * 128, 128)
+        def product_pairs(pairs, dh, saved, t0, n):
             nc.vector.tensor_tensor(
-                out=da_hi[:, 2 * t0 : 2 * (t0 + n)].rearrange("p (u i e) -> p u e i", i=4, e=2),
-                in0=bank[:].rearrange("p e (u i) -> p u e i", i=4),
-                in1=c_hi[:, :, t0 : t0 + n].rearrange("p e (u i) -> p u e i", i=4),
+                out=pairs[:, 2 * t0 : 2 * (t0 + n)].rearrange("p (u i e) -> p u e i", i=4, e=2),
+                in0=dh[:].rearrange("p e (u i) -> p u e i", i=4),
+                in1=saved[:, :, t0 : t0 + n].rearrange("p e (u i) -> p u e i", i=4),
                 op=MULT,
             )
 
-        nc.gpsimd.tensor_tensor(out=dc_row[0][:, 0:256], in0=held_row, in1=a_row0[0][:], op=MULT)
-        wb_sc = dy_sc[:].rearrange("p s (f k) -> p (s f) k", k=K)
-        load_scale_rows([nc.sync] * 4, wb_sc, wbt_scales.rearrange("f s (q r) k -> r q (f s) k", r=4))
-
-        r_tok = [tile([P, T], F32, "r_tok%d" % kt) for kt in range(2)]
-        q_tok = [tile([P, T], F32, "q_tok%d" % kt) for kt in range(2)]
-
-        def gather_pairs(s0, n):
-            words = ga[s0].rearrange("p u j -> p (u j)").bitcast(U32).rearrange("p (u h) -> p u h", h=2)
-            nc.vector.tensor_copy(out=words[:, :, 1], in_=da_hi[:].bitcast(U32).indirect(offsets(list_a, s0, n)))
+        def gather_pairs(dst, h, pairs, lst, s0):
+            words = dst.rearrange("p u j -> p (u j)").bitcast(U32).rearrange("p (u h) -> p u h", h=2)
+            nc.vector.tensor_copy(out=words[:, :, h], in_=pairs.bitcast(U32).indirect(offsets(lst, s0, dst.shape[1])))
 
         def quantise(src, name):
             slots = src.shape[1]
@@ -173,123 +126,146 @@ def tile_moe_plb_none_kernel(
             nc.vector.quantize_mx(out=codes[:].bitcast(FP8X4), scales=scales[:], in_=src.rearrange("p u j -> p (u j)"))
             return codes, scales
 
-        def hold_bank(b, held, col0):
-            n = spans[b][1]
-            nc.scalar.activation(held[:, :, col0 : col0 + n], dh_hi[b][:], COPY)
+        da_row = [tile([P, T], BF16, "da_row%d" % j) for j in range(2)]
+        da_hi = tile([P, 2 * T], BF16, "da_hi")
+        dc_hi = c_hi[:, 0, :].bitcast(BF16)
+        dh_lo = tile([P, 2, T], F32, "dh_lo")
+        ga = [tile([P, G, 4], BF16, "ga%d" % g) for g in range(2)]
+        gc = [tile([P, G, 4], BF16, "gc%d" % g) for g in range(2)]
 
-        def banks_for(n, name, tags):
-            tiles = [ps.tile([P, 2, n], F32, name="bank_%s_%s" % (name, tag), tag=tag) for tag in tags]
-            return [tiles[kt % len(tiles)] for kt in range(2)]
+        for j, widths in enumerate([(256, 256), (512,)]):
+            t0 = 0
+            for b, n in enumerate(widths):
+                dh = bank([P, n], "dh%d%d" % (j, b))
+                first_product(dh[:], j, t0, n)
+                nc.vector.tensor_tensor(out=da_row[j][:, t0 : t0 + n], in0=dh[:], in1=c_row[j][:, t0 : t0 + n], op=MULT)
+                if j == 0:
+                    nc.scalar.activation(dh_lo[:, j, t0 : t0 + n], dh[:], COPY)
+                t0 += n
+            for g in range(2):
+                nc.scalar.activation(ga[g][:, :, j], da_row[j][:].indirect(offsets(list_a, g * G, G)), COPY)
+        nc.scalar.activation(dh_lo[:, 1, :], dh[:], COPY)
+        spans = [(0, 256), (256, 128), (384, 128)]
+        dh_hi = []
+        for b, (t0, n) in enumerate(spans):
+            dh = bank([P, 2, n], "dh_hi%d" % b)
+            dh_hi.append(dh)
+            for e in range(2):
+                first_product(dh[:, e, :], 2 + e, t0, n)
+            product_pairs(da_hi, dh, c_hi, t0, n)
 
-        def first_pool(s0, n, name, tags):
-            codes, scales = quantise(ga[s0], name)
-            banks = banks_for(n, name, tags)
-            for kt in range(2):
+        wb_sc = dy_sc[:].rearrange("p s (f k) -> p (s f) k", k=K)
+        wb_rows = wbt_scales.rearrange("f s (q r) k -> r q (f s) k", r=4)
+        for r in range(4):
+            load_scale_row(nc.sync, wb_sc, wb_rows, r)
+
+        r_tok = [tile([P, T], F32, "r_tok%d" % kt) for kt in range(2)]
+        q_tok = [tile([P, T], F32, "q_tok%d" % kt) for kt in range(2)]
+
+        def expert_a(dst, quantised, s0, kt):
+            codes, scales = quantised
+            nc.tensor.matmul_mx(
+                out=dst,
+                lhsT=wa_w[:, s0 // C1, kt * 256 : (kt + 1) * 256].bitcast(FP4X4),
+                lhsT_scale=wa_sc[:, s0 // C1, kt * 128 : (kt + 1) * 128],
+                rhs=codes[:].bitcast(FP8X4),
+                rhs_scale=scales[:],
+                start=True,
+                stop=True,
+            )
+
+        def experts_b(dst, quantised, g, kt):
+            codes, scales = quantised
+            for fl in range(2):
+                cols = slice(fl * C2, (fl + 1) * C2)
                 nc.tensor.matmul_mx(
-                    out=banks[kt][:, kt, :],
-                    lhsT=wa_w[:, s0 // G, kt * 256 : (kt + 1) * 256].bitcast(FP4X4),
-                    lhsT_scale=wa_sc[:, s0 // G, kt * 128 : (kt + 1) * 128],
-                    rhs=codes[:].bitcast(FP8X4),
-                    rhs_scale=scales[:],
+                    out=dst[:, cols],
+                    lhsT=wb_w[:, 2 * g + fl, kt * 128 : (kt + 1) * 128].bitcast(FP8X4),
+                    lhsT_scale=wb_sc[:, 2 * g + fl, kt * 128 : (kt + 1) * 128],
+                    rhs=codes[:, cols].bitcast(FP8X4),
+                    rhs_scale=scales[:, cols],
                     start=True,
                     stop=True,
                 )
-            return banks
 
-        def second_pool(src, f0, banks, name):
-            codes, scales = quantise(src[:], name)
+        def leave_scalar(src, name):
+            res = tile(list(src.shape), F32, name)
+            nc.scalar.activation(res[:], src, COPY)
+            return res
+
+        def leave_vector(src, name):
+            res = tile(list(src.shape), F32, name)
+            nc.vector.tensor_copy(out=res[:], in_=src)
+            return res
+
+        def scatter_scalar(window, lst, s0, src):
+            nc.scalar.activation(window[:].indirect(offsets(lst, s0, src.shape[1])), src, COPY)
+
+        def scatter_vector(window, lst, s0, src):
+            nc.vector.tensor_copy(out=window[:].indirect(offsets(lst, s0, src.shape[1])), in_=src)
+
+        def dc_high(b):
+            product_pairs(dc_hi, dh_hi[b], a_hi, *spans[b])
+
+        dc_high(1)
+        gather_pairs(ga[0][:, 0:128, :], 1, da_hi[:], list_a, 0)
+        dc_high(2)
+        qa0 = quantise(ga[0][:, 0:128, :], "qa0")
+        gather_pairs(ga[0][:, 128:256, :], 1, da_hi[:], list_a, 128)
+        gather_pairs(ga[1][:], 1, da_hi[:], list_a, 256)
+        qa1 = quantise(ga[0][:, 128:256, :], "qa1")
+        qa2 = quantise(ga[1][:], "qa2")
+        dc_high(0)
+        for kt in range(2):
+            ru = bank([P, 128], "r0%d" % kt, "dh0%d" % kt)
+            expert_a(ru[:], qa0, 0, kt)
+            res = leave_scalar(ru[:], "r0%d" % kt)
+            scatter_scalar(r_tok[kt], list_a, 0, res[:])
+        ru = bank([P, 2, 128], "r1")
+        for kt in range(2):
+            expert_a(ru[:, kt, :], qa1, 128, kt)
+        res = leave_scalar(ru[:], "r1")
+        scatter_scalar(r_tok[0], list_a, 128, res[:, 0, :])
+        r11 = res[:, 1, :]
+        r20 = bank([P, G], "r20")
+        expert_a(r20[:], qa2, 256, 0)
+        res = leave_scalar(r20[:], "r20")
+        scatter_scalar(r_tok[0], list_a, 256, res[:])
+
+        dc_lo = tile([P, 2 * T], BF16, "dc_lo", "ga1")
+        nc.gpsimd.tensor_tensor(
+            out=dc_lo[:].rearrange("p (u i e) -> p u e i", i=4, e=2),
+            in0=dh_lo[:].rearrange("p e (u i) -> p u e i", i=4),
+            in1=a_lo[:].rearrange("p e (u i) -> p u e i", i=4),
+            op=MULT,
+        )
+        gather_pairs(gc[0][:], 1, dc_hi, list_c, 0)
+        gather_pairs(gc[1][:], 1, dc_hi, list_c, G)
+        scatter_vector(r_tok[1], list_a, 128, r11)
+        gather_pairs(gc[0][:], 0, dc_lo[:], list_c, 0)
+        gather_pairs(gc[1][:], 0, dc_lo[:], list_c, G)
+        qc = [quantise(gc[g][:], "qc%d" % g) for g in range(2)]
+        tags = [["dh10", "dh_hi0"], ["dh_hi1", "dh_hi2"]]
+        SHARE = 128
+        for g in range(2):
+            qb = [bank([P, G], "q%d%d" % (g, kt), tags[g][kt]) for kt in range(2)]
             for kt in range(2):
-                for fl in range(src.shape[1] // C2):
-                    f = f0 + fl
-                    cols = slice(fl * C2, (fl + 1) * C2)
-                    nc.tensor.matmul_mx(
-                        out=banks[kt][:, kt, (f % 2) * C2 : (f % 2 + 1) * C2],
-                        lhsT=wb_w[:, f, kt * 128 : (kt + 1) * 128].bitcast(FP8X4),
-                        lhsT_scale=wb_sc[:, f, kt * 128 : (kt + 1) * 128],
-                        rhs=codes[:, cols].bitcast(FP8X4),
-                        rhs_scale=scales[:, cols],
-                        start=True,
-                        stop=True,
-                    )
-
-        def gather_c(plane, j, s0):
-            window = dc_row[j] if j < 2 else dc_hi[:, j - 2, :]
-            pairs = plane.bitcast(BF16).rearrange("p (u e) -> p u e", e=2)
-            nc.scalar.activation(pairs[:, :, j % 2], window.indirect(offsets(list_c, s0, plane.shape[1])), COPY)
-
-        def weave(dst, room, w_lo, w_hi):
-            nc.gpsimd.tensor_copy(
-                out=dst.rearrange("p u j -> p (u j)").bitcast(U32).rearrange("p (u h) -> p u h", h=2),
-                in_=room[:, w_lo : 2 * w_hi - w_lo].rearrange("p (h u) -> p u h", h=2)[:, 0 : dst.shape[1], :],
-            )
-
-        def way_back(banks, kts, dst, lst, s0, name, room=None, part=None):
-            u0, n = part or (0, banks[0].shape[2])
-            if room is None:
-                res = tile([P, len(kts), n], F32, name)[:]
-            elif not isinstance(room, int):
-                res = room[:]
-            else:
-                res = rooms[:, room : room + len(kts) * n].bitcast(F32).rearrange("p (h u) -> p h u", u=n)
-            nc.scalar.activation(res, banks[kts[0]][:, kts[0] : kts[-1] + 1, u0 : u0 + n], COPY)
-            for i, kt in enumerate(kts):
-                nc.vector.tensor_copy(out=dst[kt][:].indirect(offsets(lst, s0 + u0, n)), in_=res[:, i, :])
-
-        LO0, HI0, LO1, HELD, HI1 = 0, 256, 256, 512, 768
-        held0 = tile([P, 2, 256], F32, "held0")
-        hold_bank(0, held0, 0)
-        gather_pairs(0, 128)
-        gather_pairs(256, 256)
-        r0 = first_pool(0, 128, "qa0", ["r00", "r01"])
-        gather_pairs(128, 128)
-        r2 = first_pool(256, 256, "qa2", ["dh1", "dh_hi0"])
-        r1 = first_pool(128, 128, "qa1", ["dh00"])
-        way_back(r0, [0], r_tok, list_a, 0, "r00")
-        way_back(r0, [1], r_tok, list_a, 0, "r01")
-        rooms = tile([P, 1280], U32, "rooms", tag="qa0_s")
-        held1 = rooms[:, HELD : HELD + 512].bitcast(F32).rearrange("p (e t) -> p e t", e=2)
-        hold_bank(1, held1, 0)
-        hold_bank(2, held1, 128)
-        nc.gpsimd.tensor_tensor(out=dc_hi[:, :, 0:256], in0=held0[:], in1=a_hi[:, :, 0:256], op=MULT)
-        for e in range(2):
-            nc.gpsimd.tensor_tensor(out=dc_hi[:, e, 256:512], in0=held1[:, e, :], in1=a_hi[:, e, 256:512], op=MULT)
-        way_back(r1, [0, 1], r_tok, list_a, 128, "r1")
-        gather_c(rooms[:, LO0 : LO0 + G], 0, 0)
-        way_back(r2, [0], r_tok, list_a, 256, "r20")
-        q0 = banks_for(G, "q0", ["dh00", "dh01"])
-        q1 = banks_for(G, "q1", ["r00", "r01"])
-        gather_c(rooms[:, LO0 : LO0 + G], 1, 0)
-        gather_c(rooms[:, HI0 : HI0 + G], 2, 0)
-        gc0 = tile([P, G, 4], BF16, "gc0")
-        for u0 in range(0, G, C2):
-            gather_c(rooms[:, HI0 + u0 : HI0 + u0 + C2], 3, u0)
-            weave(gc0[:, u0 : u0 + C2, :], rooms, LO0 + u0, HI0 + u0)
-        second_pool(gc0, 0, q0, "qc0")
-        EARLY = 160
-        LATE = G - EARLY
-        for j in range(2, 4):
-            gather_c(rooms[:, HI1 : HI1 + EARLY], j, G)
-        way_back(r2, [1], r_tok, list_a, 256, "r21", LO0)
-        for j in range(2):
-            gather_c(rooms[:, LO1 : LO1 + EARLY], j, G)
-        way_back(q0, [0], q_tok, list_c, 0, "q00")
-        gc1 = tile([P, G, 4], BF16, "gc1", tag="qc0_w")
-        weave(gc1[:, 0:EARLY, :], rooms, LO1, HI1)
-        late = tile([P, 2 * LATE], U32, "late", tag="qc0_s")
-        for j in range(4):
-            gather_c(late[:, (j // 2) * LATE : (j // 2 + 1) * LATE], j, G + EARLY)
-        weave(gc1[:, EARLY:G, :], late, 0, LATE)
-        second_pool(gc1, 2, q1, "qc1")
-        way_back(q0, [1], q_tok, list_c, 0, "q01", tile([P, 1, G], F32, "q01", tag="qc0_s"))
-        way_back(q1, [0], q_tok, list_c, 256, "q10")
-        way_back(q1, [1], q_tok, list_c, 256, "q11")
+                experts_b(qb[kt], qc[g], g, kt)
+            res = leave_vector(qb[0][:], "q%d0" % g)
+            scatter_vector(q_tok[0], list_c, g * G, res[:])
+            res = leave_scalar(qb[1][:], "q%d1" % g)
+            scatter_scalar(q_tok[1], list_c, g * G, res[:, 0 : G if g == 0 else SHARE])
+        scatter_vector(q_tok[1], list_c, G + SHARE, res[:, SHARE:G])
+        r21 = bank([P, G], "r21", "dh_hi0")
+        expert_a(r21[:], qa2, 256, 1)
+        res = leave_scalar(r21[:], "r21")
+        scatter_scalar(r_tok[1], list_a, 256, res[:])
 
         res0 = tile([P, T], F32, "res0")
         nc.gpsimd.tensor_tensor(out=res0[:], in0=r_tok[0][:], in1=q_tok[0][:], op=ADD)
-        nc.scalar.dma_start(out=out[0:P, :], in_=res0[:])
-
-        for part in range(2):
+        nc.sync.dma_start(out=out[0:P, :], in_=res0[:])
+        for part, queue in enumerate([nc.scalar, nc.sync]):
             cols = slice(part * T // 2, (part + 1) * T // 2)
             res = tile([P, T // 2], F32, "res1%d" % part)
             nc.vector.tensor_tensor(out=res[:], in0=r_tok[1][:, cols], in1=q_tok[1][:, cols], op=ADD)
-            nc.sync.dma_start(out=out[P : 2 * P, cols], in_=res[:])
+            queue.dma_start(out=out[P : 2 * P, cols], in_=res[:])

@@ -21,6 +21,7 @@ COPY = mybir.ActivationFunctionType.Copy
 P = 128
 PASSES = N // 512
 G = 256
+SHARE = 192
 
 
 def tile_moe_plb_none_kernel(
@@ -51,7 +52,7 @@ def tile_moe_plb_none_kernel(
         dy_w = tile([P, PASSES, T], I32, "dy_w")
         c_row = [tile([P, T], F32, "c_row%d" % j) for j in range(2)]
         c_hi = tile([P, 2, T], F32, "c_hi")
-        a_lo = tile([P, 2, T], F32, "a_lo")
+        a_row = [tile([P, T], F32, "a_row%d" % j) for j in range(2)]
         a_hi = tile([P, 2, T], F32, "a_hi")
         wa_w = tile([P, E1, 2 * K], U8, "wa_w")
         wb_w = tile([P, E2, K], I32, "wb_w")
@@ -76,8 +77,10 @@ def tile_moe_plb_none_kernel(
         nc.sync.dma_start(list_a[:], offs)
         nc.sync.dma_start(out=c_row[1][:], in_=c_view[:, 1, :])
         nc.sync.dma_start(out=c_hi[:], in_=c_view[:, 2:4, :])
-        nc.sync.dma_start(list_c[:], offs2)
+        nc.sync.dma_start(out=a_row[0][:], in_=a_view[:, 0, :])
         nc.sync.dma_start(out=a_hi[:], in_=a_view[:, 2:4, :])
+        nc.sync.dma_start(out=a_row[1][:], in_=a_view[:, 1, :])
+        nc.sync.dma_start(list_c[:], offs2)
         nc.sync.dma_start(out=wa_w[:].bitcast(I32), in_=wat_words.rearrange("e s p b -> p (e s) b").bitcast(I32))
 
         w2_p = [tile([P, PASSES, 2, 2 * P], U8, "w2_p%d" % h) for h in range(2)]
@@ -92,7 +95,6 @@ def tile_moe_plb_none_kernel(
         wa_rows = wat_scales.rearrange("e s (q r) k -> r q (e s) k", r=4)
         for r in range(4):
             load_scale_row(nc.sync, wa_sc, wa_rows, r)
-        nc.sync.dma_start(out=a_lo[:], in_=a_view[:, 0:2, :])
         nc.sync.dma_start(out=wb_w[:], in_=wbt_words.rearrange("f s p k d -> p (f s) (k d)").bitcast(I32))
 
         def first_product(dst, j, t0, n):
@@ -111,7 +113,7 @@ def tile_moe_plb_none_kernel(
             nc.vector.tensor_tensor(
                 out=pairs[:, 2 * t0 : 2 * (t0 + n)].rearrange("p (u i e) -> p u e i", i=4, e=2),
                 in0=dh[:].rearrange("p e (u i) -> p u e i", i=4),
-                in1=saved[:, :, t0 : t0 + n].rearrange("p e (u i) -> p u e i", i=4),
+                in1=saved.rearrange("p e (u i) -> p u e i", i=4),
                 op=MULT,
             )
 
@@ -119,17 +121,27 @@ def tile_moe_plb_none_kernel(
             words = dst.rearrange("p u j -> p (u j)").bitcast(U32).rearrange("p (u h) -> p u h", h=2)
             nc.vector.tensor_copy(out=words[:, :, h], in_=pairs.bitcast(U32).indirect(offsets(lst, s0, dst.shape[1])))
 
+        def gather_plane(dst, pairs, lst, s0):
+            nc.vector.tensor_copy(out=dst, in_=pairs.bitcast(U32).indirect(offsets(lst, s0, dst.shape[1])))
+
+        def weave(dst, planes):
+            nc.gpsimd.tensor_copy(
+                out=dst[:].rearrange("p u j -> p (u j)").bitcast(U32).rearrange("p (u h) -> p u h", h=2),
+                in_=planes[:].rearrange("p h u -> p u h"),
+            )
+
         def quantise(src, name):
             slots = src.shape[1]
             codes = tile([P, slots], U32, name + "_w")
             scales = tile([P, slots], U8, name + "_s")
             nc.vector.quantize_mx(out=codes[:].bitcast(FP8X4), scales=scales[:], in_=src.rearrange("p u j -> p (u j)"))
-            return codes, scales
+            return codes[:], scales[:]
 
         da_row = [tile([P, T], BF16, "da_row%d" % j) for j in range(2)]
         da_hi = tile([P, 2 * T], BF16, "da_hi")
         dc_hi = c_hi[:, 0, :].bitcast(BF16)
-        dh_lo = tile([P, 2, T], F32, "dh_lo")
+        dh_lo = [tile([P, T], F32, "dh_lo%d" % j) for j in range(2)]
+        dc_lo = tile([P, 2 * T], BF16, "dc_lo")
         ga = [tile([P, G, 4], BF16, "ga%d" % g) for g in range(2)]
         gc = [tile([P, G, 4], BF16, "gc%d" % g) for g in range(2)]
 
@@ -139,12 +151,11 @@ def tile_moe_plb_none_kernel(
                 dh = bank([P, n], "dh%d%d" % (j, b))
                 first_product(dh[:], j, t0, n)
                 nc.vector.tensor_tensor(out=da_row[j][:, t0 : t0 + n], in0=dh[:], in1=c_row[j][:, t0 : t0 + n], op=MULT)
-                if j == 0:
-                    nc.scalar.activation(dh_lo[:, j, t0 : t0 + n], dh[:], COPY)
+                nc.scalar.activation(dh_lo[j][:, t0 : t0 + n], dh[:], COPY)
                 t0 += n
+            nc.gpsimd.tensor_tensor(out=dc_lo[:].rearrange("p (t e) -> p t e", e=2)[:, :, j], in0=dh_lo[j][:], in1=a_row[j][:], op=MULT)
             for g in range(2):
                 nc.scalar.activation(ga[g][:, :, j], da_row[j][:].indirect(offsets(list_a, g * G, G)), COPY)
-        nc.scalar.activation(dh_lo[:, 1, :], dh[:], COPY)
         spans = [(0, 256), (256, 128), (384, 128)]
         dh_hi = []
         for b, (t0, n) in enumerate(spans):
@@ -152,7 +163,7 @@ def tile_moe_plb_none_kernel(
             dh_hi.append(dh)
             for e in range(2):
                 first_product(dh[:, e, :], 2 + e, t0, n)
-            product_pairs(da_hi, dh, c_hi, t0, n)
+            product_pairs(da_hi, dh, c_hi[:, :, t0 : t0 + n], t0, n)
 
         wb_sc = dy_sc[:].rearrange("p s (f k) -> p (s f) k", k=K)
         wb_rows = wbt_scales.rearrange("f s (q r) k -> r q (f s) k", r=4)
@@ -168,8 +179,8 @@ def tile_moe_plb_none_kernel(
                 out=dst,
                 lhsT=wa_w[:, s0 // C1, kt * 256 : (kt + 1) * 256].bitcast(FP4X4),
                 lhsT_scale=wa_sc[:, s0 // C1, kt * 128 : (kt + 1) * 128],
-                rhs=codes[:].bitcast(FP8X4),
-                rhs_scale=scales[:],
+                rhs=codes.bitcast(FP8X4),
+                rhs_scale=scales,
                 start=True,
                 stop=True,
             )
@@ -205,7 +216,8 @@ def tile_moe_plb_none_kernel(
             nc.vector.tensor_copy(out=window[:].indirect(offsets(lst, s0, src.shape[1])), in_=src)
 
         def dc_high(b):
-            product_pairs(dc_hi, dh_hi[b], a_hi, *spans[b])
+            t0, n = spans[b]
+            product_pairs(dc_hi, dh_hi[b], a_hi[:, :, t0 : t0 + n], t0, n)
 
         dc_high(1)
         gather_pairs(ga[0][:, 0:128, :], 1, da_hi[:], list_a, 0)
@@ -214,52 +226,48 @@ def tile_moe_plb_none_kernel(
         gather_pairs(ga[0][:, 128:256, :], 1, da_hi[:], list_a, 128)
         gather_pairs(ga[1][:], 1, da_hi[:], list_a, 256)
         qa1 = quantise(ga[0][:, 128:256, :], "qa1")
-        qa2 = quantise(ga[1][:], "qa2")
         dc_high(0)
+        qa2 = quantise(ga[1][:], "qa2")
         for kt in range(2):
             ru = bank([P, 128], "r0%d" % kt, "dh0%d" % kt)
             expert_a(ru[:], qa0, 0, kt)
             res = leave_scalar(ru[:], "r0%d" % kt)
             scatter_scalar(r_tok[kt], list_a, 0, res[:])
-        ru = bank([P, 2, 128], "r1")
-        for kt in range(2):
-            expert_a(ru[:, kt, :], qa1, 128, kt)
-        res = leave_scalar(ru[:], "r1")
-        scatter_scalar(r_tok[0], list_a, 128, res[:, 0, :])
-        r11 = res[:, 1, :]
+        r10 = bank([P, 128], "r10", "dh10")
+        expert_a(r10[:], qa1, 128, 0)
+        res = leave_scalar(r10[:], "r10")
+        scatter_scalar(r_tok[0], list_a, 128, res[:])
         r20 = bank([P, G], "r20")
         expert_a(r20[:], qa2, 256, 0)
         res = leave_scalar(r20[:], "r20")
         scatter_scalar(r_tok[0], list_a, 256, res[:])
+        r_mid = bank([P, G], "r_mid")
+        expert_a(r_mid[:, 0:128], qa1, 128, 1)
+        expert_a(r_mid[:, 128:G], [part[:, 0:128] for part in qa2], 256, 1)
 
-        dc_lo = tile([P, 2 * T], BF16, "dc_lo", "ga1")
-        nc.gpsimd.tensor_tensor(
-            out=dc_lo[:].rearrange("p (u i e) -> p u e i", i=4, e=2),
-            in0=dh_lo[:].rearrange("p e (u i) -> p u e i", i=4),
-            in1=a_lo[:].rearrange("p e (u i) -> p u e i", i=4),
-            op=MULT,
-        )
-        gather_pairs(gc[0][:], 1, dc_hi, list_c, 0)
-        gather_pairs(gc[1][:], 1, dc_hi, list_c, G)
-        scatter_vector(r_tok[1], list_a, 128, r11)
-        gather_pairs(gc[0][:], 0, dc_lo[:], list_c, 0)
-        gather_pairs(gc[1][:], 0, dc_lo[:], list_c, G)
-        qc = [quantise(gc[g][:], "qc%d" % g) for g in range(2)]
-        tags = [["dh10", "dh_hi0"], ["dh_hi1", "dh_hi2"]]
-        SHARE = 128
+        planes = [tile([P, 2, G], U32, "planes%d" % g, "ga%d" % g) for g in range(2)]
+        for g in range(2):
+            gather_plane(planes[g][:, 0, :], dc_lo[:], list_c, g * G)
+            gather_plane(planes[g][:, 1, :], dc_hi, list_c, g * G)
+            weave(gc[g], planes[g])
+        r_rest = tile([P, G + 128], F32, "r_rest", "ga0")
+        nc.vector.tensor_copy(out=r_rest[:, 0:G], in_=r_mid[:])
+        qc = [quantise(gc[0][:], "qc0")]
+        scatter_vector(r_tok[1], list_a, 128, r_rest[:, 0:SHARE])
+        qc.append(quantise(gc[1][:], "qc1"))
+        tags = [["dh00", "dh_hi0"], ["dh_hi1", "dh_hi2"]]
         for g in range(2):
             qb = [bank([P, G], "q%d%d" % (g, kt), tags[g][kt]) for kt in range(2)]
             for kt in range(2):
                 experts_b(qb[kt], qc[g], g, kt)
-            res = leave_vector(qb[0][:], "q%d0" % g)
-            scatter_vector(q_tok[0], list_c, g * G, res[:])
-            res = leave_scalar(qb[1][:], "q%d1" % g)
-            scatter_scalar(q_tok[1], list_c, g * G, res[:, 0 : G if g == 0 else SHARE])
-        scatter_vector(q_tok[1], list_c, G + SHARE, res[:, SHARE:G])
-        r21 = bank([P, G], "r21", "dh_hi0")
-        expert_a(r21[:], qa2, 256, 1)
-        res = leave_scalar(r21[:], "r21")
-        scatter_scalar(r_tok[1], list_a, 256, res[:])
+            res = leave_vector(qb[1][:], "q%d1" % g)
+            scatter_vector(q_tok[1], list_c, g * G, res[:])
+            res = leave_scalar(qb[0][:], "q%d0" % g)
+            scatter_scalar(q_tok[0], list_c, g * G, res[:])
+        r21 = bank([P, 128], "r21", "dh00")
+        expert_a(r21[:], [part[:, 128:G] for part in qa2], 256, 1)
+        nc.scalar.activation(r_rest[:, G : G + 128], r21[:], COPY)
+        scatter_scalar(r_tok[1], list_a, 128 + SHARE, r_rest[:, SHARE : G + 128])
 
         res0 = tile([P, T], F32, "res0")
         nc.gpsimd.tensor_tensor(out=res0[:], in0=r_tok[0][:], in1=q_tok[0][:], op=ADD)

@@ -21,7 +21,7 @@ COPY = mybir.ActivationFunctionType.Copy
 P = 128
 PASSES = N // 512
 G = 256
-SHARE = 192
+SHARE = 224
 
 
 def tile_moe_plb_none_kernel(
@@ -50,7 +50,8 @@ def tile_moe_plb_none_kernel(
         dy_sc = tile([P, PASSES, T], U8, "dy_sc")
         w2_raw = tile([P, PASSES, 2 * H], U8, "w2_raw")
         dy_w = tile([P, PASSES, T], I32, "dy_w")
-        c_row = [tile([P, T], F32, "c_row%d" % j) for j in range(2)]
+        room = tile([P, 1280], U32, "room")
+        c_row = [tile([P, T], F32, "c_row0")[:], room[:, 768:1280].bitcast(F32)]
         c_hi = tile([P, 2, T], F32, "c_hi")
         a_row = [tile([P, T], F32, "a_row%d" % j) for j in range(2)]
         a_hi = tile([P, 2, T], F32, "a_hi")
@@ -73,15 +74,14 @@ def tile_moe_plb_none_kernel(
         nc.sync.dma_start(out=dy_w[:], in_=dy_words.rearrange("s p t d -> p s (t d)").bitcast(I32))
         load_scale_row(nc.sync, dy_sc, dy_rows, 2)
         load_scale_row(nc.sync, dy_sc, dy_rows, 3)
-        nc.sync.dma_start(out=c_row[0][:], in_=c_view[:, 0, :])
+        nc.sync.dma_start(out=c_row[0], in_=c_view[:, 0, :])
         nc.sync.dma_start(list_a[:], offs)
-        nc.sync.dma_start(out=c_row[1][:], in_=c_view[:, 1, :])
+        nc.sync.dma_start(out=c_row[1], in_=c_view[:, 1, :])
         nc.sync.dma_start(out=c_hi[:], in_=c_view[:, 2:4, :])
-        nc.sync.dma_start(out=a_row[0][:], in_=a_view[:, 0, :])
-        nc.sync.dma_start(out=a_hi[:], in_=a_view[:, 2:4, :])
-        nc.sync.dma_start(out=a_row[1][:], in_=a_view[:, 1, :])
-        nc.sync.dma_start(list_c[:], offs2)
         nc.sync.dma_start(out=wa_w[:].bitcast(I32), in_=wat_words.rearrange("e s p b -> p (e s) b").bitcast(I32))
+        nc.sync.dma_start(out=a_row[0][:], in_=a_view[:, 0, :])
+        nc.sync.dma_start(out=a_row[1][:], in_=a_view[:, 1, :])
+        nc.sync.dma_start(out=a_hi[:], in_=a_view[:, 2:4, :])
 
         w2_p = [tile([P, PASSES, 2, 2 * P], U8, "w2_p%d" % h) for h in range(2)]
         w2_sc = [tile([P, PASSES, 2, P], U8, "w2_sc%d" % h) for h in range(2)]
@@ -95,6 +95,7 @@ def tile_moe_plb_none_kernel(
         wa_rows = wat_scales.rearrange("e s (q r) k -> r q (e s) k", r=4)
         for r in range(4):
             load_scale_row(nc.sync, wa_sc, wa_rows, r)
+        nc.sync.dma_start(list_c[:], offs2)
         nc.sync.dma_start(out=wb_w[:], in_=wbt_words.rearrange("f s p k d -> p (f s) (k d)").bitcast(I32))
 
         def first_product(dst, j, t0, n):
@@ -127,7 +128,7 @@ def tile_moe_plb_none_kernel(
         def weave(dst, planes):
             nc.gpsimd.tensor_copy(
                 out=dst[:].rearrange("p u j -> p (u j)").bitcast(U32).rearrange("p (u h) -> p u h", h=2),
-                in_=planes[:].rearrange("p h u -> p u h"),
+                in_=planes.rearrange("p h u -> p u h"),
             )
 
         def quantise(src, name):
@@ -142,8 +143,10 @@ def tile_moe_plb_none_kernel(
         dc_hi = c_hi[:, 0, :].bitcast(BF16)
         dh_lo = [tile([P, T], F32, "dh_lo%d" % j) for j in range(2)]
         dc_lo = tile([P, 2 * T], BF16, "dc_lo")
-        ga = [tile([P, G, 4], BF16, "ga%d" % g) for g in range(2)]
-        gc = [tile([P, G, 4], BF16, "gc%d" % g) for g in range(2)]
+        ga = room[:, 0:1024].bitcast(BF16).rearrange("p (u j) -> p u j", j=4)
+
+        def gather_row(j, s0, n):
+            nc.scalar.activation(ga[:, s0 : s0 + n, j], da_row[j][:].indirect(offsets(list_a, s0, n)), COPY)
 
         for j, widths in enumerate([(256, 256), (512,)]):
             t0 = 0
@@ -154,8 +157,9 @@ def tile_moe_plb_none_kernel(
                 nc.scalar.activation(dh_lo[j][:, t0 : t0 + n], dh[:], COPY)
                 t0 += n
             nc.gpsimd.tensor_tensor(out=dc_lo[:].rearrange("p (t e) -> p t e", e=2)[:, :, j], in0=dh_lo[j][:], in1=a_row[j][:], op=MULT)
-            for g in range(2):
-                nc.scalar.activation(ga[g][:, :, j], da_row[j][:].indirect(offsets(list_a, g * G, G)), COPY)
+            gather_row(j, 0, 384 if j == 0 else 128)
+        gather_row(0, 384, 128)
+        gather_row(1, 128, 384)
         spans = [(0, 256), (256, 128), (384, 128)]
         dh_hi = []
         for b, (t0, n) in enumerate(spans):
@@ -220,14 +224,14 @@ def tile_moe_plb_none_kernel(
             product_pairs(dc_hi, dh_hi[b], a_hi[:, :, t0 : t0 + n], t0, n)
 
         dc_high(1)
-        gather_pairs(ga[0][:, 0:128, :], 1, da_hi[:], list_a, 0)
+        gather_pairs(ga[:, 0:128, :], 1, da_hi[:], list_a, 0)
         dc_high(2)
-        qa0 = quantise(ga[0][:, 0:128, :], "qa0")
-        gather_pairs(ga[0][:, 128:256, :], 1, da_hi[:], list_a, 128)
-        gather_pairs(ga[1][:], 1, da_hi[:], list_a, 256)
-        qa1 = quantise(ga[0][:, 128:256, :], "qa1")
+        qa0 = quantise(ga[:, 0:128, :], "qa0")
+        gather_pairs(ga[:, 128:256, :], 1, da_hi[:], list_a, 128)
+        gather_pairs(ga[:, 256:512, :], 1, da_hi[:], list_a, 256)
+        qa1 = quantise(ga[:, 128:256, :], "qa1")
         dc_high(0)
-        qa2 = quantise(ga[1][:], "qa2")
+        qa2 = quantise(ga[:, 256:512, :], "qa2")
         for kt in range(2):
             ru = bank([P, 128], "r0%d" % kt, "dh0%d" % kt)
             expert_a(ru[:], qa0, 0, kt)
@@ -245,35 +249,41 @@ def tile_moe_plb_none_kernel(
         expert_a(r_mid[:, 0:128], qa1, 128, 1)
         expert_a(r_mid[:, 128:G], [part[:, 0:128] for part in qa2], 256, 1)
 
-        planes = [tile([P, 2, G], U32, "planes%d" % g, "ga%d" % g) for g in range(2)]
+        planes = [room[:, 0 : 2 * G].rearrange("p (h u) -> p h u", h=2), a_hi[:, :, 0:G].bitcast(U32)]
         for g in range(2):
             gather_plane(planes[g][:, 0, :], dc_lo[:], list_c, g * G)
             gather_plane(planes[g][:, 1, :], dc_hi, list_c, g * G)
-            weave(gc[g], planes[g])
-        r_rest = tile([P, G + 128], F32, "r_rest", "ga0")
+        gc = tile([P, G, 4], BF16, "gc0", "gc")
+        weave(gc, planes[0])
+        r_rest = room[:, 0 : G + 128].bitcast(F32)
         nc.vector.tensor_copy(out=r_rest[:, 0:G], in_=r_mid[:])
-        qc = [quantise(gc[0][:], "qc0")]
+        qc = [quantise(gc[:], "qc0")]
+        gc = tile([P, G, 4], BF16, "gc1", "gc")
+        weave(gc, planes[1])
         scatter_vector(r_tok[1], list_a, 128, r_rest[:, 0:SHARE])
-        qc.append(quantise(gc[1][:], "qc1"))
-        tags = [["dh00", "dh_hi0"], ["dh_hi1", "dh_hi2"]]
+        qc.append(quantise(gc[:], "qc1"))
         for g in range(2):
-            qb = [bank([P, G], "q%d%d" % (g, kt), tags[g][kt]) for kt in range(2)]
-            for kt in range(2):
-                experts_b(qb[kt], qc[g], g, kt)
-            res = leave_vector(qb[1][:], "q%d1" % g)
+            q0 = bank([P, G + 128], "q%d0" % g, "dh00")
+            q1 = bank([P, G], "q%d1" % g, "dh_hi0")
+            experts_b(q0[:, 0:G], qc[g], g, 0)
+            if g == 1:
+                expert_a(q0[:, G : G + 128], [part[:, 128:G] for part in qa2], 256, 1)
+            experts_b(q1, qc[g], g, 1)
+            res = leave_vector(q1[:], "q%d1" % g)
             scatter_vector(q_tok[1], list_c, g * G, res[:])
-            res = leave_scalar(qb[0][:], "q%d0" % g)
+            res = leave_scalar(q0[:, 0:G], "q%d0" % g)
+            if g == 1:
+                nc.scalar.activation(r_rest[:, G : G + 128], q0[:, G : G + 128], COPY)
             scatter_scalar(q_tok[0], list_c, g * G, res[:])
-        r21 = bank([P, 128], "r21", "dh00")
-        expert_a(r21[:], [part[:, 128:G] for part in qa2], 256, 1)
-        nc.scalar.activation(r_rest[:, G : G + 128], r21[:], COPY)
         scatter_scalar(r_tok[1], list_a, 128 + SHARE, r_rest[:, SHARE : G + 128])
 
-        res0 = tile([P, T], F32, "res0")
-        nc.gpsimd.tensor_tensor(out=res0[:], in0=r_tok[0][:], in1=q_tok[0][:], op=ADD)
-        nc.sync.dma_start(out=out[0:P, :], in_=res0[:])
-        for part, queue in enumerate([nc.scalar, nc.sync]):
+        def store_sum(engine, queue, kt, part):
             cols = slice(part * T // 2, (part + 1) * T // 2)
-            res = tile([P, T // 2], F32, "res1%d" % part)
-            nc.vector.tensor_tensor(out=res[:], in0=r_tok[1][:, cols], in1=q_tok[1][:, cols], op=ADD)
-            queue.dma_start(out=out[P : 2 * P, cols], in_=res[:])
+            res = tile([P, T // 2], F32, "res%d%d" % (kt, part))
+            engine.tensor_tensor(out=res[:], in0=r_tok[kt][:, cols], in1=q_tok[kt][:, cols], op=ADD)
+            queue.dma_start(out=out[kt * P : (kt + 1) * P, cols], in_=res[:])
+
+        store_sum(nc.gpsimd, nc.sync, 0, 0)
+        store_sum(nc.vector, nc.sync, 0, 1)
+        store_sum(nc.vector, nc.scalar, 1, 0)
+        store_sum(nc.vector, nc.sync, 1, 1)

@@ -21,7 +21,7 @@ COPY = mybir.ActivationFunctionType.Copy
 P = 128
 PASSES = N // 512
 G = 256
-SHARE = 224
+EARLY = 320
 
 
 def tile_moe_plb_none_kernel(
@@ -78,10 +78,10 @@ def tile_moe_plb_none_kernel(
         nc.sync.dma_start(list_a[:], offs)
         nc.sync.dma_start(out=c_row[1], in_=c_view[:, 1, :])
         nc.sync.dma_start(out=c_hi[:], in_=c_view[:, 2:4, :])
-        nc.sync.dma_start(out=wa_w[:].bitcast(I32), in_=wat_words.rearrange("e s p b -> p (e s) b").bitcast(I32))
+        nc.sync.dma_start(out=a_hi[:], in_=a_view[:, 2:4, :])
         nc.sync.dma_start(out=a_row[0][:], in_=a_view[:, 0, :])
         nc.sync.dma_start(out=a_row[1][:], in_=a_view[:, 1, :])
-        nc.sync.dma_start(out=a_hi[:], in_=a_view[:, 2:4, :])
+        nc.sync.dma_start(out=wa_w[:].bitcast(I32), in_=wat_words.rearrange("e s p b -> p (e s) b").bitcast(I32))
 
         w2_p = [tile([P, PASSES, 2, 2 * P], U8, "w2_p%d" % h) for h in range(2)]
         w2_sc = [tile([P, PASSES, 2, P], U8, "w2_sc%d" % h) for h in range(2)]
@@ -140,10 +140,10 @@ def tile_moe_plb_none_kernel(
 
         da_row = [tile([P, T], BF16, "da_row%d" % j) for j in range(2)]
         da_hi = tile([P, 2 * T], BF16, "da_hi")
-        dc_hi = c_hi[:, 0, :].bitcast(BF16)
+        dc_hi = c_hi[:].rearrange("p e t -> p (e t)")[:, 448 : 448 + T].bitcast(BF16)
         dh_lo = [tile([P, T], F32, "dh_lo%d" % j) for j in range(2)]
         dc_lo = tile([P, 2 * T], BF16, "dc_lo")
-        ga = room[:, 0:1024].bitcast(BF16).rearrange("p (u j) -> p u j", j=4)
+        ga = room[:, 128:1152].bitcast(BF16).rearrange("p (u j) -> p u j", j=4)
 
         def gather_row(j, s0, n):
             nc.scalar.activation(ga[:, s0 : s0 + n, j], da_row[j][:].indirect(offsets(list_a, s0, n)), COPY)
@@ -157,8 +157,8 @@ def tile_moe_plb_none_kernel(
                 nc.scalar.activation(dh_lo[j][:, t0 : t0 + n], dh[:], COPY)
                 t0 += n
             nc.gpsimd.tensor_tensor(out=dc_lo[:].rearrange("p (t e) -> p t e", e=2)[:, :, j], in0=dh_lo[j][:], in1=a_row[j][:], op=MULT)
-            gather_row(j, 0, 384 if j == 0 else 128)
-        gather_row(0, 384, 128)
+            gather_row(j, 0, EARLY if j == 0 else 128)
+        gather_row(0, EARLY, T - EARLY)
         gather_row(1, 128, 384)
         spans = [(0, 256), (256, 128), (384, 128)]
         dh_hi = []
@@ -237,30 +237,31 @@ def tile_moe_plb_none_kernel(
             expert_a(ru[:], qa0, 0, kt)
             res = leave_scalar(ru[:], "r0%d" % kt)
             scatter_scalar(r_tok[kt], list_a, 0, res[:])
-        r10 = bank([P, 128], "r10", "dh10")
-        expert_a(r10[:], qa1, 128, 0)
-        res = leave_scalar(r10[:], "r10")
+        r_mid = room[:, 0:G].bitcast(F32)
+        r1 = bank([P, 2, 128], "r1", "dh00")
+        for kt in range(2):
+            expert_a(r1[:, kt, :], qa1, 128, kt)
+        res = leave_scalar(r1[:, 0, :], "r10")
+        nc.scalar.activation(r_mid[:, 0:128], r1[:, 1, :], COPY)
         scatter_scalar(r_tok[0], list_a, 128, res[:])
-        r20 = bank([P, G], "r20")
+        r20 = bank([P, G], "r20", "dh00")
         expert_a(r20[:], qa2, 256, 0)
         res = leave_scalar(r20[:], "r20")
         scatter_scalar(r_tok[0], list_a, 256, res[:])
-        r_mid = bank([P, G], "r_mid")
-        expert_a(r_mid[:, 0:128], qa1, 128, 1)
-        expert_a(r_mid[:, 128:G], [part[:, 0:128] for part in qa2], 256, 1)
+        r21 = bank([P, 128], "r21")
+        expert_a(r21[:], [part[:, 0:128] for part in qa2], 256, 1)
 
-        planes = [room[:, 0 : 2 * G].rearrange("p (h u) -> p h u", h=2), a_hi[:, :, 0:G].bitcast(U32)]
+        planes = [room[:, 128 : 128 + 2 * G].rearrange("p (h u) -> p h u", h=2), a_hi[:, :, 0:G].bitcast(U32)]
         for g in range(2):
             gather_plane(planes[g][:, 0, :], dc_lo[:], list_c, g * G)
             gather_plane(planes[g][:, 1, :], dc_hi, list_c, g * G)
         gc = tile([P, G, 4], BF16, "gc0", "gc")
         weave(gc, planes[0])
-        r_rest = room[:, 0 : G + 128].bitcast(F32)
-        nc.vector.tensor_copy(out=r_rest[:, 0:G], in_=r_mid[:])
+        nc.vector.tensor_copy(out=r_mid[:, 128:G], in_=r21[:])
         qc = [quantise(gc[:], "qc0")]
         gc = tile([P, G, 4], BF16, "gc1", "gc")
         weave(gc, planes[1])
-        scatter_vector(r_tok[1], list_a, 128, r_rest[:, 0:SHARE])
+        scatter_vector(r_tok[1], list_a, 128, r_mid)
         qc.append(quantise(gc[:], "qc1"))
         for g in range(2):
             q0 = bank([P, G + 128], "q%d0" % g, "dh00")
@@ -269,21 +270,21 @@ def tile_moe_plb_none_kernel(
             if g == 1:
                 expert_a(q0[:, G : G + 128], [part[:, 128:G] for part in qa2], 256, 1)
             experts_b(q1, qc[g], g, 1)
-            res = leave_vector(q1[:], "q%d1" % g)
-            scatter_vector(q_tok[1], list_c, g * G, res[:])
-            res = leave_scalar(q0[:, 0:G], "q%d0" % g)
-            if g == 1:
-                nc.scalar.activation(r_rest[:, G : G + 128], q0[:, G : G + 128], COPY)
-            scatter_scalar(q_tok[0], list_c, g * G, res[:])
-        scatter_scalar(r_tok[1], list_a, 128 + SHARE, r_rest[:, SHARE : G + 128])
+            res0 = leave_scalar(q0[:, 0:G], "q%d0" % g)
+            if g == 0:
+                res1 = leave_scalar(q1[:], "q01")
+            else:
+                res1 = leave_vector(q1[:], "q11")
+                r_last = leave_scalar(q0[:, G : G + 128], "r_last")
+            scatter_scalar(q_tok[0], list_c, g * G, res0[:])
+            scatter_vector(q_tok[1], list_c, g * G, res1[:])
+        scatter_scalar(r_tok[1], list_a, 384, r_last[:])
 
-        def store_sum(engine, queue, kt, part):
-            cols = slice(part * T // 2, (part + 1) * T // 2)
-            res = tile([P, T // 2], F32, "res%d%d" % (kt, part))
-            engine.tensor_tensor(out=res[:], in0=r_tok[kt][:, cols], in1=q_tok[kt][:, cols], op=ADD)
-            queue.dma_start(out=out[kt * P : (kt + 1) * P, cols], in_=res[:])
+        def store_sum(queue, kt, t0, n):
+            res = tile([P, n], F32, "res%d_%d" % (kt, t0))
+            nc.vector.tensor_tensor(out=res[:], in0=r_tok[kt][:, t0 : t0 + n], in1=q_tok[kt][:, t0 : t0 + n], op=ADD)
+            queue.dma_start(out=out[kt * P : (kt + 1) * P, t0 : t0 + n], in_=res[:])
 
-        store_sum(nc.gpsimd, nc.sync, 0, 0)
-        store_sum(nc.vector, nc.sync, 0, 1)
-        store_sum(nc.vector, nc.scalar, 1, 0)
-        store_sum(nc.vector, nc.sync, 1, 1)
+        store_sum(nc.sync, 0, 0, T)
+        store_sum(nc.scalar, 1, 0, T // 2)
+        store_sum(nc.sync, 1, T // 2, T // 2)

@@ -54,7 +54,7 @@ def tile_moe_plb_none_kernel(
         c_row = [tile([P, T], F32, "c_row0")[:], room[:, 768:1280].bitcast(F32)]
         c_hi = tile([P, 2, T], F32, "c_hi")
         a_row = [tile([P, T], F32, "a_row%d" % j) for j in range(2)]
-        a_hi = tile([P, 2, T], F32, "a_hi")
+        a_hi = [tile([P, 2, T // 2], F32, "a_hi%d" % half) for half in range(2)]
         wa_w = tile([P, E1, 2 * K], U8, "wa_w")
         wb_w = tile([P, E2, K], I32, "wb_w")
 
@@ -78,10 +78,7 @@ def tile_moe_plb_none_kernel(
         nc.sync.dma_start(list_a[:], offs)
         nc.sync.dma_start(out=c_row[1], in_=c_view[:, 1, :])
         nc.sync.dma_start(out=c_hi[:], in_=c_view[:, 2:4, :])
-        nc.sync.dma_start(out=a_hi[:], in_=a_view[:, 2:4, :])
-        nc.sync.dma_start(out=a_row[0][:], in_=a_view[:, 0, :])
-        nc.sync.dma_start(out=a_row[1][:], in_=a_view[:, 1, :])
-        nc.sync.dma_start(out=wa_w[:].bitcast(I32), in_=wat_words.rearrange("e s p b -> p (e s) b").bitcast(I32))
+        nc.sync.dma_start(out=a_hi[1][:], in_=a_view[:, 2:4, T // 2 : T])
 
         w2_p = [tile([P, PASSES, 2, 2 * P], U8, "w2_p%d" % h) for h in range(2)]
         w2_sc = [tile([P, PASSES, 2, P], U8, "w2_sc%d" % h) for h in range(2)]
@@ -95,6 +92,10 @@ def tile_moe_plb_none_kernel(
         wa_rows = wat_scales.rearrange("e s (q r) k -> r q (e s) k", r=4)
         for r in range(4):
             load_scale_row(nc.sync, wa_sc, wa_rows, r)
+        nc.sync.dma_start(out=a_row[0][:], in_=a_view[:, 0, :])
+        nc.sync.dma_start(out=a_row[1][:], in_=a_view[:, 1, :])
+        nc.sync.dma_start(out=wa_w[:].bitcast(I32), in_=wat_words.rearrange("e s p b -> p (e s) b").bitcast(I32))
+        nc.sync.dma_start(out=a_hi[0][:], in_=a_view[:, 2:4, 0 : T // 2])
         nc.sync.dma_start(list_c[:], offs2)
         nc.sync.dma_start(out=wb_w[:], in_=wbt_words.rearrange("f s p k d -> p (f s) (k d)").bitcast(I32))
 
@@ -221,7 +222,7 @@ def tile_moe_plb_none_kernel(
 
         def dc_high(b):
             t0, n = spans[b]
-            product_pairs(dc_hi, dh_hi[b], a_hi[:, :, t0 : t0 + n], t0, n)
+            product_pairs(dc_hi, dh_hi[b], a_hi[t0 // 256][:, :, t0 % 256 : t0 % 256 + n], t0, n)
 
         dc_high(1)
         gather_pairs(ga[:, 0:128, :], 1, da_hi[:], list_a, 0)
@@ -251,7 +252,7 @@ def tile_moe_plb_none_kernel(
         r21 = bank([P, 128], "r21")
         expert_a(r21[:], [part[:, 0:128] for part in qa2], 256, 1)
 
-        planes = [room[:, 128 : 128 + 2 * G].rearrange("p (h u) -> p h u", h=2), a_hi[:, :, 0:G].bitcast(U32)]
+        planes = [room[:, 128 : 128 + 2 * G].rearrange("p (h u) -> p h u", h=2), a_hi[0][:].bitcast(U32)]
         for g in range(2):
             gather_plane(planes[g][:, 0, :], dc_lo[:], list_c, g * G)
             gather_plane(planes[g][:, 1, :], dc_hi, list_c, g * G)

@@ -21,7 +21,10 @@ COPY = mybir.ActivationFunctionType.Copy
 P = 128
 PASSES = N // 512
 G = 256
-EARLY = 320
+U0 = 128
+LOW = [(320, 192), (0, 320)]
+EARLY = 256
+UNIT_STEP = 528
 
 
 def tile_moe_plb_none_kernel(
@@ -50,11 +53,13 @@ def tile_moe_plb_none_kernel(
         dy_sc = tile([P, PASSES, T], U8, "dy_sc")
         w2_raw = tile([P, PASSES, 2 * H], U8, "w2_raw")
         dy_w = tile([P, PASSES, T], I32, "dy_w")
-        room = tile([P, 1280], U32, "room")
-        c_row = [tile([P, T], F32, "c_row0")[:], room[:, 768:1280].bitcast(F32)]
-        c_hi = tile([P, 2, T], F32, "c_hi")
-        a_row = [tile([P, T], F32, "a_row%d" % j) for j in range(2)]
-        a_hi = [tile([P, 2, T // 2], F32, "a_hi%d" % half) for half in range(2)]
+        room = tile([P, T + UNIT_STEP + 2 * (T - U0)], U32, "room")
+        rest = room[:, T + UNIT_STEP :]
+        c_row = [tile([P, T], F32, "c_row0")[:], rest[:, 2 * (EARLY - U0) :].bitcast(F32)]
+        late = tile([P, T // 2 + 2 * G], F32, "late")
+        c_hi = [tile([P, 2, G], F32, "c_hi0")[:], late[:, T // 2 :].rearrange("p (e t) -> p e t", e=2)]
+        a_lo = [tile([P, 2, n], F32, "a_lo%d" % t0) for t0, n in LOW]
+        a_hi = [tile([P, 2, G], F32, "a_hi%d" % half) for half in range(2)]
         wa_w = tile([P, E1, 2 * K], U8, "wa_w")
         wb_w = tile([P, E2, K], I32, "wb_w")
 
@@ -77,8 +82,11 @@ def tile_moe_plb_none_kernel(
         nc.sync.dma_start(out=c_row[0], in_=c_view[:, 0, :])
         nc.sync.dma_start(list_a[:], offs)
         nc.sync.dma_start(out=c_row[1], in_=c_view[:, 1, :])
-        nc.sync.dma_start(out=c_hi[:], in_=c_view[:, 2:4, :])
-        nc.sync.dma_start(out=a_hi[1][:], in_=a_view[:, 2:4, T // 2 : T])
+        for half in range(2):
+            nc.sync.dma_start(out=c_hi[half], in_=c_view[:, 2:4, half * G : (half + 1) * G])
+        nc.sync.dma_start(out=a_hi[1][:], in_=a_view[:, 2:4, G:T])
+        nc.sync.dma_start(out=a_lo[0][:], in_=a_view[:, 0:2, LOW[0][0] : T])
+        nc.sync.dma_start(out=a_hi[0][:], in_=a_view[:, 2:4, 0:G])
 
         w2_p = [tile([P, PASSES, 2, 2 * P], U8, "w2_p%d" % h) for h in range(2)]
         w2_sc = [tile([P, PASSES, 2, P], U8, "w2_sc%d" % h) for h in range(2)]
@@ -92,12 +100,10 @@ def tile_moe_plb_none_kernel(
         wa_rows = wat_scales.rearrange("e s (q r) k -> r q (e s) k", r=4)
         for r in range(4):
             load_scale_row(nc.sync, wa_sc, wa_rows, r)
-        nc.sync.dma_start(out=a_row[0][:], in_=a_view[:, 0, :])
-        nc.sync.dma_start(out=a_row[1][:], in_=a_view[:, 1, :])
         nc.sync.dma_start(out=wa_w[:].bitcast(I32), in_=wat_words.rearrange("e s p b -> p (e s) b").bitcast(I32))
-        nc.sync.dma_start(out=a_hi[0][:], in_=a_view[:, 2:4, 0 : T // 2])
-        nc.sync.dma_start(list_c[:], offs2)
+        nc.sync.dma_start(out=a_lo[1][:], in_=a_view[:, 0:2, 0 : LOW[0][0]])
         nc.sync.dma_start(out=wb_w[:], in_=wbt_words.rearrange("f s p k d -> p (f s) (k d)").bitcast(I32))
+        nc.sync.dma_start(list_c[:], offs2)
 
         def first_product(dst, j, t0, n):
             for s in range(PASSES):
@@ -111,10 +117,10 @@ def tile_moe_plb_none_kernel(
                     stop=(s == PASSES - 1),
                 )
 
-        def product_pairs(pairs, dh, saved, t0, n):
-            nc.vector.tensor_tensor(
+        def product_pairs(engine, pairs, dh, saved, t0, n):
+            engine.tensor_tensor(
                 out=pairs[:, 2 * t0 : 2 * (t0 + n)].rearrange("p (u i e) -> p u e i", i=4, e=2),
-                in0=dh[:].rearrange("p e (u i) -> p u e i", i=4),
+                in0=dh.rearrange("p e (u i) -> p u e i", i=4),
                 in1=saved.rearrange("p e (u i) -> p u e i", i=4),
                 op=MULT,
             )
@@ -139,15 +145,21 @@ def tile_moe_plb_none_kernel(
             nc.vector.quantize_mx(out=codes[:].bitcast(FP8X4), scales=scales[:], in_=src.rearrange("p u j -> p (u j)"))
             return codes[:], scales[:]
 
-        da_row = [tile([P, T], BF16, "da_row%d" % j) for j in range(2)]
-        da_hi = tile([P, 2 * T], BF16, "da_hi")
-        dc_hi = c_hi[:].rearrange("p e t -> p (e t)")[:, 448 : 448 + T].bitcast(BF16)
-        dh_lo = [tile([P, T], F32, "dh_lo%d" % j) for j in range(2)]
-        dc_lo = tile([P, 2 * T], BF16, "dc_lo")
-        ga = room[:, 128:1152].bitcast(BF16).rearrange("p (u j) -> p u j", j=4)
+        da_row = [late[:, 0 : T // 2].bitcast(BF16), tile([P, T], BF16, "da_row1")[:]]
+        da_hi = room[:, 0:T].bitcast(BF16)
+        dc_hi = late[:, 0:T].bitcast(BF16)
+        dh_lo = tile([P, 2, T], F32, "dh_lo")
+        ga0 = room[:, T : T + 2 * U0].bitcast(BF16).rearrange("p (u j) -> p u j", j=4)
+        ga1 = rest[:, 0 : 2 * (T - U0)].bitcast(BF16).rearrange("p (u j) -> p u j", j=4)
+        dc_lo = room[:, T + 8 : 2 * T + 8].bitcast(BF16)
+        ga_first = room[:, T : T + 2 * UNIT_STEP].rearrange("p (b x) -> p b x", b=2)[:, :, 0 : 2 * U0]
 
-        def gather_row(j, s0, n):
-            nc.scalar.activation(ga[:, s0 : s0 + n, j], da_row[j][:].indirect(offsets(list_a, s0, n)), COPY)
+        def dc_low(part):
+            t0, n = LOW[part]
+            product_pairs(nc.gpsimd, dc_lo, dh_lo[:, :, t0 : t0 + n], a_lo[part][:], t0, n)
+
+        def gather_row(dst, j, s0, n):
+            nc.scalar.activation(dst, da_row[j].indirect(offsets(list_a, s0, n)), COPY)
 
         for j, widths in enumerate([(256, 256), (512,)]):
             t0 = 0
@@ -155,12 +167,15 @@ def tile_moe_plb_none_kernel(
                 dh = bank([P, n], "dh%d%d" % (j, b))
                 first_product(dh[:], j, t0, n)
                 nc.vector.tensor_tensor(out=da_row[j][:, t0 : t0 + n], in0=dh[:], in1=c_row[j][:, t0 : t0 + n], op=MULT)
-                nc.scalar.activation(dh_lo[j][:, t0 : t0 + n], dh[:], COPY)
+                nc.scalar.activation(dh_lo[:, j, t0 : t0 + n], dh[:], COPY)
                 t0 += n
-            nc.gpsimd.tensor_tensor(out=dc_lo[:].rearrange("p (t e) -> p t e", e=2)[:, :, j], in0=dh_lo[j][:], in1=a_row[j][:], op=MULT)
-            gather_row(j, 0, EARLY if j == 0 else 128)
-        gather_row(0, EARLY, T - EARLY)
-        gather_row(1, 128, 384)
+            if j == 0:
+                gather_row(ga_first.bitcast(BF16).rearrange("p b (u j) -> p b u j", j=4)[:, :, :, 0], 0, 0, EARLY)
+            else:
+                gather_row(ga0[:, :, 1], 1, 0, U0)
+        dc_low(0)
+        gather_row(ga1[:, EARLY - U0 :, 0], 0, EARLY, T - EARLY)
+        gather_row(ga1[:, :, 1], 1, U0, T - U0)
         spans = [(0, 256), (256, 128), (384, 128)]
         dh_hi = []
         for b, (t0, n) in enumerate(spans):
@@ -168,7 +183,7 @@ def tile_moe_plb_none_kernel(
             dh_hi.append(dh)
             for e in range(2):
                 first_product(dh[:, e, :], 2 + e, t0, n)
-            product_pairs(da_hi, dh, c_hi[:, :, t0 : t0 + n], t0, n)
+            product_pairs(nc.vector, da_hi, dh[:], c_hi[t0 // G][:, :, t0 % G : t0 % G + n], t0, n)
 
         wb_sc = dy_sc[:].rearrange("p s (f k) -> p (s f) k", k=K)
         wb_rows = wbt_scales.rearrange("f s (q r) k -> r q (f s) k", r=4)
@@ -178,14 +193,15 @@ def tile_moe_plb_none_kernel(
         r_tok = [tile([P, T], F32, "r_tok%d" % kt) for kt in range(2)]
         q_tok = [tile([P, T], F32, "q_tok%d" % kt) for kt in range(2)]
 
-        def expert_a(dst, quantised, s0, kt):
+        def expert_a(dst, quantised, col0, s0, kt):
             codes, scales = quantised
+            n = dst.shape[1]
             nc.tensor.matmul_mx(
                 out=dst,
                 lhsT=wa_w[:, s0 // C1, kt * 256 : (kt + 1) * 256].bitcast(FP4X4),
                 lhsT_scale=wa_sc[:, s0 // C1, kt * 128 : (kt + 1) * 128],
-                rhs=codes.bitcast(FP8X4),
-                rhs_scale=scales,
+                rhs=codes[:, col0 : col0 + n].bitcast(FP8X4),
+                rhs_scale=scales[:, col0 : col0 + n],
                 start=True,
                 stop=True,
             )
@@ -220,42 +236,44 @@ def tile_moe_plb_none_kernel(
         def scatter_vector(window, lst, s0, src):
             nc.vector.tensor_copy(out=window[:].indirect(offsets(lst, s0, src.shape[1])), in_=src)
 
-        def dc_high(b):
-            t0, n = spans[b]
-            product_pairs(dc_hi, dh_hi[b], a_hi[t0 // 256][:, :, t0 % 256 : t0 % 256 + n], t0, n)
+        def dc_high(t0, n=128):
+            b = max(i for i, span in enumerate(spans) if span[0] <= t0)
+            lo = t0 - spans[b][0]
+            product_pairs(nc.vector, dc_hi, dh_hi[b][:, :, lo : lo + n], a_hi[t0 // G][:, :, t0 % G : t0 % G + n], t0, n)
 
-        dc_high(1)
-        gather_pairs(ga[:, 0:128, :], 1, da_hi[:], list_a, 0)
-        dc_high(2)
-        qa0 = quantise(ga[:, 0:128, :], "qa0")
-        gather_pairs(ga[:, 128:256, :], 1, da_hi[:], list_a, 128)
-        gather_pairs(ga[:, 256:512, :], 1, da_hi[:], list_a, 256)
-        qa1 = quantise(ga[:, 128:256, :], "qa1")
+        dc_high(256)
+        gather_pairs(ga0, 1, da_hi, list_a, 0)
+        dc_high(384)
+        qa0 = quantise(ga0, "qa0")
+        gather_pairs(ga1, 1, room[:, 0 : T + 2], list_a, U0)
+        dc_low(1)
         dc_high(0)
-        qa2 = quantise(ga[:, 256:512, :], "qa2")
+        qa1 = quantise(ga1, "qa1")
+        dc_high(128)
+        first = []
         for kt in range(2):
-            ru = bank([P, 128], "r0%d" % kt, "dh0%d" % kt)
-            expert_a(ru[:], qa0, 0, kt)
-            res = leave_scalar(ru[:], "r0%d" % kt)
-            scatter_scalar(r_tok[kt], list_a, 0, res[:])
-        r_mid = room[:, 0:G].bitcast(F32)
-        r1 = bank([P, 2, 128], "r1", "dh00")
+            ru = bank([P, U0], "r0%d" % kt, "dh0%d" % kt)
+            expert_a(ru[:], qa0, 0, 0, kt)
+            first.append(leave_scalar(ru[:], "r0%d" % kt))
         for kt in range(2):
-            expert_a(r1[:, kt, :], qa1, 128, kt)
-        res = leave_scalar(r1[:, 0, :], "r10")
-        nc.scalar.activation(r_mid[:, 0:128], r1[:, 1, :], COPY)
-        scatter_scalar(r_tok[0], list_a, 128, res[:])
-        r20 = bank([P, G], "r20", "dh00")
-        expert_a(r20[:], qa2, 256, 0)
-        res = leave_scalar(r20[:], "r20")
-        scatter_scalar(r_tok[0], list_a, 256, res[:])
+            scatter_scalar(r_tok[kt], list_a, 0, first[kt][:])
+        stage = tile([P, 640], U32, "stage")
+        r_mid = stage[:, 0:G].bitcast(F32)
+        r10 = bank([P, T - U0], "r10", "dh00")
+        expert_a(r10[:, 0:128], qa1, 0, 128, 0)
+        expert_a(r10[:, 128:384], qa1, 128, 256, 0)
+        r11 = bank([P, 128], "r11", "dh01")
+        expert_a(r11[:], qa1, 0, 128, 1)
+        res = leave_scalar(r10[:], "r10")
+        nc.scalar.activation(r_mid[:, 0:128], r11[:], COPY)
+        scatter_scalar(r_tok[0], list_a, U0, res[:])
         r21 = bank([P, 128], "r21")
-        expert_a(r21[:], [part[:, 0:128] for part in qa2], 256, 1)
+        expert_a(r21[:], qa1, 128, 256, 1)
 
-        planes = [room[:, 128 : 128 + 2 * G].rearrange("p (h u) -> p h u", h=2), a_hi[0][:].bitcast(U32)]
+        planes = [stage[:, 128 : 128 + 2 * G].rearrange("p (h u) -> p h u", h=2), a_hi[0][:].bitcast(U32)]
         for g in range(2):
-            gather_plane(planes[g][:, 0, :], dc_lo[:], list_c, g * G)
-            gather_plane(planes[g][:, 1, :], dc_hi, list_c, g * G)
+            for h, pairs in enumerate((dc_lo, dc_hi)):
+                gather_plane(planes[g][:, h, :], pairs, list_c, g * G)
         gc = tile([P, G, 4], BF16, "gc0", "gc")
         weave(gc, planes[0])
         nc.vector.tensor_copy(out=r_mid[:, 128:G], in_=r21[:])
@@ -269,7 +287,7 @@ def tile_moe_plb_none_kernel(
             q1 = bank([P, G], "q%d1" % g, "dh_hi0")
             experts_b(q0[:, 0:G], qc[g], g, 0)
             if g == 1:
-                expert_a(q0[:, G : G + 128], [part[:, 128:G] for part in qa2], 256, 1)
+                expert_a(q0[:, G : G + 128], qa1, 256, 384, 1)
             experts_b(q1, qc[g], g, 1)
             res0 = leave_scalar(q0[:, 0:G], "q%d0" % g)
             if g == 0:

@@ -22,7 +22,7 @@ P = 128
 PASSES = N // 512
 G = 256
 U0 = 128
-LOW = [(320, 192), (0, 320)]
+LOW = [(256, 256), (0, 256)]
 EARLY = 256
 UNIT_STEP = 528
 
@@ -56,8 +56,8 @@ def tile_moe_plb_none_kernel(
         room = tile([P, T + UNIT_STEP + 2 * (T - U0)], U32, "room")
         rest = room[:, T + UNIT_STEP :]
         c_row = [tile([P, T], F32, "c_row0")[:], rest[:, 2 * (EARLY - U0) :].bitcast(F32)]
-        late = tile([P, T // 2 + 2 * G], F32, "late")
-        c_hi = [tile([P, 2, G], F32, "c_hi0")[:], late[:, T // 2 :].rearrange("p (e t) -> p e t", e=2)]
+        late = tile([P, T // 2 + 2 * T], F32, "late")
+        c_hi = late[:, T // 2 :].rearrange("p (e t) -> p e t", e=2)
         a_lo = [tile([P, 2, n], F32, "a_lo%d" % t0) for t0, n in LOW]
         a_hi = [tile([P, 2, G], F32, "a_hi%d" % half) for half in range(2)]
         wa_w = tile([P, E1, 2 * K], U8, "wa_w")
@@ -82,8 +82,7 @@ def tile_moe_plb_none_kernel(
         nc.sync.dma_start(out=c_row[0], in_=c_view[:, 0, :])
         nc.sync.dma_start(list_a[:], offs)
         nc.sync.dma_start(out=c_row[1], in_=c_view[:, 1, :])
-        for half in range(2):
-            nc.sync.dma_start(out=c_hi[half], in_=c_view[:, 2:4, half * G : (half + 1) * G])
+        nc.sync.dma_start(out=c_hi, in_=c_view[:, 2:4, :])
         nc.sync.dma_start(out=a_hi[1][:], in_=a_view[:, 2:4, G:T])
         nc.sync.dma_start(out=a_lo[0][:], in_=a_view[:, 0:2, LOW[0][0] : T])
         nc.sync.dma_start(out=a_hi[0][:], in_=a_view[:, 2:4, 0:G])
@@ -167,7 +166,10 @@ def tile_moe_plb_none_kernel(
                 dh = bank([P, n], "dh%d%d" % (j, b))
                 first_product(dh[:], j, t0, n)
                 nc.vector.tensor_tensor(out=da_row[j][:, t0 : t0 + n], in0=dh[:], in1=c_row[j][:, t0 : t0 + n], op=MULT)
-                nc.scalar.activation(dh_lo[:, j, t0 : t0 + n], dh[:], COPY)
+                if (j, b) == (0, 1):
+                    nc.vector.tensor_copy(out=dh_lo[:, j, t0 : t0 + n], in_=dh[:])
+                else:
+                    nc.scalar.activation(dh_lo[:, j, t0 : t0 + n], dh[:], COPY)
                 t0 += n
             if j == 0:
                 gather_row(ga_first.bitcast(BF16).rearrange("p b (u j) -> p b u j", j=4)[:, :, :, 0], 0, 0, EARLY)
@@ -183,7 +185,7 @@ def tile_moe_plb_none_kernel(
             dh_hi.append(dh)
             for e in range(2):
                 first_product(dh[:, e, :], 2 + e, t0, n)
-            product_pairs(nc.vector, da_hi, dh[:], c_hi[t0 // G][:, :, t0 % G : t0 % G + n], t0, n)
+            product_pairs(nc.vector, da_hi, dh[:], c_hi[:, :, t0 : t0 + n], t0, n)
 
         wb_sc = dy_sc[:].rearrange("p s (f k) -> p (s f) k", k=K)
         wb_rows = wbt_scales.rearrange("f s (q r) k -> r q (f s) k", r=4)
@@ -241,12 +243,13 @@ def tile_moe_plb_none_kernel(
             lo = t0 - spans[b][0]
             product_pairs(nc.vector, dc_hi, dh_hi[b][:, :, lo : lo + n], a_hi[t0 // G][:, :, t0 % G : t0 % G + n], t0, n)
 
-        dc_high(256)
+        dc_high(256, 64)
         gather_pairs(ga0, 1, da_hi, list_a, 0)
-        dc_high(384)
+        dc_high(320, 64)
         qa0 = quantise(ga0, "qa0")
         gather_pairs(ga1, 1, room[:, 0 : T + 2], list_a, U0)
         dc_low(1)
+        dc_high(384)
         dc_high(0)
         qa1 = quantise(ga1, "qa1")
         dc_high(128)
@@ -259,15 +262,14 @@ def tile_moe_plb_none_kernel(
             scatter_scalar(r_tok[kt], list_a, 0, first[kt][:])
         stage = tile([P, 640], U32, "stage")
         r_mid = stage[:, 0:G].bitcast(F32)
-        r10 = bank([P, T - U0], "r10", "dh00")
+        r10 = bank([P, T], "r10", "dh00")
         expert_a(r10[:, 0:128], qa1, 0, 128, 0)
         expert_a(r10[:, 128:384], qa1, 128, 256, 0)
-        r11 = bank([P, 128], "r11", "dh01")
-        expert_a(r11[:], qa1, 0, 128, 1)
-        res = leave_scalar(r10[:], "r10")
-        nc.scalar.activation(r_mid[:, 0:128], r11[:], COPY)
+        expert_a(r10[:, 384:T], qa1, 0, 128, 1)
+        res = leave_scalar(r10[:, 0:384], "r10")
+        nc.scalar.activation(r_mid[:, 0:128], r10[:, 384:T], COPY)
         scatter_scalar(r_tok[0], list_a, U0, res[:])
-        r21 = bank([P, 128], "r21")
+        r21 = bank([P, 128], "r21", "dh01")
         expert_a(r21[:], qa1, 128, 256, 1)
 
         planes = [stage[:, 128 : 128 + 2 * G].rearrange("p (h u) -> p h u", h=2), a_hi[0][:].bitcast(U32)]

@@ -23,7 +23,6 @@ PASSES = N // 512
 G = 256
 U0 = 128
 LOW = [(256, 256), (0, 256)]
-EARLY = 256
 UNIT_STEP = 528
 
 
@@ -55,7 +54,7 @@ def tile_moe_plb_none_kernel(
         dy_w = tile([P, PASSES, T], I32, "dy_w")
         room = tile([P, T + UNIT_STEP + 2 * (T - U0)], U32, "room")
         rest = room[:, T + UNIT_STEP :]
-        c_row = [tile([P, T], F32, "c_row0")[:], rest[:, 2 * (EARLY - U0) :].bitcast(F32)]
+        c_row = [tile([P, T], F32, "c_row0")[:], room[:, T : 2 * T].bitcast(F32)]
         late = tile([P, T // 2 + 2 * T], F32, "late")
         c_hi = late[:, T // 2 :].rearrange("p (e t) -> p e t", e=2)
         a_lo = [tile([P, 2, n], F32, "a_lo%d" % t0) for t0, n in LOW]
@@ -151,7 +150,6 @@ def tile_moe_plb_none_kernel(
         ga0 = room[:, T : T + 2 * U0].bitcast(BF16).rearrange("p (u j) -> p u j", j=4)
         ga1 = rest[:, 0 : 2 * (T - U0)].bitcast(BF16).rearrange("p (u j) -> p u j", j=4)
         dc_lo = room[:, T + 8 : 2 * T + 8].bitcast(BF16)
-        ga_first = room[:, T : T + 2 * UNIT_STEP].rearrange("p (b x) -> p b x", b=2)[:, :, 0 : 2 * U0]
 
         def dc_low(part):
             t0, n = LOW[part]
@@ -172,11 +170,10 @@ def tile_moe_plb_none_kernel(
                     nc.scalar.activation(dh_lo[:, j, t0 : t0 + n], dh[:], COPY)
                 t0 += n
             if j == 0:
-                gather_row(ga_first.bitcast(BF16).rearrange("p b (u j) -> p b u j", j=4)[:, :, :, 0], 0, 0, EARLY)
-            else:
-                gather_row(ga0[:, :, 1], 1, 0, U0)
+                gather_row(ga1[:, :, 0], 0, U0, T - U0)
         dc_low(0)
-        gather_row(ga1[:, EARLY - U0 :, 0], 0, EARLY, T - EARLY)
+        for j in range(2):
+            gather_row(ga0[:, :, j], j, 0, U0)
         gather_row(ga1[:, :, 1], 1, U0, T - U0)
         spans = [(0, 256), (256, 128), (384, 128)]
         dh_hi = []
@@ -238,18 +235,18 @@ def tile_moe_plb_none_kernel(
         def scatter_vector(window, lst, s0, src):
             nc.vector.tensor_copy(out=window[:].indirect(offsets(lst, s0, src.shape[1])), in_=src)
 
-        def dc_high(t0, n=128):
+        def dc_high(t0):
+            n = 128
             b = max(i for i, span in enumerate(spans) if span[0] <= t0)
             lo = t0 - spans[b][0]
             product_pairs(nc.vector, dc_hi, dh_hi[b][:, :, lo : lo + n], a_hi[t0 // G][:, :, t0 % G : t0 % G + n], t0, n)
 
-        dc_high(256, 64)
+        dc_high(256)
         gather_pairs(ga0, 1, da_hi, list_a, 0)
-        dc_high(320, 64)
+        dc_high(384)
         qa0 = quantise(ga0, "qa0")
         gather_pairs(ga1, 1, room[:, 0 : T + 2], list_a, U0)
         dc_low(1)
-        dc_high(384)
         dc_high(0)
         qa1 = quantise(ga1, "qa1")
         dc_high(128)

@@ -22,8 +22,7 @@ P = 128
 PASSES = N // 512
 G = 256
 U0 = 128
-LOW = [(256, 256), (0, 256)]
-UNIT_STEP = 528
+SHARE = 192
 
 
 def tile_moe_plb_none_kernel(
@@ -52,12 +51,9 @@ def tile_moe_plb_none_kernel(
         dy_sc = tile([P, PASSES, T], U8, "dy_sc")
         w2_raw = tile([P, PASSES, 2 * H], U8, "w2_raw")
         dy_w = tile([P, PASSES, T], I32, "dy_w")
-        room = tile([P, T + UNIT_STEP + 2 * (T - U0)], U32, "room")
-        rest = room[:, T + UNIT_STEP :]
-        c_row = [tile([P, T], F32, "c_row0")[:], room[:, T : 2 * T].bitcast(F32)]
-        late = tile([P, T // 2 + 2 * T], F32, "late")
-        c_hi = late[:, T // 2 :].rearrange("p (e t) -> p e t", e=2)
-        a_lo = [tile([P, 2, n], F32, "a_lo%d" % t0) for t0, n in LOW]
+        c_row = [tile([P, T], F32, "c_row%d" % j) for j in range(2)]
+        c_hi = tile([P, 2, T], F32, "c_hi")
+        a_lo = [tile([P, 2, G], F32, "a_lo%d" % half) for half in range(2)]
         a_hi = [tile([P, 2, G], F32, "a_hi%d" % half) for half in range(2)]
         wa_w = tile([P, E1, 2 * K], U8, "wa_w")
         wb_w = tile([P, E2, K], I32, "wb_w")
@@ -78,13 +74,10 @@ def tile_moe_plb_none_kernel(
         nc.sync.dma_start(out=dy_w[:], in_=dy_words.rearrange("s p t d -> p s (t d)").bitcast(I32))
         load_scale_row(nc.sync, dy_sc, dy_rows, 2)
         load_scale_row(nc.sync, dy_sc, dy_rows, 3)
-        nc.sync.dma_start(out=c_row[0], in_=c_view[:, 0, :])
+        nc.sync.dma_start(out=c_row[0][:], in_=c_view[:, 0, :])
         nc.sync.dma_start(list_a[:], offs)
-        nc.sync.dma_start(out=c_row[1], in_=c_view[:, 1, :])
-        nc.sync.dma_start(out=c_hi, in_=c_view[:, 2:4, :])
-        nc.sync.dma_start(out=a_hi[1][:], in_=a_view[:, 2:4, G:T])
-        nc.sync.dma_start(out=a_lo[0][:], in_=a_view[:, 0:2, LOW[0][0] : T])
-        nc.sync.dma_start(out=a_hi[0][:], in_=a_view[:, 2:4, 0:G])
+        nc.sync.dma_start(out=c_row[1][:], in_=c_view[:, 1, :])
+        nc.sync.dma_start(out=c_hi[:], in_=c_view[:, 2:4, :])
 
         w2_p = [tile([P, PASSES, 2, 2 * P], U8, "w2_p%d" % h) for h in range(2)]
         w2_sc = [tile([P, PASSES, 2, P], U8, "w2_sc%d" % h) for h in range(2)]
@@ -99,9 +92,12 @@ def tile_moe_plb_none_kernel(
         for r in range(4):
             load_scale_row(nc.sync, wa_sc, wa_rows, r)
         nc.sync.dma_start(out=wa_w[:].bitcast(I32), in_=wat_words.rearrange("e s p b -> p (e s) b").bitcast(I32))
-        nc.sync.dma_start(out=a_lo[1][:], in_=a_view[:, 0:2, 0 : LOW[0][0]])
-        nc.sync.dma_start(out=wb_w[:], in_=wbt_words.rearrange("f s p k d -> p (f s) (k d)").bitcast(I32))
+        nc.sync.dma_start(out=a_lo[1][:], in_=a_view[:, 0:2, G:T])
         nc.sync.dma_start(list_c[:], offs2)
+        for half in (1, 0):
+            nc.sync.dma_start(out=a_hi[half][:], in_=a_view[:, 2:4, half * G : (half + 1) * G])
+        nc.sync.dma_start(out=a_lo[0][:], in_=a_view[:, 0:2, 0:G])
+        nc.sync.dma_start(out=wb_w[:], in_=wbt_words.rearrange("f s p k d -> p (f s) (k d)").bitcast(I32))
 
         def first_product(dst, j, t0, n):
             for s in range(PASSES):
@@ -143,20 +139,20 @@ def tile_moe_plb_none_kernel(
             nc.vector.quantize_mx(out=codes[:].bitcast(FP8X4), scales=scales[:], in_=src.rearrange("p u j -> p (u j)"))
             return codes[:], scales[:]
 
-        da_row = [late[:, 0 : T // 2].bitcast(BF16), tile([P, T], BF16, "da_row1")[:]]
-        da_hi = room[:, 0:T].bitcast(BF16)
-        dc_hi = late[:, 0:T].bitcast(BF16)
+        da_row = [tile([P, T], BF16, "da_row%d" % j) for j in range(2)]
+        highs = tile([P, 2 * T], U32, "highs")
+        da_hi = highs[:, 0:T].bitcast(BF16)
+        dc_hi = highs[:, T:].bitcast(BF16)
         dh_lo = tile([P, 2, T], F32, "dh_lo")
-        ga0 = room[:, T : T + 2 * U0].bitcast(BF16).rearrange("p (u j) -> p u j", j=4)
-        ga1 = rest[:, 0 : 2 * (T - U0)].bitcast(BF16).rearrange("p (u j) -> p u j", j=4)
-        dc_lo = room[:, T + 8 : 2 * T + 8].bitcast(BF16)
+        room = tile([P, 2 * T], U32, "room")
+        ga = room[:].bitcast(BF16).rearrange("p (u j) -> p u j", j=4)
+        dc_lo = room[:, 0:T].bitcast(BF16)
 
-        def dc_low(part):
-            t0, n = LOW[part]
-            product_pairs(nc.gpsimd, dc_lo, dh_lo[:, :, t0 : t0 + n], a_lo[part][:], t0, n)
+        def dc_low(half):
+            product_pairs(nc.gpsimd, dc_lo, dh_lo[:, :, half * G : (half + 1) * G], a_lo[half][:], half * G, G)
 
-        def gather_row(dst, j, s0, n):
-            nc.scalar.activation(dst, da_row[j].indirect(offsets(list_a, s0, n)), COPY)
+        def gather_row(j, s0, n):
+            nc.scalar.activation(ga[:, s0 : s0 + n, j], da_row[j][:].indirect(offsets(list_a, s0, n)), COPY)
 
         for j, widths in enumerate([(256, 256), (512,)]):
             t0 = 0
@@ -169,12 +165,8 @@ def tile_moe_plb_none_kernel(
                 else:
                     nc.scalar.activation(dh_lo[:, j, t0 : t0 + n], dh[:], COPY)
                 t0 += n
-            if j == 0:
-                gather_row(ga1[:, :, 0], 0, U0, T - U0)
-        dc_low(0)
-        for j in range(2):
-            gather_row(ga0[:, :, j], j, 0, U0)
-        gather_row(ga1[:, :, 1], 1, U0, T - U0)
+            for half in range(2):
+                gather_row(j, half * G, G)
         spans = [(0, 256), (256, 128), (384, 128)]
         dh_hi = []
         for b, (t0, n) in enumerate(spans):
@@ -241,52 +233,53 @@ def tile_moe_plb_none_kernel(
             lo = t0 - spans[b][0]
             product_pairs(nc.vector, dc_hi, dh_hi[b][:, :, lo : lo + n], a_hi[t0 // G][:, :, t0 % G : t0 % G + n], t0, n)
 
-        dc_high(256)
-        gather_pairs(ga0, 1, da_hi, list_a, 0)
-        dc_high(384)
-        qa0 = quantise(ga0, "qa0")
-        gather_pairs(ga1, 1, room[:, 0 : T + 2], list_a, U0)
+        for u in range(2):
+            gather_pairs(ga[:, u * U0 : (u + 1) * U0, :], 1, da_hi, list_a, u * U0)
+        qa = [quantise(ga[:, u * U0 : (u + 1) * U0, :], "qa%d" % u) for u in range(2)]
         dc_low(1)
-        dc_high(0)
-        qa1 = quantise(ga1, "qa1")
-        dc_high(128)
-        first = []
-        for kt in range(2):
-            ru = bank([P, U0], "r0%d" % kt, "dh0%d" % kt)
-            expert_a(ru[:], qa0, 0, 0, kt)
-            first.append(leave_scalar(ru[:], "r0%d" % kt))
-        for kt in range(2):
-            scatter_scalar(r_tok[kt], list_a, 0, first[kt][:])
-        stage = tile([P, 640], U32, "stage")
+        dc_low(0)
+        for t0 in (256, 384, 0, 128):
+            dc_high(t0)
+        gather_pairs(ga[:, G:T, :], 1, highs[:, 0 : T + 2], list_a, G)
+        stage = tile([P, 2 * G], U32, "stage")
+        planes = [stage[:].rearrange("p (h u) -> p h u", h=2), a_lo[0][:].bitcast(U32)]
+        gather_plane(planes[0][:, 1, :], dc_hi, list_c, 0)
+        qa.append(quantise(ga[:, G:T, :], "qa2"))
+        for u in range(2):
+            short = []
+            for kt in range(2):
+                ru = bank([P, U0], "r%d%d" % (u, kt), "dh0%d" % kt)
+                expert_a(ru[:], qa[u], 0, u * U0, kt)
+                short.append(leave_scalar(ru[:], "r%d%d" % (u, kt)))
+            for kt in range(2):
+                scatter_scalar(r_tok[kt], list_a, u * U0, short[kt][:])
         r_mid = stage[:, 0:G].bitcast(F32)
-        r10 = bank([P, T], "r10", "dh00")
-        expert_a(r10[:, 0:128], qa1, 0, 128, 0)
-        expert_a(r10[:, 128:384], qa1, 128, 256, 0)
-        expert_a(r10[:, 384:T], qa1, 0, 128, 1)
-        res = leave_scalar(r10[:, 0:384], "r10")
-        nc.scalar.activation(r_mid[:, 0:128], r10[:, 384:T], COPY)
-        scatter_scalar(r_tok[0], list_a, U0, res[:])
+        r20 = bank([P, G], "r20", "dh00")
+        expert_a(r20[:], qa[2], 0, G, 0)
+        res = leave_scalar(r20[:, 0:SHARE], "r20")
+        scatter_scalar(r_tok[0], list_a, G, res[:])
         r21 = bank([P, 128], "r21", "dh01")
-        expert_a(r21[:], qa1, 128, 256, 1)
+        expert_a(r21[:], qa[2], 0, G, 1)
 
-        planes = [stage[:, 128 : 128 + 2 * G].rearrange("p (h u) -> p h u", h=2), a_hi[0][:].bitcast(U32)]
-        for g in range(2):
-            for h, pairs in enumerate((dc_lo, dc_hi)):
-                gather_plane(planes[g][:, h, :], pairs, list_c, g * G)
+        gather_plane(planes[0][:, 0, :], dc_lo, list_c, 0)
+        gather_plane(planes[1][:, 1, :], dc_hi, list_c, G)
+        gather_plane(planes[1][:, 0, :], dc_lo, list_c, G)
         gc = tile([P, G, 4], BF16, "gc0", "gc")
         weave(gc, planes[0])
-        nc.vector.tensor_copy(out=r_mid[:, 128:G], in_=r21[:])
         qc = [quantise(gc[:], "qc0")]
+        nc.vector.tensor_copy(out=r_mid[:, 0:128], in_=r21[:])
+        nc.vector.tensor_copy(out=r_mid[:, SHARE:G], in_=r20[:, SHARE:G])
         gc = tile([P, G, 4], BF16, "gc1", "gc")
         weave(gc, planes[1])
-        scatter_vector(r_tok[1], list_a, 128, r_mid)
+        scatter_vector(r_tok[1], list_a, G, r_mid[:, 0:128])
+        scatter_vector(r_tok[0], list_a, G + SHARE, r_mid[:, SHARE:G])
         qc.append(quantise(gc[:], "qc1"))
         for g in range(2):
-            q0 = bank([P, G + 128], "q%d0" % g, "dh00")
+            q0 = bank([P, G + 128], "q%d0" % g, "dh_hi1")
             q1 = bank([P, G], "q%d1" % g, "dh_hi0")
             experts_b(q0[:, 0:G], qc[g], g, 0)
             if g == 1:
-                expert_a(q0[:, G : G + 128], qa1, 256, 384, 1)
+                expert_a(q0[:, G : G + 128], qa[2], 128, 384, 1)
             experts_b(q1, qc[g], g, 1)
             res0 = leave_scalar(q0[:, 0:G], "q%d0" % g)
             if g == 0:

@@ -22,7 +22,7 @@ P = 128
 PASSES = N // 512
 G = 256
 U0 = 128
-SHARE = 192
+SHARE = 160
 
 
 def tile_moe_plb_none_kernel(
@@ -52,8 +52,9 @@ def tile_moe_plb_none_kernel(
         w2_raw = tile([P, PASSES, 2 * H], U8, "w2_raw")
         dy_w = tile([P, PASSES, T], I32, "dy_w")
         c_row = [tile([P, T], F32, "c_row%d" % j) for j in range(2)]
-        c_hi = tile([P, 2, T], F32, "c_hi")
-        a_lo = [tile([P, 2, G], F32, "a_lo%d" % half) for half in range(2)]
+        c_hi = [tile([P, 2, G], F32, "c_hi%d" % half) for half in range(2)]
+        a_low = tile([P, 2, T], F32, "a_low")
+        a_lo = [a_low[:, :, half * G : (half + 1) * G] for half in range(2)]
         a_hi = [tile([P, 2, G], F32, "a_hi%d" % half) for half in range(2)]
         wa_w = tile([P, E1, 2 * K], U8, "wa_w")
         wb_w = tile([P, E2, K], I32, "wb_w")
@@ -77,7 +78,8 @@ def tile_moe_plb_none_kernel(
         nc.sync.dma_start(out=c_row[0][:], in_=c_view[:, 0, :])
         nc.sync.dma_start(list_a[:], offs)
         nc.sync.dma_start(out=c_row[1][:], in_=c_view[:, 1, :])
-        nc.sync.dma_start(out=c_hi[:], in_=c_view[:, 2:4, :])
+        for half in range(2):
+            nc.sync.dma_start(out=c_hi[half][:], in_=c_view[:, 2:4, half * G : (half + 1) * G])
 
         w2_p = [tile([P, PASSES, 2, 2 * P], U8, "w2_p%d" % h) for h in range(2)]
         w2_sc = [tile([P, PASSES, 2, P], U8, "w2_sc%d" % h) for h in range(2)]
@@ -92,11 +94,10 @@ def tile_moe_plb_none_kernel(
         for r in range(4):
             load_scale_row(nc.sync, wa_sc, wa_rows, r)
         nc.sync.dma_start(out=wa_w[:].bitcast(I32), in_=wat_words.rearrange("e s p b -> p (e s) b").bitcast(I32))
-        nc.sync.dma_start(out=a_lo[1][:], in_=a_view[:, 0:2, G:T])
+        nc.sync.dma_start(out=a_low[:], in_=a_view[:, 0:2, :])
         nc.sync.dma_start(list_c[:], offs2)
-        for half in (1, 0):
+        for half in range(2):
             nc.sync.dma_start(out=a_hi[half][:], in_=a_view[:, 2:4, half * G : (half + 1) * G])
-        nc.sync.dma_start(out=a_lo[0][:], in_=a_view[:, 0:2, 0:G])
         nc.sync.dma_start(out=wb_w[:], in_=wbt_words.rearrange("f s p k d -> p (f s) (k d)").bitcast(I32))
 
         def first_product(dst, j, t0, n):
@@ -140,16 +141,16 @@ def tile_moe_plb_none_kernel(
             return codes[:], scales[:]
 
         da_row = [tile([P, T], BF16, "da_row%d" % j) for j in range(2)]
-        highs = tile([P, 2 * T], U32, "highs")
+        highs = tile([P, 4 * T], U32, "highs")
         da_hi = highs[:, 0:T].bitcast(BF16)
-        dc_hi = highs[:, T:].bitcast(BF16)
+        dc_hi = highs[:, T : 2 * T].bitcast(BF16)
         dh_lo = tile([P, 2, T], F32, "dh_lo")
-        room = tile([P, 2 * T], U32, "room")
-        ga = room[:].bitcast(BF16).rearrange("p (u j) -> p u j", j=4)
+        room = highs[:, 2 * T :]
+        ga = room.bitcast(BF16).rearrange("p (u j) -> p u j", j=4)
         dc_lo = room[:, 0:T].bitcast(BF16)
 
         def dc_low(half):
-            product_pairs(nc.gpsimd, dc_lo, dh_lo[:, :, half * G : (half + 1) * G], a_lo[half][:], half * G, G)
+            product_pairs(nc.gpsimd, dc_lo, dh_lo[:, :, half * G : (half + 1) * G], a_lo[half], half * G, G)
 
         def gather_row(j, s0, n):
             nc.scalar.activation(ga[:, s0 : s0 + n, j], da_row[j][:].indirect(offsets(list_a, s0, n)), COPY)
@@ -174,7 +175,7 @@ def tile_moe_plb_none_kernel(
             dh_hi.append(dh)
             for e in range(2):
                 first_product(dh[:, e, :], 2 + e, t0, n)
-            product_pairs(nc.vector, da_hi, dh[:], c_hi[:, :, t0 : t0 + n], t0, n)
+            product_pairs(nc.vector, da_hi, dh[:], c_hi[t0 // G][:, :, t0 % G : t0 % G + n], t0, n)
 
         wb_sc = dy_sc[:].rearrange("p s (f k) -> p (s f) k", k=K)
         wb_rows = wbt_scales.rearrange("f s (q r) k -> r q (f s) k", r=4)
@@ -227,22 +228,20 @@ def tile_moe_plb_none_kernel(
         def scatter_vector(window, lst, s0, src):
             nc.vector.tensor_copy(out=window[:].indirect(offsets(lst, s0, src.shape[1])), in_=src)
 
-        def dc_high(t0):
-            n = 128
-            b = max(i for i, span in enumerate(spans) if span[0] <= t0)
-            lo = t0 - spans[b][0]
-            product_pairs(nc.vector, dc_hi, dh_hi[b][:, :, lo : lo + n], a_hi[t0 // G][:, :, t0 % G : t0 % G + n], t0, n)
+        def dc_high(b):
+            t0, n = spans[b]
+            product_pairs(nc.vector, dc_hi, dh_hi[b][:], a_hi[t0 // G][:, :, t0 % G : t0 % G + n], t0, n)
 
         for u in range(2):
             gather_pairs(ga[:, u * U0 : (u + 1) * U0, :], 1, da_hi, list_a, u * U0)
         qa = [quantise(ga[:, u * U0 : (u + 1) * U0, :], "qa%d" % u) for u in range(2)]
-        dc_low(1)
         dc_low(0)
-        for t0 in (256, 384, 0, 128):
-            dc_high(t0)
-        gather_pairs(ga[:, G:T, :], 1, highs[:, 0 : T + 2], list_a, G)
+        dc_low(1)
+        for b in range(len(spans)):
+            dc_high(b)
+        gather_pairs(ga[:, G:T, :], 1, highs[:, 0 : T + G + 2], list_a, G)
         stage = tile([P, 2 * G], U32, "stage")
-        planes = [stage[:].rearrange("p (h u) -> p h u", h=2), a_lo[0][:].bitcast(U32)]
+        planes = [stage[:].rearrange("p (h u) -> p h u", h=2), tile([P, 2, G], U32, "planes1")[:]]
         gather_plane(planes[0][:, 1, :], dc_hi, list_c, 0)
         qa.append(quantise(ga[:, G:T, :], "qa2"))
         for u in range(2):
@@ -261,9 +260,9 @@ def tile_moe_plb_none_kernel(
         r21 = bank([P, 128], "r21", "dh01")
         expert_a(r21[:], qa[2], 0, G, 1)
 
-        gather_plane(planes[0][:, 0, :], dc_lo, list_c, 0)
-        gather_plane(planes[1][:, 1, :], dc_hi, list_c, G)
-        gather_plane(planes[1][:, 0, :], dc_lo, list_c, G)
+        gather_plane(planes[0][:, 0, :], room[:, 0 : T + 2], list_c, 0)
+        gather_plane(planes[1][:, 1, :], highs[:, T : 3 * T + 2], list_c, G)
+        gather_plane(planes[1][:, 0, :], room[:, 0 : T + 2], list_c, G)
         gc = tile([P, G, 4], BF16, "gc0", "gc")
         weave(gc, planes[0])
         qc = [quantise(gc[:], "qc0")]

@@ -53,9 +53,9 @@ def tile_moe_plb_none_kernel(
         dy_w = tile([P, PASSES, T], I32, "dy_w")
         c_row = [tile([P, T], F32, "c_row%d" % j) for j in range(2)]
         c_hi = [tile([P, 2, G], F32, "c_hi%d" % half) for half in range(2)]
-        a_low = tile([P, 2, T], F32, "a_low")
-        a_lo = [a_low[:, :, half * G : (half + 1) * G] for half in range(2)]
-        a_hi = [tile([P, 2, G], F32, "a_hi%d" % half) for half in range(2)]
+        a_first = tile([P, 4, G], F32, "a_first")
+        a_lo = [a_first[:, 0:2, :], tile([P, 2, G], F32, "a_lo")[:]]
+        a_hi = [a_first[:, 2:4, :], tile([P, 2, G], F32, "a_hi")[:]]
         wa_w = tile([P, E1, 2 * K], U8, "wa_w")
         wb_w = tile([P, E2, K], I32, "wb_w")
 
@@ -94,10 +94,10 @@ def tile_moe_plb_none_kernel(
         for r in range(4):
             load_scale_row(nc.sync, wa_sc, wa_rows, r)
         nc.sync.dma_start(out=wa_w[:].bitcast(I32), in_=wat_words.rearrange("e s p b -> p (e s) b").bitcast(I32))
-        nc.sync.dma_start(out=a_low[:], in_=a_view[:, 0:2, :])
         nc.sync.dma_start(list_c[:], offs2)
-        for half in range(2):
-            nc.sync.dma_start(out=a_hi[half][:], in_=a_view[:, 2:4, half * G : (half + 1) * G])
+        nc.sync.dma_start(out=a_first[:], in_=a_view[:, :, 0:G])
+        nc.sync.dma_start(out=a_hi[1], in_=a_view[:, 2:4, G:T])
+        nc.sync.dma_start(out=a_lo[1], in_=a_view[:, 0:2, G:T])
         nc.sync.dma_start(out=wb_w[:], in_=wbt_words.rearrange("f s p k d -> p (f s) (k d)").bitcast(I32))
 
         def first_product(dst, j, t0, n):

@@ -22,6 +22,7 @@ P = 128
 PASSES = N // 512
 G = 256
 U0 = 128
+EARLY = 384
 SHARE = 160
 
 
@@ -51,7 +52,8 @@ def tile_moe_plb_none_kernel(
         dy_sc = tile([P, PASSES, T], U8, "dy_sc")
         w2_raw = tile([P, PASSES, 2 * H], U8, "w2_raw")
         dy_w = tile([P, PASSES, T], I32, "dy_w")
-        c_row = [tile([P, T], F32, "c_row%d" % j) for j in range(2)]
+        highs = tile([P, 2 * T + 2 * EARLY + T], U32, "highs")
+        c_row = [tile([P, T], F32, "c_row0")[:], highs[:, 2 * T + 2 * EARLY :].bitcast(F32)]
         c_hi = [tile([P, 2, G], F32, "c_hi%d" % half) for half in range(2)]
         a_first = tile([P, 4, G], F32, "a_first")
         a_lo = [a_first[:, 0:2, :], tile([P, 2, G], F32, "a_lo")[:]]
@@ -75,9 +77,9 @@ def tile_moe_plb_none_kernel(
         nc.sync.dma_start(out=dy_w[:], in_=dy_words.rearrange("s p t d -> p s (t d)").bitcast(I32))
         load_scale_row(nc.sync, dy_sc, dy_rows, 2)
         load_scale_row(nc.sync, dy_sc, dy_rows, 3)
-        nc.sync.dma_start(out=c_row[0][:], in_=c_view[:, 0, :])
+        nc.sync.dma_start(out=c_row[0], in_=c_view[:, 0, :])
         nc.sync.dma_start(list_a[:], offs)
-        nc.sync.dma_start(out=c_row[1][:], in_=c_view[:, 1, :])
+        nc.sync.dma_start(out=c_row[1], in_=c_view[:, 1, :])
         for half in range(2):
             nc.sync.dma_start(out=c_hi[half][:], in_=c_view[:, 2:4, half * G : (half + 1) * G])
 
@@ -141,11 +143,10 @@ def tile_moe_plb_none_kernel(
             return codes[:], scales[:]
 
         da_row = [tile([P, T], BF16, "da_row%d" % j) for j in range(2)]
-        highs = tile([P, 4 * T], U32, "highs")
         da_hi = highs[:, 0:T].bitcast(BF16)
         dc_hi = highs[:, T : 2 * T].bitcast(BF16)
         dh_lo = tile([P, 2, T], F32, "dh_lo")
-        room = highs[:, 2 * T :]
+        room = highs[:, 2 * T : 4 * T]
         ga = room.bitcast(BF16).rearrange("p (u j) -> p u j", j=4)
         dc_lo = room[:, 0:T].bitcast(BF16)
 
@@ -155,19 +156,22 @@ def tile_moe_plb_none_kernel(
         def gather_row(j, s0, n):
             nc.scalar.activation(ga[:, s0 : s0 + n, j], da_row[j][:].indirect(offsets(list_a, s0, n)), COPY)
 
-        for j, widths in enumerate([(256, 256), (512,)]):
-            t0 = 0
-            for b, n in enumerate(widths):
-                dh = bank([P, n], "dh%d%d" % (j, b))
-                first_product(dh[:], j, t0, n)
-                nc.vector.tensor_tensor(out=da_row[j][:, t0 : t0 + n], in0=dh[:], in1=c_row[j][:, t0 : t0 + n], op=MULT)
-                if (j, b) == (0, 1):
-                    nc.vector.tensor_copy(out=dh_lo[:, j, t0 : t0 + n], in_=dh[:])
-                else:
-                    nc.scalar.activation(dh_lo[:, j, t0 : t0 + n], dh[:], COPY)
-                t0 += n
-            for half in range(2):
-                gather_row(j, half * G, G)
+        def low_row(j, t0, n, name):
+            dh = bank([P, n], name)
+            first_product(dh[:], j, t0, n)
+            nc.vector.tensor_tensor(out=da_row[j][:, t0 : t0 + n], in0=dh[:], in1=c_row[j][:, t0 : t0 + n], op=MULT)
+            return dh
+
+        dh = low_row(0, 0, G, "dh00")
+        nc.scalar.activation(dh_lo[:, 0, 0:G], dh[:], COPY)
+        dh = low_row(0, G, G, "dh01")
+        nc.vector.tensor_copy(out=dh_lo[:, 0, G:T], in_=dh[:])
+        gather_row(0, 0, EARLY)
+        dh = low_row(1, 0, T, "dh10")
+        gather_row(1, 0, G)
+        nc.scalar.activation(dh_lo[:, 1, :], dh[:], COPY)
+        gather_row(0, EARLY, T - EARLY)
+        gather_row(1, G, G)
         spans = [(0, 256), (256, 128), (384, 128)]
         dh_hi = []
         for b, (t0, n) in enumerate(spans):

@@ -248,14 +248,19 @@ def tile_moe_plb_none_kernel(
         planes = [stage[:].rearrange("p (h u) -> p h u", h=2), tile([P, 2, G], U32, "planes1")[:]]
         gather_plane(planes[0][:, 1, :], dc_hi, list_c, 0)
         qa.append(quantise(ga[:, G:T, :], "qa2"))
+        r00 = bank([P, U0], "r00", "dh00")
+        r01 = bank([P, G], "r01", "dh01")
+        expert_a(r00[:], qa[0], 0, 0, 0)
         for u in range(2):
-            short = []
-            for kt in range(2):
-                ru = bank([P, U0], "r%d%d" % (u, kt), "dh0%d" % kt)
-                expert_a(ru[:], qa[u], 0, u * U0, kt)
-                short.append(leave_scalar(ru[:], "r%d%d" % (u, kt)))
-            for kt in range(2):
-                scatter_scalar(r_tok[kt], list_a, u * U0, short[kt][:])
+            expert_a(r01[:, u * U0 : (u + 1) * U0], qa[u], 0, u * U0, 1)
+        res00 = leave_scalar(r00[:], "r00")
+        res01 = leave_scalar(r01[:], "r01")
+        scatter_scalar(r_tok[0], list_a, 0, res00[:])
+        r10 = bank([P, U0], "r10", "dh00")
+        expert_a(r10[:], qa[1], 0, U0, 0)
+        res10 = leave_scalar(r10[:], "r10")
+        scatter_scalar(r_tok[1], list_a, 0, res01[:])
+        scatter_scalar(r_tok[0], list_a, U0, res10[:])
         r_mid = stage[:, 0:G].bitcast(F32)
         r20 = bank([P, G], "r20", "dh00")
         expert_a(r20[:], qa[2], 0, G, 0)

from contextlib import ExitStack

import concourse.mybir as mybir

K, T, H, N = 256, 512, 512, 1024
E1, C1, E2, C2 = 2, 256, 4, 128
FLOPS = 2 * N * H * T + 2 * 2 * H * K * T

F32 = mybir.dt.float32
BF16 = mybir.dt.bfloat16
I32 = mybir.dt.int32
U32 = mybir.dt.uint32
U16 = mybir.dt.uint16
U8 = mybir.dt.uint8
FP8X4 = mybir.dt.float8_e4m3fn_x4
FP4X4 = mybir.dt.float4_e2m1fn_x4
MULT = mybir.AluOpType.mult
ADD = mybir.AluOpType.add
COPY = mybir.ActivationFunctionType.Copy

P = 128
PASSES = N // 512
G = 256
U0 = 128
EARLY = 384
SHARE = 160


def tile_moe_plb_none_kernel(
    tc, dy_words, dy_scales, w2t_words, w2t_scales, wat_words, wat_scales, wbt_words, wbt_scales, a, c, offs, offs2, out
):
    nc = tc.nc
    with ExitStack() as ctx:
        sb = ctx.enter_context(tc.tile_pool(name="sb", bufs=1))
        ps = ctx.enter_context(tc.psum_pool(name="ps", bufs=1))

        def tile(shape, dtype, name, tag=None):
            return sb.tile(shape, dtype, name=name, tag=tag or name, align_bytes=64)

        def bank(shape, name, tag=None):
            return ps.tile(shape, F32, name=name, tag=tag or name)

        def load_scale_row(queue, plane, rows, r):
            queue.dma_start(out=plane[r:P:32, :, :].bitcast(I32), in_=rows[r].bitcast(I32))

        def offsets(lst, s0, n):
            return lst[:, s0 // 16 : (s0 + n) // 16]

        list_a = tile([P, T // 16], U16, "list_a")
        list_c = tile([P, T // 16], U16, "list_c")
        w2_sc_raw = tile([P, PASSES, H], U8, "w2_sc_raw")
        dy_sc = tile([P, PASSES, T], U8, "dy_sc")
        w2_raw = tile([P, PASSES, 2 * H], U8, "w2_raw")
        dy_w = tile([P, PASSES, T], I32, "dy_w")
        highs = tile([P, 2 * T + 2 * EARLY + T], U32, "highs")
        c_row = [tile([P, T], F32, "c_row0")[:], highs[:, 2 * T + 2 * EARLY :].bitcast(F32)]
        c_hi = [tile([P, 2, G], F32, "c_hi%d" % half) for half in range(2)]
        a_first = tile([P, 4, G], F32, "a_first")
        a_lo = [a_first[:, 0:2, :], tile([P, 2, G], F32, "a_lo")[:]]
        a_hi = [a_first[:, 2:4, :], tile([P, 2, G], F32, "a_hi")[:]]
        wa_w = tile([P, E1, 2 * K], U8, "wa_w")
        wb_w = tile([P, E2, K], I32, "wb_w")

        nc.vector.memset(w2_sc_raw[:].bitcast(I32), 0)
        nc.vector.memset(dy_sc[:].bitcast(I32), 0)

        c_view = c.rearrange("(p j) t -> p j t", j=4)
        a_view = a.rearrange("(p j) t -> p j t", j=4)
        dy_rows = dy_scales.rearrange("s (q r) t -> r q s t", r=4)
        w2_rows = w2t_scales.rearrange("s (q r) i -> r q s i", r=4)

        nc.sync.dma_start(out=w2_raw[:].bitcast(I32), in_=w2t_words.rearrange("s p b -> p s b").bitcast(I32))
        for r, queue in enumerate([nc.scalar, nc.scalar, nc.sync, nc.sync]):
            load_scale_row(queue, w2_sc_raw, w2_rows, r)
        load_scale_row(nc.sync, dy_sc, dy_rows, 0)
        load_scale_row(nc.sync, dy_sc, dy_rows, 1)
        nc.sync.dma_start(out=dy_w[:], in_=dy_words.rearrange("s p t d -> p s (t d)").bitcast(I32))
        load_scale_row(nc.sync, dy_sc, dy_rows, 2)
        load_scale_row(nc.sync, dy_sc, dy_rows, 3)
        nc.sync.dma_start(out=c_row[0], in_=c_view[:, 0, :])
        nc.sync.dma_start(list_a[:], offs)
        nc.sync.dma_start(out=c_row[1], in_=c_view[:, 1, :])
        for half in range(2):
            nc.sync.dma_start(out=c_hi[half][:], in_=c_view[:, 2:4, half * G : (half + 1) * G])

        w2_p = [tile([P, PASSES, 2, 2 * P], U8, "w2_p%d" % h) for h in range(2)]
        w2_sc = [tile([P, PASSES, 2, P], U8, "w2_sc%d" % h) for h in range(2)]
        sc_view = w2_sc_raw[:].rearrange("p s (m j) -> p s m j", j=4)
        w_view = w2_raw[:].bitcast(U16).rearrange("p s (m j) -> p s m j", j=4)
        for h in range(2):
            nc.vector.tensor_copy(out=w2_p[h][:].bitcast(U16).rearrange("p s e m -> p s m e"), in_=w_view[:, :, :, 2 * h : 2 * h + 2])
            nc.vector.tensor_copy(out=w2_sc[h][:].rearrange("p s e m -> p s m e"), in_=sc_view[:, :, :, 2 * h : 2 * h + 2])

        wa_sc = w2_sc_raw[:, 0, :].rearrange("p (e k) -> p e k", k=K)
        wa_rows = wat_scales.rearrange("e s (q r) k -> r q (e s) k", r=4)
        for r in range(4):
            load_scale_row(nc.sync, wa_sc, wa_rows, r)
        nc.sync.dma_start(out=wa_w[:].bitcast(I32), in_=wat_words.rearrange("e s p b -> p (e s) b").bitcast(I32))
        nc.sync.dma_start(list_c[:], offs2)
        nc.sync.dma_start(out=a_first[:], in_=a_view[:, :, 0:G])
        nc.sync.dma_start(out=a_hi[1], in_=a_view[:, 2:4, G:T])
        nc.sync.dma_start(out=a_lo[1], in_=a_view[:, 0:2, G:T])
        nc.sync.dma_start(out=wb_w[:], in_=wbt_words.rearrange("f s p k d -> p (f s) (k d)").bitcast(I32))

        def first_product(dst, j, t0, n):
            for s in range(PASSES):
                nc.tensor.matmul_mx(
                    out=dst,
                    lhsT=w2_p[j // 2][:, s, j % 2, :].bitcast(FP4X4),
                    lhsT_scale=w2_sc[j // 2][:, s, j % 2, :],
                    rhs=dy_w[:, s, t0 : t0 + n].bitcast(FP8X4),
                    rhs_scale=dy_sc[:, s, t0 : t0 + n],
                    start=(s == 0),
                    stop=(s == PASSES - 1),
                )

        def product_pairs(engine, pairs, dh, saved, t0, n):
            engine.tensor_tensor(
                out=pairs[:, 2 * t0 : 2 * (t0 + n)].rearrange("p (u i e) -> p u e i", i=4, e=2),
                in0=dh.rearrange("p e (u i) -> p u e i", i=4),
                in1=saved.rearrange("p e (u i) -> p u e i", i=4),
                op=MULT,
            )

        def gather_pairs(dst, h, pairs, lst, s0):
            words = dst.rearrange("p u j -> p (u j)").bitcast(U32).rearrange("p (u h) -> p u h", h=2)
            nc.vector.tensor_copy(out=words[:, :, h], in_=pairs.bitcast(U32).indirect(offsets(lst, s0, dst.shape[1])))

        def gather_plane(dst, pairs, lst, s0):
            nc.vector.tensor_copy(out=dst, in_=pairs.bitcast(U32).indirect(offsets(lst, s0, dst.shape[1])))

        def weave(dst, planes):
            nc.gpsimd.tensor_copy(
                out=dst[:].rearrange("p u j -> p (u j)").bitcast(U32).rearrange("p (u h) -> p u h", h=2),
                in_=planes.rearrange("p h u -> p u h"),
            )

        def quantise(src, name):
            slots = src.shape[1]
            codes = tile([P, slots], U32, name + "_w")
            scales = tile([P, slots], U8, name + "_s")
            nc.vector.quantize_mx(out=codes[:].bitcast(FP8X4), scales=scales[:], in_=src.rearrange("p u j -> p (u j)"))
            return codes[:], scales[:]

        da_row = [tile([P, T], BF16, "da_row%d" % j) for j in range(2)]
        da_hi = highs[:, 0:T].bitcast(BF16)
        dc_hi = highs[:, T : 2 * T].bitcast(BF16)
        dh_lo = tile([P, 2, T], F32, "dh_lo")
        room = highs[:, 2 * T : 4 * T]
        ga = room.bitcast(BF16).rearrange("p (u j) -> p u j", j=4)
        dc_lo = room[:, 0:T].bitcast(BF16)

        def dc_low(half):
            product_pairs(nc.gpsimd, dc_lo, dh_lo[:, :, half * G : (half + 1) * G], a_lo[half], half * G, G)

        def gather_row(j, s0, n):
            nc.scalar.activation(ga[:, s0 : s0 + n, j], da_row[j][:].indirect(offsets(list_a, s0, n)), COPY)

        def low_row(j, t0, n, name):
            dh = bank([P, n], name)
            first_product(dh[:], j, t0, n)
            nc.vector.tensor_tensor(out=da_row[j][:, t0 : t0 + n], in0=dh[:], in1=c_row[j][:, t0 : t0 + n], op=MULT)
            return dh

        dh = low_row(0, 0, G, "dh00")
        nc.scalar.activation(dh_lo[:, 0, 0:G], dh[:], COPY)
        dh = low_row(0, G, G, "dh01")
        nc.vector.tensor_copy(out=dh_lo[:, 0, G:T], in_=dh[:])
        gather_row(0, 0, EARLY)
        dh = low_row(1, 0, T, "dh10")
        gather_row(1, 0, G)
        nc.scalar.activation(dh_lo[:, 1, :], dh[:], COPY)
        gather_row(0, EARLY, T - EARLY)
        gather_row(1, G, G)
        spans = [(0, 256), (256, 128), (384, 128)]
        dh_hi = []
        for b, (t0, n) in enumerate(spans):
            dh = bank([P, 2, n], "dh_hi%d" % b)
            dh_hi.append(dh)
            for e in range(2):
                first_product(dh[:, e, :], 2 + e, t0, n)
            product_pairs(nc.vector, da_hi, dh[:], c_hi[t0 // G][:, :, t0 % G : t0 % G + n], t0, n)

        wb_sc = dy_sc[:].rearrange("p s (f k) -> p (s f) k", k=K)
        wb_rows = wbt_scales.rearrange("f s (q r) k -> r q (f s) k", r=4)
        for r in range(4):
            load_scale_row(nc.sync, wb_sc, wb_rows, r)

        r_tok = [tile([P, T], F32, "r_tok%d" % kt) for kt in range(2)]
        q_tok = [tile([P, T], F32, "q_tok%d" % kt) for kt in range(2)]

        def expert_a(dst, quantised, col0, s0, kt):
            codes, scales = quantised
            n = dst.shape[1]
            nc.tensor.matmul_mx(
                out=dst,
                lhsT=wa_w[:, s0 // C1, kt * 256 : (kt + 1) * 256].bitcast(FP4X4),
                lhsT_scale=wa_sc[:, s0 // C1, kt * 128 : (kt + 1) * 128],
                rhs=codes[:, col0 : col0 + n].bitcast(FP8X4),
                rhs_scale=scales[:, col0 : col0 + n],
                start=True,
                stop=True,
            )

        def experts_b(dst, quantised, g, kt):
            codes, scales = quantised
            for fl in range(2):
                cols = slice(fl * C2, (fl + 1) * C2)
                nc.tensor.matmul_mx(
                    out=dst[:, cols],
                    lhsT=wb_w[:, 2 * g + fl, kt * 128 : (kt + 1) * 128].bitcast(FP8X4),
                    lhsT_scale=wb_sc[:, 2 * g + fl, kt * 128 : (kt + 1) * 128],
                    rhs=codes[:, cols].bitcast(FP8X4),
                    rhs_scale=scales[:, cols],
                    start=True,
                    stop=True,
                )

        def leave_scalar(src, name):
            res = tile(list(src.shape), F32, name)
            nc.scalar.activation(res[:], src, COPY)
            return res

        def leave_vector(src, name):
            res = tile(list(src.shape), F32, name)
            nc.vector.tensor_copy(out=res[:], in_=src)
            return res

        def scatter_scalar(window, lst, s0, src):
            nc.scalar.activation(window[:].indirect(offsets(lst, s0, src.shape[1])), src, COPY)

        def scatter_vector(window, lst, s0, src):
            nc.vector.tensor_copy(out=window[:].indirect(offsets(lst, s0, src.shape[1])), in_=src)

        def dc_high(b):
            t0, n = spans[b]
            product_pairs(nc.vector, dc_hi, dh_hi[b][:], a_hi[t0 // G][:, :, t0 % G : t0 % G + n], t0, n)

        for u in range(2):
            gather_pairs(ga[:, u * U0 : (u + 1) * U0, :], 1, da_hi, list_a, u * U0)
        qa = [quantise(ga[:, u * U0 : (u + 1) * U0, :], "qa%d" % u) for u in range(2)]
        dc_low(0)
        dc_low(1)
        for b in range(len(spans)):
            dc_high(b)
        gather_pairs(ga[:, G:T, :], 1, highs[:, 0 : T + G + 2], list_a, G)
        stage = tile([P, 2 * G], U32, "stage")
        planes = [stage[:].rearrange("p (h u) -> p h u", h=2), tile([P, 2, G], U32, "planes1")[:]]
        gather_plane(planes[0][:, 1, :], dc_hi, list_c, 0)
        qa.append(quantise(ga[:, G:T, :], "qa2"))
        r00 = bank([P, U0], "r00", "dh00")
        r01 = bank([P, G], "r01", "dh01")
        expert_a(r00[:], qa[0], 0, 0, 0)
        for u in range(2):
            expert_a(r01[:, u * U0 : (u + 1) * U0], qa[u], 0, u * U0, 1)
        res00 = leave_scalar(r00[:], "r00")
        res01 = leave_scalar(r01[:], "r01")
        scatter_scalar(r_tok[0], list_a, 0, res00[:])
        r10 = bank([P, U0], "r10", "dh00")
        expert_a(r10[:], qa[1], 0, U0, 0)
        res10 = leave_scalar(r10[:], "r10")
        scatter_scalar(r_tok[1], list_a, 0, res01[:])
        scatter_scalar(r_tok[0], list_a, U0, res10[:])
        r_mid = stage[:, 0:G].bitcast(F32)
        r20 = bank([P, G], "r20", "dh00")
        expert_a(r20[:], qa[2], 0, G, 0)
        res = leave_scalar(r20[:, 0:SHARE], "r20")
        scatter_scalar(r_tok[0], list_a, G, res[:])
        r21 = bank([P, 128], "r21", "dh01")
        expert_a(r21[:], qa[2], 0, G, 1)

        gather_plane(planes[0][:, 0, :], room[:, 0 : T + 2], list_c, 0)
        gather_plane(planes[1][:, 1, :], highs[:, T : 3 * T + 2], list_c, G)
        gather_plane(planes[1][:, 0, :], room[:, 0 : T + 2], list_c, G)
        gc = tile([P, G, 4], BF16, "gc0", "gc")
        weave(gc, planes[0])
        qc = [quantise(gc[:], "qc0")]
        nc.vector.tensor_copy(out=r_mid[:, 0:128], in_=r21[:])
        nc.vector.tensor_copy(out=r_mid[:, SHARE:G], in_=r20[:, SHARE:G])
        gc = tile([P, G, 4], BF16, "gc1", "gc")
        weave(gc, planes[1])
        scatter_vector(r_tok[1], list_a, G, r_mid[:, 0:128])
        scatter_vector(r_tok[0], list_a, G + SHARE, r_mid[:, SHARE:G])
        qc.append(quantise(gc[:], "qc1"))
        for g in range(2):
            q0 = bank([P, G + 128], "q%d0" % g, "dh_hi1")
            q1 = bank([P, G], "q%d1" % g, "dh_hi0")
            experts_b(q0[:, 0:G], qc[g], g, 0)
            if g == 1:
                expert_a(q0[:, G : G + 128], qa[2], 128, 384, 1)
            experts_b(q1, qc[g], g, 1)
            res0 = leave_scalar(q0[:, 0:G], "q%d0" % g)
            if g == 0:
                res1 = leave_scalar(q1[:], "q01")
            else:
                res1 = leave_vector(q1[:], "q11")
                r_last = leave_scalar(q0[:, G : G + 128], "r_last")
            scatter_scalar(q_tok[0], list_c, g * G, res0[:])
            scatter_vector(q_tok[1], list_c, g * G, res1[:])
        scatter_scalar(r_tok[1], list_a, 384, r_last[:])

        def store_sum(queue, kt, t0, n):
            res = tile([P, n], F32, "res%d_%d" % (kt, t0))
            nc.vector.tensor_tensor(out=res[:], in0=r_tok[kt][:, t0 : t0 + n], in1=q_tok[kt][:, t0 : t0 + n], op=ADD)
            queue.dma_start(out=out[kt * P : (kt + 1) * P, t0 : t0 + n], in_=res[:])

        store_sum(nc.sync, 0, 0, T)
        store_sum(nc.scalar, 1, 0, T // 2)
        store_sum(nc.sync, 1, T // 2, T // 2)
